import numpy as np, ml_dtypes
CORES = [10,34,74,98]
N = 4
BF = ml_dtypes.bfloat16
def gentries(a):
    return np.ascontiguousarray(a.reshape(8, 16, -1).transpose(0, 2, 1)).reshape(8, -1)
def gtable(e):
    e = np.asarray(e); return np.ascontiguousarray(e.reshape(8, -1, 16).transpose(0, 2, 1)).reshape(128, -1).astype(np.int32)
def f(rng, *shape):
    return (rng.standard_normal(shape, dtype=np.float32) * np.exp2(rng.integers(-2, 3, shape[:-1] + (1,)))).astype(BF)
def wide(rng, *shape):
    v = f(rng, *shape).astype(np.float32); k = shape[:-2] + (1, shape[-1])
    return (v * np.exp2(rng.integers(-6, 7, k)) * (rng.random(k) > 0.0625)).astype(BF)
W, K, S, RO, FI, CAP = 4096, 2048, 3, 3, 6, 128
def parts(rng):
    b = rng.random((N, 8, S, W)) < rng.choice(np.array([0.5, 0.6, 0.75]), (N, 8, S, 1)); b[..., 0] = True; b[..., W - 1] = True
    nx = np.zeros((N, 8, S, W), np.int64); cur = np.zeros((N, 8, S, K), np.int64)
    for a in range(N):
        for g in range(8):
            for i in range(S):
                v = np.nonzero(b[a, g, i])[0]
                nx[a, g, i] = rng.choice(v, W); nx[a, g, i, v] = rng.permutation(v); cur[a, g, i] = rng.choice(v, K)
    return b, nx, cur, rng.integers(0, S, (N, 8, K)), rng.integers(0, W, (N, 8, W))
def pack(x, b, nx, cur, typ, fro, w):
    mem = np.add.reduce(b.astype(np.int64) << np.arange(S)[:, None], axis=2)
    return {"x": x.astype(BF).reshape(N, 128, W), "nxt": nx.reshape(N, 8, S * W).astype(np.int32), "mem": mem.astype(np.int32), "fro": fro.astype(np.int32),
            "cur": np.stack([gtable(a.reshape(8, S * K)) for a in cur]), "typ": np.stack([gtable(a) for a in typ]), "w0": w.astype(BF).reshape(N, 128, K)}
def setup_inputs(rng):
    b, nx, cur, typ, fro = parts(rng)
    return pack(f(rng, N, 128, W), b, nx, cur, typ, fro, f(rng, N, 128, K))
def setup_inputs_room(rng):
    b, nx, cur, typ, fro = parts(rng)
    x = np.minimum(f(rng, N, 128, W).astype(np.float32), 24); w = f(rng, N, 128, K).astype(np.float32).reshape(N, 8, 16, K)
    w[:, ::2] = np.abs(w[:, ::2]) + 32; w[:, 1] = np.abs(w[:, 1]) + 32
    at = np.take_along_axis(cur, typ[:, :, None, :], 2)[:, :, 0]
    for q in range(FI): at = np.take_along_axis(nx.reshape(N, 8, S * W), typ * W + at, 2)
    z = np.where(typ == S - 1, 0, typ + 1)
    for a in range(N):
        m, zz, cc, i = at[a, 1], z[a, 1], cur[a, 1], a % S
        o = rng.permutation(np.arange(1, K - 1)); o = o[b[a, 1, zz[o], m[o]] & (m[o] > 0) & (m[o] < W - 2)]
        o = rng.permutation(o[np.unique(m[o], return_index=True)[1]])
        by = [o[zz[o] == j] for j in range(S)]
        cc[zz, np.arange(K)] = m
        for j in range(S): cc[j, by[j][:3]] = (0, W - 2, W - 1)
        u, v, p, q, e1, e2 = by[i][3:9]
        ends = [K - 1, 0] if a % 2 == 0 else [0, K - 1]
        typ[a, 1, ends] = typ[a, 1, [u, v]]; cc[:, ends] = cc[:, [u, v]]
        cc[i, ends[0]] = m[q]; cc[i, p] = m[v]
        r = rng.choice(np.nonzero(~b[a, 1, i, :W - 2])[0]); nx[a, 1, i, r] = nx[a, 1, i, m[e1]]; cc[i, e1] = r; cc[i, e2] = r
        b[a, 1, typ[a, 1, [u, p]], m[[u, p]]] = False
    for a in range(N):
        for g in range(0, 8, 2):
            m = at[a, g]; zz = z[a, g]; e = rng.permutation(np.nonzero(b[a, g, zz, m])[0])
            k = int(rng.choice(np.array([0, 1, CAP - 1, CAP, CAP + 1, len(e)])))
            if a < 2: k = ((CAP, CAP + 1, CAP - 1, 0), (1, CAP, len(e), CAP + 1))[a][g // 2]
            cur[a, g, zz[e], e] = m[e]
            one = e[(zz[e] == 0) & (m[e] != 0)][:1] if k == 1 else e[:0]
            e = np.concatenate([one, e])[:k]; k = len(e)
            c = rng.choice(np.concatenate([rng.permutation(W)[:int(rng.choice(np.array([24, 150, 600, W])))], m[e[:k // 4]]]), k)
            cur[a, g, zz[e], e] = np.where(c == m[e], (c + 1) % W, c)
            cur[a, g, 0, one] = 0
    return pack(x, b, nx, cur, typ, fro, w)
def setup_inputs_ties(rng):
    b, nx, cur, typ, fro = parts(rng)
    x = 4.0 * rng.integers(-3, 4, (N, 8, 16, W)); w = 4.0 * rng.integers(-3, 4, (N, 8, 16, K))
    x[::2, 5] = rng.choice(np.array([7.96875, 8, 8, 8, 8.0625]), (N // 2, 16, W)); x[1::2, 5] = 64
    w[:, 5] = rng.choice(np.array([-1.0, 1.0]), (N, 16, K)) * np.exp2(-1.0 * rng.integers(14, 21, (N, 16, K)))
    return pack(x, b, nx, cur, typ, fro, w)
def setup_inputs_alike(rng):
    b, nx, cur, typ, fro = parts(rng)
    cur[:, 0] = rng.choice(np.array([0, W - 1]), (N, S, K)); nx[:, 1] = rng.choice(np.array([0, 3, W // 2, W - 1]), (N, S, W)); nx[:, 2] = np.arange(W)
    fro[:, 3] = rng.choice(np.array([0, W - 1]), (N, W)); b[:, 4] = True; b[:, 5] = False; typ[:, 6] = 0; cur[:, 7] = np.repeat(cur[:, 7, :1], S, axis=1)
    return pack(f(rng, N, 128, W), b, nx, cur, typ, fro, f(rng, N, 128, K))
def setup_inputs_hot(rng):
    b, nx, cur, typ, fro = parts(rng)
    sh = rng.choice(np.array([-64, 0, 64]), (N, 8, 1, 1)); sh[0, :4, 0, 0] = (-64, 64, -64, 0); sh[1, 4:, 0, 0] = (0, -64, 64, -64)
    b[rng.random((N, 8)) < 0.3] = True; b[0, 0] = True; b[1, 5] = True
    x = f(rng, N, 128, W).reshape(N, 8, 16, W); w = f(rng, N, 128, K).astype(np.float32).reshape(N, 8, 16, K) + sh
    for g in (3, 6):
        b[:, g] = True; w[:, g] = 4
        x[::2, g] = (rng.integers(0, 25, x[::2, g].shape) * 0.125).astype(BF); x[1::2, g] = (rng.integers(-32, -7, x[1::2, g].shape) * 0.125).astype(BF)
    for a in range(0, N, 2):
        o = np.concatenate([CAP // 2 + rng.permutation(CAP // 2)[:CAP // 4], CAP + rng.permutation(K - CAP)[:CAP // 8]])
        w[a, 6][:, o] = 1000
    return pack(x, b, nx, cur, typ, fro, w)
def setup_inputs_spread(rng):
    b, nx, cur, typ, fro = parts(rng)
    return pack(wide(rng, N, 128, W), b, nx, cur, typ, fro, wide(rng, N, 128, K))
def check_inputs(d):
    bad = []
    for k, hi in (("nxt", W - 1), ("mem", 2 ** S - 1), ("fro", W - 1), ("cur", W - 1), ("typ", S - 1)):
        if np.min(d[k]) < 0 or np.max(d[k]) > hi: bad.append("range of " + k)
    for k in ("x", "w0"):
        if not np.all(np.abs(d[k].astype(np.float32)) < 2.0 ** 60): bad.append("size of " + k)
    return bad
def reference(x, nxt, mem, fro, cur, typ, w0):
    pick = np.take_along_axis
    X = x.astype(np.float32).reshape(N, 8, 16, W); w = w0.astype(np.float32).reshape(N, 8, 16, K)
    nx = nxt.astype(np.int64); mb = mem.astype(np.int64); fo = fro.astype(np.int64)
    c = np.stack([gentries(a) for a in cur]).astype(np.int64).reshape(N, 8, S, K); s = np.stack([gentries(a) for a in typ]).astype(np.int64)
    for t in range(RO):
        for q in range(FI):
            at = pick(c, s[:, :, None, :], 2)[:, :, 0]
            m = pick(nx, s * W + at, 2)
            hit = np.add.reduce((pick(X, m[:, :, None, :], 3) >= w).astype(np.int64), axis=2) >= 9
            bits = pick(mb, m, 2)
            for i in range(S): c[:, :, i] = np.where((s == i) | (hit & (((bits >> i) & 1) == 1)), m, c[:, :, i])
            s = np.where(hit, np.where(s == S - 1, 0, s + 1), s)
        z = np.where(s == S - 1, 0, s + 1)
        m = pick(c, s[:, :, None, :], 2)[:, :, 0]; e = pick(c, z[:, :, None, :], 2)[:, :, 0]
        want = (((pick(mb, m, 2) >> z) & 1) == 1) & (m != e)
        slot = want & (np.add.accumulate(want.astype(np.int64), axis=2) <= CAP)
        for a in range(N):
            for g in range(8):
                j = np.nonzero(slot[a, g])[0]
                p1 = z[a, g, j] * W + m[a, g, j]; p2 = z[a, g, j] * W + e[a, g, j]
                named = np.bincount(np.concatenate([p1, p2]), minlength=S * W)
                ok = (named[p1] == 1) & (named[p2] == 1); p1 = p1[ok]; p2 = p2[ok]
                v1 = nx[a, g, p1]; v2 = nx[a, g, p2]
                nx[a, g, p1] = v2; nx[a, g, p2] = v1
        k = pick(fo, m, 2)
        y = np.stack([pick(X[(a + 1 + t) % N], k[a][:, None, :], 2) for a in range(N)])
        w = w + np.minimum(np.maximum(y - w, np.float32(-8)), np.float32(8))
    return {"yc": np.stack([gtable(a.reshape(8, S * K)) for a in c]).astype(np.float32), "yw": w.reshape(N, 128, K).astype(np.float32), "yn": nx.astype(np.float32)}

@@ -1,0 +1,599 @@
+from concourse.mybir import AluOpType as A, ActivationFunctionType as AF
+
+ROUNDS, FINDS, W, K = 3, 6, 4096, 2048
+DUMP = 3 * W
+B, FL, IN, U16, SB = "bfloat16", "float32", "int32", "uint16", "sbuf"
+rNA, rNB, rND, rV, rJB, rJD, rFR, rS, rDL, rONE = 0, 2, 4, 6, 8, 9, 10, 12, 13, 14
+
+SCRATCH = {}
+for _dt, _names in (
+    (B, "X:12288 TB:12544 xb0:4096 xb1:4096 xb2:4096 TG:2064 C2:2064 D2:2048 CM0:1024 CM1:1024 SM:128 SC:128 CP:1024 CP2:128 IOR:128 BDb:128 EC0:128 EC1:128 "
+        "NL:768 NH:768 MJ:768 FB:512 VB:512 HM0:128 HM1:128 WT:128 INC:128 A1:128 A2:128 A3:128 ON:128 WF:64 WL:64 WB:64 WR:64 XW2:16 PMX:256 PB:2048 EQ:4096 "
+        "G3:256 G4:256 G5:256"),
+    (FL, "w:2048 D0:512 D1:512 DD0:512 DD1:512 DD2:512 DD3:512 ya:256 yb:256 CF:384 EQ3:384 PR:384 u0:128 u1:128 p0:64 p1:64 q0:128 q1:128 "
+         "ZA0:132 ZA1:132 ZB0:132 ZB1:132 ZC0:132 ZC1:132 ZD0:132 ZD1:132 NE:128 RKW:136 CEN:8 BX:128 JX:128 GM16:8 PIf:8 COF:512 GM:8 RM:16 RMX:256 BDm:128 IDn:128 "
+         "RS:128 WC:64 PG:16 OW:256 OK:128 Y:256 YK:256 KD:2 DL:16 LPf:16 YF:768"),
+    (IN, "NX:768 NI:768 ME:256 MI:768 FR:256 FI:512 VI:256 VJ:512 CU:384 TY:128 ST0:192 ST1:192 CD0:128 CD1:128 PIi:4 COL:128 CO2:384 RSi:128"),
+    (U16, "LA:128 LB:128 LD:128 LK:128 LQ:8 LJ:8 LP:16"),
+):
+    for _n in _names.split():
+        SCRATCH[_n.split(":")[0]] = (SB, [128, int(_n.split(":")[1])], _dt)
+for _n in "tb0 tb1 cb0 cb1 lb0 lb1 pa pb".split():
+    SCRATCH[_n] = ("psum", [128, 512], FL)
+GROUPS = "ldx0 ldw ldn ldm ldf ldc r1 r2 r3 r4 r5 r6 r7 r8 wa00 wa01 wa10 wa11 wa20 rb0 rb1 out0 out1 out2 out3 yl".split()
+SEMAPHORES = ["qv", "qs", "qt", "qg", "xs", "x0", "x1", "x2"] + GROUPS
+
+
+def rank_program(g, core, T, topo):
+    rank = T.rank_of(core)
+    if rank is None:
+        return
+    Q = {"v": g.vector, "s": g.scalar, "t": g.tensor, "g": g, "y": g.sync}
+    V, S, P = g.vector, g.scalar, g.tensor
+    SEMOF = {"v": "qv", "s": "qs", "t": "qt", "g": "qg"}
+    count, known, clock, acc, closed = {}, {q: {} for q in Q}, {}, {}, {}
+
+    def r(name, c0, c1, step=1, p0=0, p1=128, ps=1):
+        return (name, c0, c1, step, p0, p1, ps)
+
+    def ap(k):
+        if k[6] != 1:
+            return T[k[0]][k[4]:k[5]:k[6], k[1]:k[2]]
+        if k[3] != 1:
+            return T[k[0]][k[4]:k[5], k[1]:k[2]:k[3]]
+        return T[k[0]][k[4]:k[5], k[1]:k[2]]
+
+    def psum(n):
+        return SCRATCH[n][0] == "psum"
+
+    def meet(a, b):
+        if a[1] >= b[2] or b[1] >= a[2] or a[4] >= b[5] or b[4] >= a[5]:
+            return False
+        if a[6] == 16 and b[6] == 16 and a[4] % 16 != b[4] % 16:
+            return False
+        if a[3] == b[3] and a[3] > 1 and (a[1] - b[1]) % a[3]:
+            return False
+        return True
+
+    def cover(a, b):
+        return a[3] == 1 and a[6] == 1 and a[1] <= b[1] and a[2] >= b[2] and a[4] <= b[4] and a[5] >= b[5]
+
+    def wait(q, ev):
+        sem, n = ev
+        if sem in GROUPS:
+            n = count[sem]
+            closed[sem] = True
+        if known[q].get(sem, 0) >= n:
+            return
+        Q[q].wait_ge(T.sem[sem], n)
+        known[q][sem] = n
+        for k2, n2 in clock.get((sem, n), {}).items():
+            if known[q].get(k2, 0) < n2:
+                known[q][k2] = n2
+
+    def deps(q, reads, writes):
+        best = {}
+        for isw, lst in ((False, reads), (True, writes)):
+            for k in lst:
+                for (k2, w2, ev, q2) in acc.get(k[0], []):
+                    if psum(k[0]):
+                        if q2 == q and (q == "t" or not (isw or w2) or not meet(k, k2)):
+                            continue
+                    elif not ((isw or w2) and meet(k, k2)):
+                        continue
+                    best[ev[0]] = max(best.get(ev[0], 0), ev[1])
+        for s_ in sorted(best):
+            wait(q, (s_, best[s_]))
+
+    def note(q, reads, writes, ev, dma):
+        tag = "dma" if dma else q
+        for isw, lst in ((False, reads), (True, writes)):
+            for k in lst:
+                old = acc.get(k[0], [])
+                if psum(k[0]):
+                    old = [o for o in old if o[3] == tag and o[0] != k]
+                    if isw and tag != "t":
+                        old = [o for o in old if not cover(k, o[0])]
+                elif isw:
+                    old = [o for o in old if not cover(k, o[0])]
+                elif not dma:
+                    old = [o for o in old if not (o[3] == tag and not o[1] and o[0] == k)]
+                acc[k[0]] = old + [(k, isw, ev, tag)]
+
+    def op(q, fn, reads, writes):
+        deps(q, reads, writes)
+        sem = SEMOF[q]
+        count[sem] = count.get(sem, 0) + 1
+        ev = (sem, count[sem])
+        fn().then_inc(T.sem[sem], 1)
+        c = dict(known[q])
+        c[sem] = count[sem]
+        clock[ev] = c
+        note(q, reads, writes, ev, False)
+
+    def dma(q, grp, out, in_, outk=None, ink=None):
+        assert not closed.get(grp)
+        rd, wr = [ink] if ink else [], [outk] if outk else []
+        deps(q, rd, wr)
+        count[grp] = count.get(grp, 0) + 16
+        Q[q].dma_start(out, in_).then_inc(T.sem[grp], 16)
+        note(q, rd, wr, (grp, 0), True)
+
+    def mv(q, grp, o, i):
+        dma(q, grp, ap(o), ap(i), o, i)
+
+    def add(grp, o, i):
+        deps("g", [i], [o])
+        count[grp] = count.get(grp, 0) + 16
+        g.dma_start(ap(o), ap(i), accum_op=A.add).then_inc(T.sem[grp], 16)
+        note("g", [i], [o], (grp, 0), True)
+
+    def tt(o, a, b, f):
+        op("v", lambda: V.tensor_tensor(ap(o), ap(a), ap(b), f), [a, b], [o])
+
+    def ts(o, a, s1, f, s2=None, f2=None):
+        rd = [a] + [k for k in (s1, s2) if isinstance(k, tuple)]
+        x1 = ap(s1) if isinstance(s1, tuple) else s1
+        x2 = ap(s2) if isinstance(s2, tuple) else s2
+        if f2 is None:
+            op("v", lambda: V.tensor_scalar(ap(o), ap(a), x1, None, f), rd, [o])
+        else:
+            op("v", lambda: V.tensor_scalar(ap(o), ap(a), x1, x2, f, f2), rd, [o])
+
+    def cp(o, a):
+        op("v", lambda: V.tensor_copy(ap(o), ap(a)), [a], [o])
+
+    def mset(o, c):
+        op("v", lambda: V.memset(ap(o), c), [], [o])
+
+    def mm(o, l, h, start, stop):
+        op("t", lambda: P.matmul(ap(o), ap(l), ap(h), start, stop), [l, h], [o])
+
+    def act(o, a, f, bias=0.0, scale=1.0):
+        b = ap(bias) if isinstance(bias, tuple) else bias
+        op("s", lambda: S.activation(ap(o), ap(a), f, b, scale), [a] + ([bias] if isinstance(bias, tuple) else []), [o])
+
+    def sca(o, a, c):
+        op("s", lambda: S.activation(ap(o), ap(a), AF.Copy, 0.0, ap(c)), [a, c], [o])
+
+    def look(q, o, win, off):
+        if q == "v":
+            op("v", lambda: V.tensor_copy(ap(o), ap(win).indirect(ap(off))), [win, off], [o])
+        else:
+            op("s", lambda: S.activation(ap(o), ap(win).indirect(ap(off)), AF.Copy), [win, off], [o])
+
+    def iota(o, pat, base, cm):
+        op("g", lambda: g.iota(ap(o), pat, base, cm), [], [o])
+
+    dma("y", "ldn", T.NX[:, :], T.nxt[:, :], r("NX", 0, 768))
+    dma("s", "ldx0", T.X[:, 0:W], T.x[:, :], r("X", 0, W))
+    dma("y", "ldm", T.ME[:, :], T.mem[:, :], r("ME", 0, 256))
+    dma("y", "ldf", T.FR[:, :], T.fro[:, :], r("FR", 0, 256))
+    dma("y", "ldc", T.CU[:, :], T.cur[:, :], r("CU", 0, 384))
+    dma("y", "ldc", T.TY[:, :], T.typ[:, :], r("TY", 0, 128))
+    dma("s", "ldw", T.C2[:, 0:K], T.w0[:, :], r("C2", 0, K))
+    iota(r("PIi", 0, 1), [[1, 1]], 0, 1)
+    iota(r("COL", 0, 128), [[1, 128]], 0, 0)
+    iota(r("VI", 0, 256), [[1, 256]], 0, 256)
+    iota(r("RSi", 0, 128), [[0, 16], [1, 8]], 0, 0)
+
+    wait("g", ("ldx0", 0))
+    nloc = 0
+    for t in range(ROUNDS):
+        dst = T.cores[(rank - 1 - t) % len(T.cores)]
+        rid, pid, _se = topo.addr(dst)
+        g.remote_dma(T["xb%d" % t][:, :], T.X[:, 0:W], T.sem["x%d" % t], T.sem.xs, pid, rid, topo.mask(core, dst))
+        nloc += len(topo.engines(core, dst))
+        src = T.cores[(rank + 1 + t) % len(T.cores)]
+        count["x%d" % t] = len(topo.engines(src, core))
+        acc["xb%d" % t] = [(r("xb%d" % t, 0, W), True, ("x%d" % t, count["x%d" % t]), "dma")]
+
+    ts(r("PIi", 1, 2), r("PIi", 0, 1), 4, A.logical_shift_right)
+    ts(r("PIi", 2, 3), r("PIi", 0, 1), 15, A.bitwise_and)
+    ts(r("PIi", 3, 4), r("PIi", 0, 1), 63, A.bitwise_and)
+    cp(r("COF", 0, 128), r("COL", 0, 128))
+    cp(r("PIf", 0, 4), r("PIi", 0, 4))
+    pP, pG, pR, pC = (r("PIf", i, i + 1) for i in range(4))
+    cC, cG, cR, cQ = (r("COF", 128 * i, 128 * i + 128) for i in range(4))
+    ts(r("GM", 0, 8), r("COF", 0, 8), pG, A.is_equal)
+    ts(r("RM", 0, 16), r("COF", 0, 16), pR, A.is_equal)
+    cols = {}
+
+    def col(*terms):
+        key = ()
+        for (rw, wt) in terms:
+            prev = cols.get(key)
+            key = key + ((rw, wt),)
+            if key not in cols:
+                n = len(cols)
+                o = r("WC", n, n + 1)
+                if prev is None:
+                    ts(o, r("RM", rw, rw + 1), float(wt), A.mult)
+                else:
+                    ts(o, r("RM", rw, rw + 1), float(wt), A.mult, prev, A.add)
+                cols[key] = o
+        return cols[key]
+
+    def num(a, f=1):
+        return ((a, f), (a + 1, 64 * f))
+
+    def trow(rw, c0, c1):
+        return r("TB", c0, c1, 1, rw, 128, 16)
+
+    def rebuild(grp):
+        for i in range(2):
+            for d0, d1, s0, a in ((0, 2 * W, W, 1), (2 * W, 3 * W, 0, 1), (0, W, 2 * W, 2), (W, 3 * W, 0, 2)):
+                mv("y", grp, trow(2 * a + i, d0, d1), trow(i, s0, s0 + d1 - d0))
+
+    mset(r("TB", 2 * W, 3 * W + 256), 0.0)
+    for s in range(3):
+        fc = col((rS, s), (rDL, 1 if s < 2 else -2), (rONE, 1))
+        if s < 2:
+            ts(r("TB", W * s, W * s + W), r("TB", 2 * W, 3 * W), fc, A.add)
+        else:
+            act(r("TB", W * s, W * s + W), r("TB", W * s, W * s + W), AF.Identity, fc)
+    ts(r("NI", 0, 768), r("NX", 0, 768), 63, A.bitwise_and)
+    cp(r("NL", 0, 768), r("NI", 0, 768))
+    ts(r("VI", 0, 256), r("VI", 0, 256), 4095, A.bitwise_and)
+    ts(r("NI", 0, 768), r("NX", 0, 768), 6, A.logical_shift_right)
+    cp(r("NH", 0, 768), r("NI", 0, 768))
+    mv("y", "r1", trow(rNA, 0, 3 * W), r("NL", 0, 768))
+    mv("y", "r2", trow(rNA + 1, 0, 3 * W), r("NH", 0, 768))
+    ts(r("VJ", 0, 256), r("VI", 0, 256), 63, A.bitwise_and)
+    ts(r("VJ", 256, 512), r("VI", 0, 256), 6, A.logical_shift_right)
+    cp(r("VB", 0, 512), r("VJ", 0, 512))
+    ts(r("FI", 0, 256), r("FR", 0, 256), 63, A.bitwise_and)
+    ts(r("FI", 256, 512), r("FR", 0, 256), 6, A.logical_shift_right)
+    cp(r("FB", 0, 512), r("FI", 0, 512))
+    for i in range(3):
+        ts(r("MI", 256 * i, 256 * i + 256), r("ME", 0, 256), i, A.logical_shift_right, 1, A.bitwise_and)
+    ts(r("MJ", 0, 768), r("MI", 0, 768), -1.0, A.mult, 1.0, A.add)
+    for s in (1, 2):
+        act(r("X", W * s, W * s + W), r("X", 0, W), AF.Copy)
+    act(r("w", 0, K), r("C2", 0, K), AF.Copy)
+    for i in range(2):
+        mv("y", "r3", trow(rV + i, 0, W), r("VB", 256 * i, 256 * i + 256))
+    rebuild("r5")
+    for s in (0, 1):
+        for i in range(2):
+            mv("y", "r6", trow(rV + i, W * s + W, W * s + 2 * W), trow(rV + i, 0, W))
+    for i in range(2):
+        mv("y", "r4", trow(rFR + i, 0, W), r("FB", 256 * i, 256 * i + 256))
+    for s in range(3):
+        mv("y", "r7", trow(rJB, W * s, W * s + W), r("MJ", 256 * ((s + 1) % 3), 256 * ((s + 1) % 3) + 256))
+    for s in (0, 1):
+        for i in range(2):
+            mv("y", "r6", trow(rFR + i, W * s + W, W * s + 2 * W), trow(rFR + i, 0, W))
+    mv("y", "r8", trow(rJD, 0, 2 * W), trow(rJB, W, 3 * W))
+    mv("y", "r8", trow(rJD, 2 * W, 3 * W), trow(rJB, 0, W))
+
+    for i in range(3):
+        ts(r("EQ3", 128 * i, 128 * i + 128), r("TY", 0, 128), float(i), A.is_equal)
+        ts(r("CF", 128 * i, 128 * i + 128), r("CU", 128 * i, 128 * i + 128), float(W * i), A.add)
+    for n, L in enumerate(("LA", "LB", "LD")):
+        for i in range(3):
+            e = (i - n) % 3
+            tt(r("PR", 128 * i, 128 * i + 128), r("CF", 128 * i, 128 * i + 128), r("EQ3", 128 * e, 128 * e + 128), A.mult)
+        tt(r("NE", 0, 128), r("PR", 0, 128), r("PR", 128, 256), A.add)
+        tt(r("NE", 0, 128), r("NE", 0, 128), r("PR", 256, 384), A.add)
+        cp(r(L, 0, 128), r("NE", 0, 128))
+
+    ts(r("CO2", 0, 128), r("COL", 0, 128), 4, A.logical_shift_right)
+    ts(r("CO2", 128, 256), r("COL", 0, 128), 15, A.bitwise_and)
+    ts(r("CO2", 256, 384), r("COL", 0, 128), 63, A.bitwise_and)
+    cp(r("COF", 128, 512), r("CO2", 0, 384))
+    ts(r("RMX", 0, 128), cR, pR, A.is_equal)
+    ts(r("RMX", 128, 256), cR, pR, A.is_equal)
+    ts(r("BDm", 0, 128), cG, pG, A.is_equal)
+    ts(r("IDn", 0, 128), cC, pP, A.is_equal)
+    ts(r("OK", 0, 128), cQ, pC, A.is_equal)
+    cp(r("A1", 0, 128), r("OK", 0, 128))
+    ts(r("JX", 0, 128), cC, pP, A.is_ge)
+    tt(r("JX", 0, 128), r("JX", 0, 128), r("OK", 0, 128), A.mult)
+    tt(r("A2", 0, 128), r("JX", 0, 128), r("OK", 0, 128), A.subtract)
+    ts(r("A3", 0, 128), cQ, pC, A.is_gt)
+    mset(r("ON", 0, 128), 1.0)
+    ts(r("BX", 0, 128), cQ, pC, A.is_ge)
+    ts(r("OK", 0, 128), cC, 64.0, A.is_ge)
+    tt(r("EC0", 0, 128), r("BX", 0, 128), r("OK", 0, 128), A.max)
+    tt(r("EC1", 0, 128), r("BX", 0, 128), r("OK", 0, 128), A.mult)
+    cp(r("IOR", 0, 128), cC)
+    cp(r("BDb", 0, 128), r("BDm", 0, 128))
+    ts(r("GM16", 0, 8), r("GM", 0, 8), 16.0, A.mult)
+    mset(r("RKW", 128, 136), 9999.0)
+    mset(r("TG", 2048, 2064), 0.0)
+    mset(r("C2", 2048, 2064), 0.0)
+    ts(r("RS", 0, 128), r("RSi", 0, 128), 0.0, A.is_gt)
+    ts(r("KD", 0, 1), pP, -1.0, A.mult, 16384.0 - DUMP, A.add)
+    ts(r("KD", 1, 2), pP, -1.0, A.mult, 16384.0 - DUMP - 128, A.add)
+    ts(r("DL", 0, 16), r("COF", 0, 16), 16.0, A.mult, float(DUMP), A.add)
+    ts(r("DL", 0, 16), r("DL", 0, 16), pR, A.add)
+    for z in ("ZA0", "ZA1", "ZB0", "ZB1", "ZC0", "ZC1", "ZD0", "ZD1"):
+        mset(r(z, 0, 132), 0.0)
+
+    def wblock(buf, i, *terms):
+        sca(r(buf, 8 * i, 8 * i + 8), r("GM", 0, 8), col(*terms))
+
+    s4 = (rS, W)
+    packA = num(rV, W) + num(rNA)
+    packD = num(rV, W) + num(rND)
+    nextA = (s4,) + num(rNA)
+    for i, c in enumerate((packA, nextA)):
+        wblock("WR", i, *c)
+    minusA = ((rNA, -1), (rNA + 1, -64))
+    for i, c in enumerate((num(rNB), packD, ((rJB, 1),), ((rJD, 1),), minusA + num(rNB) + ((rDL, W),), packD, packA, nextA)):
+        wblock("WF", i, *c)
+    for i, c in enumerate((num(rV), packD, ((rJB, 1),), ((rJD, 1),), ((rDL, W),), packD, packA, num(rV) + (s4,))):
+        wblock("WL", i, *c)
+    for i in range(2):
+        cp(r("XW2", 8 * i, 8 * i + 8), r("GM", 0, 8))
+    for i, c in enumerate((num(rV), ((rONE, 1), (rJB, -1)), (s4, (rDL, W)), ((rONE, 3 * W), (rS, -2 * W), (rDL, -W)), num(rFR))):
+        wblock("WB", i, *c)
+    for i, c in enumerate(((s4, (rDL, W)), (s4,))):
+        pc = col(*(num(rV) + c + ((rONE, -16384),)))
+        sca(r("PG", 8 * i, 8 * i + 8), r("GM", 0, 8), pc)
+        sca(r("PMX", 128 * i, 128 * i + 128), r("BDm", 0, 128), pc)
+        for g_ in range(8):
+            sca(r("PB", 256 * g_ + 128 * i, 256 * g_ + 128 * i + 128), r("ON", 0, 128), r("PG", 8 * i + g_, 8 * i + g_ + 1))
+    isn = col((rNA, 1), (rNA + 1, 1))
+    ts(r("PIf", 5, 6), isn, -1.0, A.mult, 1.0, A.add)
+
+    def units(ps, src, c0, wbuf, n):
+        for b in range(16):
+            k, e = b // 2, b % 2
+            mm(r(ps, k, 64 * n, 8, 64 * e, 64 * e + 64), r(src, c0 + b, c0 + 1024, 16), r(wbuf, 0, 8 * n), True, True)
+
+    def zc(z):
+        return r(z, 1, 129, 2)
+
+    def turn(z, ps, pc):
+        mm(r(ps, pc, pc + 64), r(z, 1, 129), r("IDn", 0, 64), True, False)
+        mm(r(ps, pc, pc + 64), r(z, 0, 128), r("IDn", 64, 128), False, True)
+
+    def mklist(z, ps, pc, dst, h):
+        turn(z, ps, pc)
+        return lambda: cp(r(dst, 64 * h, 64 * h + 64), r(ps, pc, pc + 64))
+
+    TBw = r("TB", 0, DUMP + 256)
+
+    def ask(q, buf, L, h):
+        look(q, r(buf, 1024 * h, 1024 * h + 1024), TBw, r(L, 64 * h, 64 * h + 64))
+
+    def refresh():
+        for n, (buf, L) in enumerate((("TG", "LA"), ("C2", "LB"))):
+            for h in range(2):
+                ask("vs"[(h + n) % 2], buf, L, h)
+        fin = []
+        for h in range(2):
+            units("tb%d" % h, "TG", 1024 * h, "WR", 2)
+            cp(zc("ZA%d" % h), r("tb%d" % h, 64, 128))
+            fin.append(mklist("ZA%d" % h, "lb%d" % h, 0, "LA", h))
+            units("cb%d" % h, "C2", 1024 * h, "WR", 1)
+        for f in fin:
+            f()
+        ask("s", "TG", "LA", 0)
+        match(0, False)
+        for h in range(2):
+            ask("vs"[h], "D2", "LD", h)
+        ask("s", "TG", "LA", 1)
+        match(1, False)
+        for h in range(2):
+            st, pd = "ST%d" % h, ("pa", "pb")[h]
+            cp(r(st, 128, 192), r("cb%d" % h, 0, 64))
+            units(pd, "D2", 1024 * h, "WR", 1)
+            ts(r(st, 0, 64), r(st, 128, 192), 4095, A.bitwise_and)
+            cp(r(st, 64, 128), r(pd, 0, 64))
+
+    def match(h, last):
+        off = r("LA", 64 * h, 64 * h + 64)
+        xw, cm, wv = r("X", 0, 3 * W), r("CM%d" % h, 0, 1024), r("w", 1024 * h, 1024 * h + 1024)
+        op("v", lambda: V.tensor_tensor(ap(cm), ap(xw).indirect(ap(off)), ap(wv), A.is_ge), [xw, off, wv], [cm])
+        units("tb%d" % h, "TG", 1024 * h, "WL" if last else "WF", 8)
+
+    def names(h):
+        return ["%s%d" % (n, h) for n in ("tb", "cb", "ST", "u", "q", "p", "HM", "ZA")] + [("pa", "pb")[h]]
+
+    def before(h, last):
+        tb, cb, st, u, q, p, hm, z, dl = names(h)
+        sl = lambda a, b: r(tb, 64 * a, 64 * b)
+        if last:
+            ts(r(st, 0, 64), r(st, 128, 192), 12, A.logical_shift_right)
+        return [lambda: tt(r(u, 0, 128), r(st, 0, 128), sl(0, 2), A.subtract),
+                lambda: tt(r(dl, 0, 64), sl(6, 7), r(st, 64, 128), A.subtract),
+                lambda: tt(r(q, 0, 128), r(u, 0, 128), sl(2, 4), A.mult),
+                lambda: tt(sl(0, 2), r(q, 0, 128), sl(4, 6), A.add),
+                lambda: tt(r(dl, 64, 128), sl(1, 2), r(st, 128, 192), A.subtract)]
+
+    def counts(h):
+        units("cb%d" % h, "CM%d" % h, 0, "XW2", 2)
+
+    def hit(h):
+        act(r("HM%d" % h, 0, 128), r("cb%d" % h, 0, 128), AF.Sigmoid, -3400.0, 400.0)
+
+    def finds():
+        counts(0)
+        hit(0)
+        for f in before(0, False):
+            f()
+        for n in range(2 * FINDS):
+            h, last = n % 2, n // 2 == FINDS - 1
+            tb, cb, st, u, q, p, hm, z, dl = names(h)
+            nxt = before(1 - h, (n + 1) // 2 == FINDS - 1) if n + 1 < 2 * FINDS else []
+            step = lambda k: nxt[k]() if nxt else None
+            tt(r(p, 0, 64), r(tb, 0, 64), r(hm, 0, 64), A.mult)
+            step(0)
+            tt(zc(z), r(p, 0, 64), r(tb, 448, 512), A.add)
+            fin = mklist(z, "lb%d" % h, 0, "LA", h)
+            tt(r(dl, 0, 128), r(dl, 0, 128), r(hm, 0, 128), A.mult)
+            if nxt:
+                counts(1 - h)
+            step(2)
+            tt(r(st, 64, 192), r(st, 64, 192), r(dl, 0, 128), A.add)
+            step(1)
+            fin()
+            if not last:
+                ask("s", "TG", "LA", h)
+            if nxt:
+                hit(1 - h)
+            step(3)
+            if not last:
+                ts(r(st, 0, 64), r(st, 128, 192), 4095, A.bitwise_and)
+            step(4)
+            if not last:
+                match(h, n // 2 + 1 == FINDS - 1)
+
+    def boundary(t):
+        fast = t == ROUNDS - 1
+        for h in range(2):
+            ask("vs"[h], "TG", "LA", h)
+        for h in range(2):
+            ts(r("CD%d" % h, 0, 128), r("ST%d" % h, 64, 192), 12, A.logical_shift_right)
+            units("tb%d" % h, "TG", 1024 * h, "WB", 5)
+        fin = []
+        for h in range(2):
+            tb, cd = "tb%d" % h, "CD%d" % h
+            tt(zc("ZA%d" % h), r(tb, 128, 192), r(cd, 64, 128), A.add)
+            fin.append(mklist("ZA%d" % h, "lb%d" % h, 0, "LB", h))
+            tt(r("NE", 64 * h, 64 * h + 64), r(tb, 0, 64), r(cd, 64, 128), A.not_equal)
+            tt(r("WT", 64 * h, 64 * h + 64), r(tb, 64, 128), r("NE", 64 * h, 64 * h + 64), A.mult)
+        for f in fin:
+            f()
+        for h in range(2):
+            ask("s", "C2", "LB", h)
+        op("v", lambda: V.tensor_tensor_scan(T.INC[:, :], T.RS[:, :], T.WT[:, :], 0.0, A.mult, A.add), [r("RS", 0, 128), r("WT", 0, 128)], [r("INC", 0, 128)])
+        for h in range(2):
+            c = 64 * h
+            mm(r("pa", c, c + 64), r("A2", 0, 128), r("WT", c, c + 64), True, False)
+            mm(r("pa", c, c + 64), r("A1", 0, 128), r("INC", c, c + 64), False, False)
+            for k in range(8):
+                if h:
+                    mm(r("pa", c + k, c + 64, 8), r("ON", 0, 128), r("INC", 7, 64, 8), False, False)
+                mm(r("pa", c + k, c + 64, 8), r("A3", 0, 128), r("INC", c + 7, c + 64, 8), False, k == 7)
+        for h in range(2):
+            mm(r("pa", 128, 136), r("EC%d" % h, 0, 128), r("INC", 64 * h + 7, 64 * h + 64, 8), h == 0, h == 1)
+        cp(r("CEN", 0, 8), r("pa", 128, 136))
+        for h in range(2):
+            cp(zc("ZD%d" % h), r("pa", 64 * h, 64 * h + 64))
+            turn("ZD%d" % h, "cb%d" % h, 0)
+        for g_ in range(8):
+            ts(r("CP", 128 * g_, 128 * g_ + 128), r("IOR", 0, 128), r("CEN", g_, g_ + 1), A.is_ge)
+            mm(r("pb", 16 * g_, 16 * g_ + 16), r("CP", 128 * g_, 128 * g_ + 128), r("ON", 0, 16), True, True)
+        for h in range(2):
+            cp(r("RKW", 64 * h, 64 * h + 64), r("cb%d" % h, 0, 64))
+        tt(r("BX", 0, 128), r("pb", 0, 128), r("RMX", 0, 128), A.mult)
+        mm(r("pb", 128, 136), r("BX", 0, 128), r("GM", 0, 8), True, True)
+        fin = []
+        for h in range(2):
+            tb, cd = "tb%d" % h, "CD%d" % h
+            cp(zc("ZC%d" % h), r(tb, 256, 320))
+            fin.append(mklist("ZC%d" % h, "lb%d" % h, 0, "LK", h))
+            tt(zc("ZB%d" % h), r(tb, 192, 256), r(cd, 0, 64), A.add)
+            fin.append(mklist("ZB%d" % h, "lb%d" % h, 64, "LD", h))
+        for f in fin:
+            f()
+        cp(r("LQ", 0, 8), r("pb", 128, 136))
+        if fast:
+            pull(t, 0)
+        op("v", lambda: V.tensor_tensor(T.CP2[:, :], T.RKW[:, 0:136].indirect(T.LQ[:, 0:8]), ap(cC), A.is_le), [r("RKW", 0, 136), r("LQ", 0, 8), cC], [r("CP2", 0, 128)])
+        mm(r("pa", 0, 128), r("CP2", 0, 128), r("BDb", 0, 128), True, True)
+        if fast:
+            pull(t, 1)
+        tt(r("JX", 0, 128), r("pa", 0, 128), r("RMX", 0, 128), A.mult)
+        mm(r("pa", 128, 136), r("JX", 0, 128), r("GM", 0, 8), True, False)
+        mm(r("pa", 128, 136), r("BX", 0, 128), r("GM16", 0, 8), False, True)
+        cp(r("LJ", 0, 8), r("pa", 128, 136))
+        look("v", r("SM", 0, 128), r("TG", 0, 2064), r("LJ", 0, 8))
+        look("s", r("SC", 0, 128), r("C2", 0, 2064), r("LJ", 0, 8))
+        SWs = (r("SM", 0, 128), r("SC", 0, 128))
+        for i in range(2):
+            mm(r("pb", 128 * i, 128 * i + 128), SWs[i], r("PMX", 128 * i, 128 * i + 128), True, True)
+        cp(r("OW", 0, 256), r("pb", 0, 256))
+        banks = ("cb0", "cb1", "lb0", "lb1")
+        order = (4, 6, 0, 1, 7, 2, 3, 5)
+        for g_ in range(8):
+            b, o = banks[g_ // 2], 256 * (g_ % 2)
+            for i in range(2):
+                mm(r(b, o + 128 * i, o + 128 * i + 128), r("PB", 256 * g_ + 128 * i, 256 * g_ + 128 * i + 128), SWs[i], True, True)
+        for g_ in order:
+            b, o = banks[g_ // 2], 256 * (g_ % 2)
+            for i in range(2):
+                e, own = r("EQ", 512 * g_ + 256 * i, 512 * g_ + 256 * i + 256), r("OW", 128 * i + 16 * g_, 128 * i + 16 * g_ + 1)
+                if g_ < 5:
+                    ts(e, r(b, o, o + 256), own, A.is_equal)
+                else:
+                    y = r(("ya", "yb")[i], 0, 256)
+                    act(y, r(b, o, o + 256), AF.Abs, own, -1.0)
+                    act(e, y, AF.Relu, 1.0, -1.0)
+        for g_ in order:
+            for i in range(4):
+                mm(r("pa", 16 * g_, 16 * g_ + 16), r("EQ", 512 * g_ + 128 * i, 512 * g_ + 128 * i + 128), r("ON", 0, 16), i == 0, i == 3)
+        for i in range(2):
+            ts(r("Y", 128 * i, 128 * i + 128), r("OW", 128 * i, 128 * i + 128), r("KD", i, i + 1), A.add)
+        tt(r("Y", 0, 256), r("Y", 0, 256), r("RMX", 0, 256), A.mult)
+        ts(r("OK", 0, 128), r("pa", 0, 128), 2.5, A.is_le)
+        for i in range(2):
+            tt(r("YK", 128 * i, 128 * i + 128), r("Y", 128 * i, 128 * i + 128), r("OK", 0, 128), A.mult)
+            mm(r("pb", 8 * i, 8 * i + 8), r("YK", 128 * i, 128 * i + 128), r("GM", 0, 8), True, True)
+        tt(r("LPf", 0, 16), r("pb", 0, 16), r("DL", 0, 16), A.add)
+        cp(r("LP", 0, 16), r("LPf", 0, 16))
+        look("v", r("G3", 0, 256), TBw, r("LP", 0, 16))
+        ts(r("G4", 0, 256), r("G3", 0, 256), r("PIf", 5, 6), A.mult)
+        ts(r("G5", 0, 128), r("G3", 128, 256), isn, A.mult)
+        ts(r("G5", 128, 256), r("G3", 0, 128), isn, A.mult)
+        tt(r("G4", 0, 256), r("G4", 0, 256), r("G5", 0, 256), A.add)
+        op("v", lambda: V.tensor_copy(ap(TBw).indirect(T.LP[:, 0:16]), T.G4[:, :]), [r("G4", 0, 256), r("LP", 0, 16)], [TBw])
+        if fast:
+            for i, d in ((0, "NL"), (1, "NH")):
+                mv("ys"[i], "yl", r(d, 0, 768), trow(i, 0, 3 * W))
+        else:
+            rebuild("rb%d" % t)
+        for c in (2, 3) if fast else range(4):
+            pull(t, c)
+
+    def pull(t, c):
+        xb = r("xb%d" % t, 0, W)
+        d, wv = r("D%d" % (c % 2), 0, 512), r("w", 512 * c, 512 * c + 512)
+        off, cl = r("LK", 32 * c, 32 * c + 32), r("DD%d" % c, 0, 512)
+        op("v", lambda: V.tensor_tensor(ap(d), ap(xb).indirect(ap(off)), ap(wv), A.subtract), [xb, off, wv], [d])
+        if t == ROUNDS - 1 and c > 1:
+            cl = r("tb%d" % (c % 2), 0, 512)
+            ts(cl, d, -8.0, A.max, 8.0, A.min)
+            tt(wv, wv, cl, A.add)
+        else:
+            ts(cl, d, -8.0, A.max, 8.0, A.min)
+            add("wa%d%d" % (t, c // 2), wv, cl)
+
+    refresh()
+    for t in range(ROUNDS):
+        finds()
+        boundary(t)
+        if t < ROUNDS - 1:
+            refresh()
+    for i in range(2):
+        dma("y", "out%d" % i, T.yw[:, 1024 * i:1024 * i + 1024], T.w[:, 1024 * i:1024 * i + 1024], None, r("w", 1024 * i, 1024 * i + 1024))
+    for c0, c1, b in ((0, 512, "cb0"), (512, 768, "cb1")):
+        act(r(b, 0, c1 - c0), r("NH", c0, c1), AF.Copy, 0.0, 64.0)
+        tt(r("YF", c0, c1), r("NL", c0, c1), r(b, 0, c1 - c0), A.add)
+    dma("y", "out3", T.yn[:, :], T.YF[:, :], None, r("YF", 0, 768))
+    a_, b_, d_ = (r("PR", 128 * i, 128 * i + 128) for i in range(3))
+    y0, y1, y2 = (r("CF", 128 * i, 128 * i + 128) for i in range(3))
+    for k, L in ((a_, "LA"), (b_, "LB"), (d_, "LD")):
+        cp(k, r(L, 0, 128))
+    lo, hi, sm = (r("EQ3", 128 * i, 128 * i + 128) for i in range(3))
+    tt(lo, a_, b_, A.min)
+    tt(hi, a_, b_, A.max)
+    tt(sm, a_, b_, A.add)
+    tt(y0, lo, d_, A.min)
+    tt(hi, hi, d_, A.max)
+    tt(sm, sm, d_, A.add)
+    tt(sm, sm, y0, A.subtract)
+    ts(y2, hi, -2.0 * W, A.add)
+    tt(sm, sm, hi, A.subtract)
+    ts(y1, sm, -1.0 * W, A.add)
+    dma("y", "out2", T.yc[:, :], T.CF[:, :], None, r("CF", 0, 384))
+    for sem in SEMAPHORES:
+        if sem == "xs":
+            g.wait_ge(T.sem.xs, nloc)
+        elif count.get(sem, 0):
+            known["g"].pop(sem, None)
+            wait("g", (sem, count[sem]))

@@ -3,24 +3,31 @@ from concourse.mybir import AluOpType as A, ActivationFunctionType as AF
 ROUNDS, FINDS, W, K = 3, 6, 4096, 2048
 DUMP = 3 * W
 B, FL, IN, U16, SB = "bfloat16", "float32", "int32", "uint16", "sbuf"
-rNA, rNB, rND, rV, rJB, rJD, rFR, rS, rDL, rONE = 0, 2, 4, 6, 8, 9, 10, 12, 13, 14
+rNA, rNB, rND, rV, rJB, rJD, rFR, rU0, rU1, rONE, rTWO = 0, 2, 4, 6, 8, 9, 10, 12, 13, 14, 15
+BIG1, BIG2 = 2 ** 15, 2 ** 25
 
 SCRATCH = {}
 for _dt, _names in (
-    (B, "X:12288 TB:12544 xb0:4096 xb1:4096 xb2:4096 TG:2064 C2:2064 D2:2048 CM0:1024 CM1:1024 SM:128 SC:128 CP:1024 CP2:128 IOR:128 BDb:128 EC0:128 EC1:128 "
-        "NL:768 NH:768 MJ:768 FB:512 VB:512 HM0:128 HM1:128 WT:128 INC:128 A1:128 A2:128 A3:128 ON:128 WF:64 WL:64 WB:64 WR:64 XW2:16 PMX:256 PB:2048 EQ:4096 "
-        "G3:256 G4:256 G5:256"),
-    (FL, "w:2048 D0:512 D1:512 DD0:512 DD1:512 DD2:512 DD3:512 ya:256 yb:256 CF:384 EQ3:384 PR:384 u0:128 u1:128 p0:64 p1:64 q0:128 q1:128 "
-         "ZA0:132 ZA1:132 ZB0:132 ZB1:132 ZC0:132 ZC1:132 ZD0:132 ZD1:132 NE:128 RKW:136 CEN:8 BX:128 JX:128 GM16:8 PIf:8 COF:512 GM:8 RM:16 RMX:256 BDm:128 IDn:128 "
-         "RS:128 WC:64 PG:16 OW:256 OK:128 Y:256 YK:256 KD:2 DL:16 LPf:16 YF:768"),
-    (IN, "NX:768 NI:768 ME:256 MI:768 FR:256 FI:512 VI:256 VJ:512 CU:384 TY:128 ST0:192 ST1:192 CD0:128 CD1:128 PIi:4 COL:128 CO2:384 RSi:128"),
-    (U16, "LA:128 LB:128 LD:128 LK:128 LQ:8 LJ:8 LP:16"),
+    (B, "X:12288 TB:12288 TA:12544 xb0:4096 xb1:4096 xb2:4096 TG:2048 C2:2048 D2:2048 CM0:1024 CM1:1024 CP:1024 EQ:4096 "
+        "N1:768 N2:768 MJ:768 FB:512 VL:768 VH:768 ZR:256 HM0:128 HM1:128 WW:160 XW2:16 GM8:64 GK:16 ONb:128 TWO:128 IDb:128 BDb:128 BD2:128 "
+        "M1:128 M2:128 ISN:128 KEEP:128 RC:128 CUM:136 CB:128 NE0:64 NE1:64 G3:256 G4:256"),
+    (FL, "w:2048 D0:512 D1:512 DD0:512 DD1:512 DD2:512 DD3:512 E5:640 PR:1152 CF:384 y0:128 y1:128 p0:64 p1:64 ONf:256 IDn:128 BDf:128 "
+         "IO2:128 RS:256 RW:136 MW:136 CW:136 EE:128 PM:256 MK:256 OWS:256 OW1:16 DL:16 LPf:16 HV:4 YF:768"),
+    (IN, "NX:768 ME:256 MI:768 FR:256 CU:384 TY:128 CD0:128 CD1:128 HI:4 DI:16"),
+    (U16, "LA:128 LB:128 LD:128 LK:128 LQ:8 LG:16 LP:16 PU:256"),
 ):
     for _n in _names.split():
         SCRATCH[_n.split(":")[0]] = (SB, [128, int(_n.split(":")[1])], _dt)
+ZNAMES = "A0 A1 B0 D0 K0 M0 B1 D1 K1 M1".split()
+SCRATCH["ZF"] = (SB, [128, 16 * len(ZNAMES) + 1, 8], FL)
+SCRATCH["ZW"] = (SB, [128, 33, 8], B)
+SCRATCH["RMX"] = (SB, [128, 16, 16], FL)
+SCRATCH["OKX"] = (SB, [128, 8, 16], B)
+SCRATCH["ST0"] = (SB, [128, 3, 64], IN)
+SCRATCH["ST1"] = (SB, [128, 3, 64], IN)
 for _n in "tb0 tb1 cb0 cb1 lb0 lb1 pa pb".split():
     SCRATCH[_n] = ("psum", [128, 512], FL)
-GROUPS = "ldx0 ldw ldn ldm ldf ldc r1 r2 r3 r4 r5 r6 r7 r8 wa00 wa01 wa10 wa11 wa20 rb0 rb1 out0 out1 out2 out3 yl".split()
+GROUPS = "ldx ldw ldn ldm ldf ldc r1 r2 r3 r4 r5 r6 r7 cpa fra wa00 wa01 wa10 wa11 wa20 rb0 rb1 out0 out1 out2 yl".split()
 SEMAPHORES = ["qv", "qs", "qt", "qg", "xs", "x0", "x1", "x2"] + GROUPS
 
 
@@ -34,9 +41,18 @@ def rank_program(g, core, T, topo):
     count, known, clock, acc, closed = {}, {q: {} for q in Q}, {}, {}, {}
 
     def r(name, c0, c1, step=1, p0=0, p1=128, ps=1):
-        return (name, c0, c1, step, p0, p1, ps)
+        return (name, c0, c1, step, p0, p1, ps, None)
+
+    def r3(name, a0, a1, astep=1, b0=0, b1=None):
+        n = SCRATCH[name][1][2]
+        b1 = n if b1 is None else b1
+        last = a0 + (a1 - 1 - a0) // astep * astep
+        return (name, a0 * n + b0, last * n + b1, 1, 0, 128, 1, (a0, a1, astep, b0, b1))
 
     def ap(k):
+        if k[7]:
+            a0, a1, st, b0, b1 = k[7]
+            return T[k[0]][:, a0:a1:st, b0:b1]
         if k[6] != 1:
             return T[k[0]][k[4]:k[5]:k[6], k[1]:k[2]]
         if k[3] != 1:
@@ -44,7 +60,7 @@ def rank_program(g, core, T, topo):
         return T[k[0]][k[4]:k[5], k[1]:k[2]]
 
     def psum(n):
-        return SCRATCH[n][0] == "psum"
+        return n in SCRATCH and SCRATCH[n][0] == "psum"
 
     def meet(a, b):
         if a[1] >= b[2] or b[1] >= a[2] or a[4] >= b[5] or b[4] >= a[5]:
@@ -56,7 +72,10 @@ def rank_program(g, core, T, topo):
         return True
 
     def cover(a, b):
-        return a[3] == 1 and a[6] == 1 and a[1] <= b[1] and a[2] >= b[2] and a[4] <= b[4] and a[5] >= b[5]
+        if a == b:
+            return True
+        whole = a[7] is None or (a[7][2] == 1 and a[7][4] - a[7][3] == SCRATCH[a[0]][1][2])
+        return whole and a[3] == 1 and a[6] == 1 and a[1] <= b[1] and a[2] >= b[2] and a[4] <= b[4] and a[5] >= b[5]
 
     def wait(q, ev):
         sem, n = ev
@@ -123,6 +142,7 @@ def rank_program(g, core, T, topo):
         dma(q, grp, ap(o), ap(i), o, i)
 
     def add(grp, o, i):
+        assert not closed.get(grp)
         deps("g", [i], [o])
         count[grp] = count.get(grp, 0) + 16
         g.dma_start(ap(o), ap(i), accum_op=A.add).then_inc(T.sem[grp], 16)
@@ -146,15 +166,16 @@ def rank_program(g, core, T, topo):
     def mset(o, c):
         op("v", lambda: V.memset(ap(o), c), [], [o])
 
+    def scan(o, keep, a, init):
+        rd = [keep, a] + ([init] if isinstance(init, tuple) else [])
+        x = ap(init) if isinstance(init, tuple) else init
+        op("v", lambda: V.tensor_tensor_scan(ap(o), ap(keep), ap(a), x, A.mult, A.add), rd, [o])
+
     def mm(o, l, h, start, stop):
         op("t", lambda: P.matmul(ap(o), ap(l), ap(h), start, stop), [l, h], [o])
 
-    def act(o, a, f, bias=0.0, scale=1.0):
-        b = ap(bias) if isinstance(bias, tuple) else bias
-        op("s", lambda: S.activation(ap(o), ap(a), f, b, scale), [a] + ([bias] if isinstance(bias, tuple) else []), [o])
-
-    def sca(o, a, c):
-        op("s", lambda: S.activation(ap(o), ap(a), AF.Copy, 0.0, ap(c)), [a, c], [o])
+    def act(o, a, f=AF.Copy, bias=0.0, scale=1.0):
+        op("s", lambda: S.activation(ap(o), ap(a), f, bias, scale), [a], [o])
 
     def look(q, o, win, off):
         if q == "v":
@@ -162,438 +183,417 @@ def rank_program(g, core, T, topo):
         else:
             op("s", lambda: S.activation(ap(o), ap(win).indirect(ap(off)), AF.Copy), [win, off], [o])
 
-    def iota(o, pat, base, cm):
-        op("g", lambda: g.iota(ap(o), pat, base, cm), [], [o])
+    def lookt(o, win, off, b, f):
+        op("v", lambda: V.tensor_tensor(ap(o), ap(win).indirect(ap(off)), ap(b), f), [win, off, b], [o])
 
+    def iota(o, pat, base, cm):
+        if SCRATCH[o[0]][2] == IN:
+            op("g", lambda: g.iota(ap(o), pat, base, cm), [], [o])
+        else:
+            op("g", lambda: g.iota(ap(o), pat, base, cm, allow_small_or_imprecise_dtypes=True), [], [o])
+
+    def sel(o, a, pat, f, fill, base, cm):
+        op("g", lambda: g.affine_select(ap(o), ap(a), pat, f, float(fill), base, cm), [a], [o])
+
+    def band(o, a, pat):
+        sel(o, a, pat, A.is_ge, 0, 0, 1)
+        return lambda: sel(o, o, [[-s_, n] for s_, n in pat], A.is_ge, 0, 15, -1)
+
+    def mark(name):
+        pass
+
+    mark("setup")
     dma("y", "ldn", T.NX[:, :], T.nxt[:, :], r("NX", 0, 768))
-    dma("s", "ldx0", T.X[:, 0:W], T.x[:, :], r("X", 0, W))
     dma("y", "ldm", T.ME[:, :], T.mem[:, :], r("ME", 0, 256))
-    dma("y", "ldf", T.FR[:, :], T.fro[:, :], r("FR", 0, 256))
     dma("y", "ldc", T.CU[:, :], T.cur[:, :], r("CU", 0, 384))
     dma("y", "ldc", T.TY[:, :], T.typ[:, :], r("TY", 0, 128))
-    dma("s", "ldw", T.C2[:, 0:K], T.w0[:, :], r("C2", 0, K))
-    iota(r("PIi", 0, 1), [[1, 1]], 0, 1)
-    iota(r("COL", 0, 128), [[1, 128]], 0, 0)
-    iota(r("VI", 0, 256), [[1, 256]], 0, 256)
-    iota(r("RSi", 0, 128), [[0, 16], [1, 8]], 0, 0)
+    dma("y", "ldf", T.FR[:, :], T.fro[:, :], r("FR", 0, 256))
+    dma("y", "ldx", T.X[:, 0:W], T.x[:, :], r("X", 0, W))
 
-    wait("g", ("ldx0", 0))
-    nloc = 0
+    nloc = [0]
     for t in range(ROUNDS):
-        dst = T.cores[(rank - 1 - t) % len(T.cores)]
-        rid, pid, _se = topo.addr(dst)
-        g.remote_dma(T["xb%d" % t][:, :], T.X[:, 0:W], T.sem["x%d" % t], T.sem.xs, pid, rid, topo.mask(core, dst))
-        nloc += len(topo.engines(core, dst))
         src = T.cores[(rank + 1 + t) % len(T.cores)]
         count["x%d" % t] = len(topo.engines(src, core))
         acc["xb%d" % t] = [(r("xb%d" % t, 0, W), True, ("x%d" % t, count["x%d" % t]), "dma")]
 
-    ts(r("PIi", 1, 2), r("PIi", 0, 1), 4, A.logical_shift_right)
-    ts(r("PIi", 2, 3), r("PIi", 0, 1), 15, A.bitwise_and)
-    ts(r("PIi", 3, 4), r("PIi", 0, 1), 63, A.bitwise_and)
-    cp(r("COF", 0, 128), r("COL", 0, 128))
-    cp(r("PIf", 0, 4), r("PIi", 0, 4))
-    pP, pG, pR, pC = (r("PIf", i, i + 1) for i in range(4))
-    cC, cG, cR, cQ = (r("COF", 128 * i, 128 * i + 128) for i in range(4))
-    ts(r("GM", 0, 8), r("COF", 0, 8), pG, A.is_equal)
-    ts(r("RM", 0, 16), r("COF", 0, 16), pR, A.is_equal)
-    cols = {}
+    def send(t):
+        wait("g", ("ldx", 0))
+        wait("g", ("qv", count["qv"]) if t else ("r5", 0))
+        dst = T.cores[(rank - 1 - t) % len(T.cores)]
+        rid, pid, _se = topo.addr(dst)
+        g.remote_dma(T["xb%d" % t][:, :], T.X[:, 0:W], T.sem["x%d" % t], T.sem.xs, pid, rid, topo.mask(core, dst))
+        nloc[0] += len(topo.engines(core, dst))
 
-    def col(*terms):
-        key = ()
-        for (rw, wt) in terms:
-            prev = cols.get(key)
-            key = key + ((rw, wt),)
-            if key not in cols:
-                n = len(cols)
-                o = r("WC", n, n + 1)
-                if prev is None:
-                    ts(o, r("RM", rw, rw + 1), float(wt), A.mult)
-                else:
-                    ts(o, r("RM", rw, rw + 1), float(wt), A.mult, prev, A.add)
-                cols[key] = o
-        return cols[key]
+    one = lambda a, f=1: ((a, f), (a + 1, f))
+    rec = lambda f=1: ((rV, f), (rV + 1, 256 * f))
+    typ0 = ((rU0, 2 * W), (rU1, W), (rONE, -W))
+    step = ((rU0, -3 * W), (rU1, -3 * W))
+    typ1 = ((rU0, -W), (rU1, -2 * W), (rONE, 3 * W))
+    typ2 = ((rU0, -W), (rU1, W), (rONE, W))
+    packA = rec(W) + one(rNA)
+    packD = rec(W) + one(rND) + ((rJD, -BIG2),)
+    keepD = ((rONE, -BIG2), (rJD, BIG2))
+    own = ((rJB, BIG1), (rONE, 4 * W - BIG1))
+    new = ((rJB, -BIG1), (rONE, 4 * W))
+    WR = (packA, one(rNA) + typ0)
+    WF = (one(rNA, -1) + step + own, keepD, one(rNA, -1) + one(rNB) + step + new, packD, packA, one(rNA) + typ0)
+    WL = (rec(-1) + step + own, keepD, step + new, packD, packA, rec() + typ0)
+    WB = (rec(), ((rONE, 1), (rJB, -1)), typ1, typ2, one(rFR), rec() + typ1 + ((rTWO, 1),))
+    WPOS = {"R": 0, "F": 2, "L": 8, "B": 14}
 
-    def num(a, f=1):
-        return ((a, f), (a + 1, 64 * f))
+    def weights(*sets):
+        todo = [(WPOS[n] + i, list(terms)) for n, ws in sets for i, terms in enumerate(ws)]
+        while todo:
+            for a, terms in todo:
+                rw, wt = terms.pop()
+                k = r("WW", 8 * a, 8 * a + 8)
+                sel(k, k, [[-16, 8]], A.not_equal, wt, -rw, 1)
+            todo = [x for x in todo if x[1]]
 
-    def trow(rw, c0, c1):
-        return r("TB", c0, c1, 1, rw, 128, 16)
+    def wts(name, a0, n):
+        return r("WW", 8 * (WPOS[name] + a0), 8 * (WPOS[name] + a0 + n))
+
+    ONb, IDn, IDb, BDb, BDf = (r(n, 0, 128) for n in ("ONb", "IDn", "IDb", "BDb", "BDf"))
+    iota(r("WW", 0, 160), [[0, 160]], 0, 0)
+    iota(r("HI", 0, 3), [[1, 3]], 0, 3)
+    iota(r("VL", 0, 768), [[0, 3], [1, 256]], 0, 0)
+    iota(r("ONf", 0, 256), [[0, 256]], 1, 0)
+    sel(IDn, r("ONf", 0, 128), [[-1, 128]], A.is_equal, 0, 0, 1)
+    weights(("R", WR), ("F", WF))
+
+    def trow(tab, rw, c0, c1):
+        return r(tab, c0, c1, 1, rw, 128, 16)
 
     def rebuild(grp):
-        for i in range(2):
-            for d0, d1, s0, a in ((0, 2 * W, W, 1), (2 * W, 3 * W, 0, 1), (0, W, 2 * W, 2), (W, 3 * W, 0, 2)):
-                mv("y", grp, trow(2 * a + i, d0, d1), trow(i, s0, s0 + d1 - d0))
+        for d0, d1, s0, a in ((0, 3 * W, 0, 0), (0, 2 * W, W, 1), (W, 3 * W, 0, 2), (2 * W, 3 * W, 0, 1), (0, W, 2 * W, 2)):
+            for i in range(2):
+                mv("y", grp, trow("TB", 2 * a + i, d0, d1), trow("TA", i, s0, s0 + d1 - d0))
 
-    mset(r("TB", 2 * W, 3 * W + 256), 0.0)
-    for s in range(3):
-        fc = col((rS, s), (rDL, 1 if s < 2 else -2), (rONE, 1))
-        if s < 2:
-            ts(r("TB", W * s, W * s + W), r("TB", 2 * W, 3 * W), fc, A.add)
-        else:
-            act(r("TB", W * s, W * s + W), r("TB", W * s, W * s + W), AF.Identity, fc)
-    ts(r("NI", 0, 768), r("NX", 0, 768), 63, A.bitwise_and)
-    cp(r("NL", 0, 768), r("NI", 0, 768))
-    ts(r("VI", 0, 256), r("VI", 0, 256), 4095, A.bitwise_and)
-    ts(r("NI", 0, 768), r("NX", 0, 768), 6, A.logical_shift_right)
-    cp(r("NH", 0, 768), r("NI", 0, 768))
-    mv("y", "r1", trow(rNA, 0, 3 * W), r("NL", 0, 768))
-    mv("y", "r2", trow(rNA + 1, 0, 3 * W), r("NH", 0, 768))
-    ts(r("VJ", 0, 256), r("VI", 0, 256), 63, A.bitwise_and)
-    ts(r("VJ", 256, 512), r("VI", 0, 256), 6, A.logical_shift_right)
-    cp(r("VB", 0, 512), r("VJ", 0, 512))
-    ts(r("FI", 0, 256), r("FR", 0, 256), 63, A.bitwise_and)
-    ts(r("FI", 256, 512), r("FR", 0, 256), 6, A.logical_shift_right)
-    cp(r("FB", 0, 512), r("FI", 0, 512))
+    mset(r("TB", 0, K), 1.0)
+    for i in range(3, 6):
+        act(r("TB", K * i, K * i + K), r("TB", 0, K), AF.Sigmoid, 0.0, 400.0)
+    mset(r("TB", K, 3 * K), 1.0)
+    cp(r("N1", 0, 768), r("NX", 0, 768))
+    mset(r("ZR", 0, 256), 0.0)
+    mv("y", "r1", trow("TA", 0, 0, 3 * W), r("N1", 0, 768))
+    tt(r("N2", 0, 768), r("NX", 0, 768), r("N1", 0, 768), A.subtract)
+    mv("y", "r2", trow("TA", 1, 0, 3 * W), r("N2", 0, 768))
+    dma("y", "ldw", T.D2[:, 0:K], T.w0[:, :], r("D2", 0, K))
+    ts(r("HI", 0, 3), r("HI", 0, 3), 15, A.bitwise_and)
     for i in range(3):
-        ts(r("MI", 256 * i, 256 * i + 256), r("ME", 0, 256), i, A.logical_shift_right, 1, A.bitwise_and)
-    ts(r("MJ", 0, 768), r("MI", 0, 768), -1.0, A.mult, 1.0, A.add)
-    for s in (1, 2):
-        act(r("X", W * s, W * s + W), r("X", 0, W), AF.Copy)
-    act(r("w", 0, K), r("C2", 0, K), AF.Copy)
-    for i in range(2):
-        mv("y", "r3", trow(rV + i, 0, W), r("VB", 256 * i, 256 * i + 256))
+        ts(r("MI", 256 * i, 256 * i + 256), r("ME", 0, 256), 2 ** i, A.bitwise_and)
+    cp(r("HV", 0, 3), r("HI", 0, 3))
+    ts(r("MJ", 0, 768), r("MI", 0, 768), 0.0, A.is_equal)
+    for i in range(3):
+        ts(r("VH", 256 * i, 256 * i + 256), r("ZR", 0, 256), r("HV", i, i + 1), A.add)
+    mv("y", "r3", trow("TB", rU0, 0, W), r("ZR", 0, 256))
+    mv("y", "r3", trow("TB", rU1, W, 2 * W), r("ZR", 0, 256))
+    mv("y", "r3", trow("TB", rV, 0, 3 * W), r("VL", 0, 768))
+    mv("y", "r4", trow("TB", rV + 1, 0, 3 * W), r("VH", 0, 768))
+    for s in range(3):
+        for rw, o in ((rJB, 1), (rJD, 2)):
+            mv("y", "r4", trow("TB", rw, W * s, W * s + W), r("MJ", 256 * ((s + o) % 3), 256 * ((s + o) % 3) + 256))
     rebuild("r5")
-    for s in (0, 1):
-        for i in range(2):
-            mv("y", "r6", trow(rV + i, W * s + W, W * s + 2 * W), trow(rV + i, 0, W))
-    for i in range(2):
-        mv("y", "r4", trow(rFR + i, 0, W), r("FB", 256 * i, 256 * i + 256))
-    for s in range(3):
-        mv("y", "r7", trow(rJB, W * s, W * s + W), r("MJ", 256 * ((s + 1) % 3), 256 * ((s + 1) % 3) + 256))
-    for s in (0, 1):
-        for i in range(2):
-            mv("y", "r6", trow(rFR + i, W * s + W, W * s + 2 * W), trow(rFR + i, 0, W))
-    mv("y", "r8", trow(rJD, 0, 2 * W), trow(rJB, W, 3 * W))
-    mv("y", "r8", trow(rJD, 2 * W, 3 * W), trow(rJB, 0, W))
 
+    mset(r3("ZF", 0, 33), 0.0)
     for i in range(3):
-        ts(r("EQ3", 128 * i, 128 * i + 128), r("TY", 0, 128), float(i), A.is_equal)
-        ts(r("CF", 128 * i, 128 * i + 128), r("CU", 128 * i, 128 * i + 128), float(W * i), A.add)
-    for n, L in enumerate(("LA", "LB", "LD")):
+        ts(r("tb0", 128 * i, 128 * i + 128), r("CU", 128 * i, 128 * i + 128), float(W * i), A.add)
+    for i in range(5):
+        ts(r("E5", 128 * i, 128 * i + 128), r("TY", 0, 128), float((i + 1) % 3), A.is_equal)
+    for n in range(3):
+        tt(r("PR", 384 * n, 384 * n + 384), r("tb0", 0, 384), r("E5", 128 * (2 - n), 128 * (5 - n)), A.mult)
         for i in range(3):
-            e = (i - n) % 3
-            tt(r("PR", 128 * i, 128 * i + 128), r("CF", 128 * i, 128 * i + 128), r("EQ3", 128 * e, 128 * e + 128), A.mult)
-        tt(r("NE", 0, 128), r("PR", 0, 128), r("PR", 128, 256), A.add)
-        tt(r("NE", 0, 128), r("NE", 0, 128), r("PR", 256, 384), A.add)
-        cp(r(L, 0, 128), r("NE", 0, 128))
+            mm(r(("lb0", "lb1", "pa")[n], 0, 128), IDn, r("PR", 384 * n + 128 * i, 384 * n + 128 * i + 128), i == 0, i == 2)
+    mset(ONb, 1.0)
+    for n, L in enumerate(("LA", "LB", "LD")):
+        cp(r(L, 0, 128), r(("lb0", "lb1", "pa")[n], 0, 128))
+    cp(r("X", W, 2 * W), r("X", 0, W))
+    act(r("w", 0, K), r("D2", 0, K))
+    act(r("X", 2 * W, 3 * W), r("X", 0, W))
+    cp(r("FB", 0, 256), r("FR", 0, 256))
+    iota(r("DI", 0, 16), [[1, 16]], 0, 16)
+    band(r("XW2", 0, 16), r("ONb", 0, 16), [[0, 2], [-16, 8]])()
+    tt(r("FB", 256, 512), r("FR", 0, 256), r("FB", 0, 256), A.subtract)
+    ts(r("DI", 0, 16), r("DI", 0, 16), 255, A.bitwise_and)
+    mset(r("CUM", 0, 8), 0.0)
+    ts(r("DL", 0, 16), r("DI", 0, 16), float(DUMP), A.add)
 
-    ts(r("CO2", 0, 128), r("COL", 0, 128), 4, A.logical_shift_right)
-    ts(r("CO2", 128, 256), r("COL", 0, 128), 15, A.bitwise_and)
-    ts(r("CO2", 256, 384), r("COL", 0, 128), 63, A.bitwise_and)
-    cp(r("COF", 128, 512), r("CO2", 0, 384))
-    ts(r("RMX", 0, 128), cR, pR, A.is_equal)
-    ts(r("RMX", 128, 256), cR, pR, A.is_equal)
-    ts(r("BDm", 0, 128), cG, pG, A.is_equal)
-    ts(r("IDn", 0, 128), cC, pP, A.is_equal)
-    ts(r("OK", 0, 128), cQ, pC, A.is_equal)
-    cp(r("A1", 0, 128), r("OK", 0, 128))
-    ts(r("JX", 0, 128), cC, pP, A.is_ge)
-    tt(r("JX", 0, 128), r("JX", 0, 128), r("OK", 0, 128), A.mult)
-    tt(r("A2", 0, 128), r("JX", 0, 128), r("OK", 0, 128), A.subtract)
-    ts(r("A3", 0, 128), cQ, pC, A.is_gt)
-    mset(r("ON", 0, 128), 1.0)
-    ts(r("BX", 0, 128), cQ, pC, A.is_ge)
-    ts(r("OK", 0, 128), cC, 64.0, A.is_ge)
-    tt(r("EC0", 0, 128), r("BX", 0, 128), r("OK", 0, 128), A.max)
-    tt(r("EC1", 0, 128), r("BX", 0, 128), r("OK", 0, 128), A.mult)
-    cp(r("IOR", 0, 128), cC)
-    cp(r("BDb", 0, 128), r("BDm", 0, 128))
-    ts(r("GM16", 0, 8), r("GM", 0, 8), 16.0, A.mult)
-    mset(r("RKW", 128, 136), 9999.0)
-    mset(r("TG", 2048, 2064), 0.0)
-    mset(r("C2", 2048, 2064), 0.0)
-    ts(r("RS", 0, 128), r("RSi", 0, 128), 0.0, A.is_gt)
-    ts(r("KD", 0, 1), pP, -1.0, A.mult, 16384.0 - DUMP, A.add)
-    ts(r("KD", 1, 2), pP, -1.0, A.mult, 16384.0 - DUMP - 128, A.add)
-    ts(r("DL", 0, 16), r("COF", 0, 16), 16.0, A.mult, float(DUMP), A.add)
-    ts(r("DL", 0, 16), r("DL", 0, 16), pR, A.add)
-    for z in ("ZA0", "ZA1", "ZB0", "ZB1", "ZC0", "ZC1", "ZD0", "ZD1"):
-        mset(r(z, 0, 132), 0.0)
+    weights(("L", WL), ("B", WB))
 
-    def wblock(buf, i, *terms):
-        sca(r(buf, 8 * i, 8 * i + 8), r("GM", 0, 8), col(*terms))
+    def later():
+        mv("y", "cpa", r("TA", 0, 3 * W), r("TB", 0, 3 * W))
+        for s in range(3):
+            for i in range(2):
+                mv("y", "fra", trow("TA", rFR + i, W * s, W * s + W), r("FB", 256 * i, 256 * i + 256))
+        iota(r3("ZF", 33, 16 * len(ZNAMES) + 1), [[0, 1024]], 0, 0)
+        iota(r3("ZW", 0, 33), [[0, 264]], 0, 0)
+        iota(r3("RMX", 0, 16), [[0, 256]], 0, 0)
+        iota(r("TWO", 0, 128), [[0, 128]], 2, 0)
+        iota(r("GK", 0, 16), [[0, 16]], 16384, 0)
+        for n in ("RW", "MW", "CW"):
+            iota(r(n, 128, 136), [[0, 8]], 0, 0)
+        fin = [band(BDb, ONb, [[-16, 8], [0, 16]]), band(BDf, r("ONf", 0, 128), [[-16, 8], [0, 16]]),
+               band(r("BD2", 0, 128), r("TWO", 0, 128), [[-16, 8], [0, 16]]), band(r("GM8", 0, 64), r("ONb", 0, 64), [[-16, 8], [0, 8]]),
+               band(r("GK", 0, 16), r("GK", 0, 16), [[0, 2], [-16, 8]])]
+        sel(IDb, ONb, [[-1, 128]], A.is_equal, 0, 0, 1)
+        for f in fin:
+            f()
+        iota(r("RC", 0, 128), [[0, 8], [1, 16]], 0, 0)
+        iota(r("IO2", 0, 128), [[2, 128]], 1, 0)
+        sel(r("RS", 0, 256), r("ONf", 0, 256), [[0, 16], [1, 16]], A.is_gt, 0, 0, 0)
+        sel(r("ISN", 0, 128), IDb, [[0, 8], [-1, 16]], A.is_ge, 0, 1, 0)
+        sel(r("KEEP", 0, 128), IDb, [[0, 8], [1, 16]], A.is_ge, 0, -2, 0)
+        sel(r("M1", 0, 128), r("BD2", 0, 128), [[1, 128]], A.is_gt, 0, 0, -1)
+        sel(r("M2", 0, 128), r("BD2", 0, 128), [[-1, 128]], A.is_gt, 0, 0, 1)
+        for n in ("M1", "M2"):
+            sel(r(n, 0, 128), r(n, 0, 128), [[-1, 128]], A.not_equal, 1, 0, 1)
+        for k in range(8):
+            sel(r3("RMX", 0, 16), r3("RMX", 0, 16), [[0, 16], [-1, 16]], A.not_equal, 1, -16 * k, 1)
 
-    s4 = (rS, W)
-    packA = num(rV, W) + num(rNA)
-    packD = num(rV, W) + num(rND)
-    nextA = (s4,) + num(rNA)
-    for i, c in enumerate((packA, nextA)):
-        wblock("WR", i, *c)
-    minusA = ((rNA, -1), (rNA + 1, -64))
-    for i, c in enumerate((num(rNB), packD, ((rJB, 1),), ((rJD, 1),), minusA + num(rNB) + ((rDL, W),), packD, packA, nextA)):
-        wblock("WF", i, *c)
-    for i, c in enumerate((num(rV), packD, ((rJB, 1),), ((rJD, 1),), ((rDL, W),), packD, packA, num(rV) + (s4,))):
-        wblock("WL", i, *c)
-    for i in range(2):
-        cp(r("XW2", 8 * i, 8 * i + 8), r("GM", 0, 8))
-    for i, c in enumerate((num(rV), ((rONE, 1), (rJB, -1)), (s4, (rDL, W)), ((rONE, 3 * W), (rS, -2 * W), (rDL, -W)), num(rFR))):
-        wblock("WB", i, *c)
-    for i, c in enumerate(((s4, (rDL, W)), (s4,))):
-        pc = col(*(num(rV) + c + ((rONE, -16384),)))
-        sca(r("PG", 8 * i, 8 * i + 8), r("GM", 0, 8), pc)
-        sca(r("PMX", 128 * i, 128 * i + 128), r("BDm", 0, 128), pc)
-        for g_ in range(8):
-            sca(r("PB", 256 * g_ + 128 * i, 256 * g_ + 128 * i + 128), r("ON", 0, 128), r("PG", 8 * i + g_, 8 * i + g_ + 1))
-    isn = col((rNA, 1), (rNA + 1, 1))
-    ts(r("PIf", 5, 6), isn, -1.0, A.mult, 1.0, A.add)
+    def units(ps, src, c0, wk):
+        n = wk[2] - wk[1]
+        for b in range(8):
+            mm(r(ps, b, 8 * n, 8), r(src, c0 + b, c0 + 1024, 8), wk, True, True)
 
-    def units(ps, src, c0, wbuf, n):
-        for b in range(16):
-            k, e = b // 2, b % 2
-            mm(r(ps, k, 64 * n, 8, 64 * e, 64 * e + 64), r(src, c0 + b, c0 + 1024, 16), r(wbuf, 0, 8 * n), True, True)
-
-    def zc(z):
-        return r(z, 1, 129, 2)
+    def zin(z, n=1):
+        i = 16 * ZNAMES.index(z)
+        return r3("ZF", i + 1, i + 16 * n, 2)
 
     def turn(z, ps, pc):
-        mm(r(ps, pc, pc + 64), r(z, 1, 129), r("IDn", 0, 64), True, False)
-        mm(r(ps, pc, pc + 64), r(z, 0, 128), r("IDn", 64, 128), False, True)
+        if z[0] == "W":
+            buf, i, ident = "ZW", 16 * int(z[1]), "IDb"
+        else:
+            buf, i, ident = "ZF", 16 * ZNAMES.index(z), "IDn"
+        mm(r(ps, pc, pc + 64), r3(buf, i + 1, i + 17), r(ident, 0, 128, 2), True, False)
+        mm(r(ps, pc, pc + 64), r3(buf, i, i + 16), r(ident, 1, 128, 2), False, True)
 
-    def mklist(z, ps, pc, dst, h):
-        turn(z, ps, pc)
-        return lambda: cp(r(dst, 64 * h, 64 * h + 64), r(ps, pc, pc + 64))
+    def ask(q, buf, tab, L, h, c0=0, c1=64):
+        look(q, r(buf, 1024 * h + 16 * c0, 1024 * h + 16 * c1), r(tab, 0, DUMP), r(L, 64 * h + c0, 64 * h + c1))
 
-    TBw = r("TB", 0, DUMP + 256)
-
-    def ask(q, buf, L, h):
-        look(q, r(buf, 1024 * h, 1024 * h + 1024), TBw, r(L, 64 * h, 64 * h + 64))
-
-    def refresh():
-        for n, (buf, L) in enumerate((("TG", "LA"), ("C2", "LB"))):
-            for h in range(2):
-                ask("vs"[(h + n) % 2], buf, L, h)
-        fin = []
-        for h in range(2):
-            units("tb%d" % h, "TG", 1024 * h, "WR", 2)
-            cp(zc("ZA%d" % h), r("tb%d" % h, 64, 128))
-            fin.append(mklist("ZA%d" % h, "lb%d" % h, 0, "LA", h))
-            units("cb%d" % h, "C2", 1024 * h, "WR", 1)
-        for f in fin:
-            f()
-        ask("s", "TG", "LA", 0)
-        match(0, False)
-        for h in range(2):
-            ask("vs"[h], "D2", "LD", h)
-        ask("s", "TG", "LA", 1)
-        match(1, False)
-        for h in range(2):
-            st, pd = "ST%d" % h, ("pa", "pb")[h]
-            cp(r(st, 128, 192), r("cb%d" % h, 0, 64))
-            units(pd, "D2", 1024 * h, "WR", 1)
-            ts(r(st, 0, 64), r(st, 128, 192), 4095, A.bitwise_and)
-            cp(r(st, 64, 128), r(pd, 0, 64))
-
-    def match(h, last):
-        off = r("LA", 64 * h, 64 * h + 64)
-        xw, cm, wv = r("X", 0, 3 * W), r("CM%d" % h, 0, 1024), r("w", 1024 * h, 1024 * h + 1024)
-        op("v", lambda: V.tensor_tensor(ap(cm), ap(xw).indirect(ap(off)), ap(wv), A.is_ge), [xw, off, wv], [cm])
-        units("tb%d" % h, "TG", 1024 * h, "WL" if last else "WF", 8)
-
-    def names(h):
-        return ["%s%d" % (n, h) for n in ("tb", "cb", "ST", "u", "q", "p", "HM", "ZA")] + [("pa", "pb")[h]]
-
-    def before(h, last):
-        tb, cb, st, u, q, p, hm, z, dl = names(h)
-        sl = lambda a, b: r(tb, 64 * a, 64 * b)
-        if last:
-            ts(r(st, 0, 64), r(st, 128, 192), 12, A.logical_shift_right)
-        return [lambda: tt(r(u, 0, 128), r(st, 0, 128), sl(0, 2), A.subtract),
-                lambda: tt(r(dl, 0, 64), sl(6, 7), r(st, 64, 128), A.subtract),
-                lambda: tt(r(q, 0, 128), r(u, 0, 128), sl(2, 4), A.mult),
-                lambda: tt(sl(0, 2), r(q, 0, 128), sl(4, 6), A.add),
-                lambda: tt(r(dl, 64, 128), sl(1, 2), r(st, 128, 192), A.subtract)]
-
-    def counts(h):
-        units("cb%d" % h, "CM%d" % h, 0, "XW2", 2)
+    def match(h):
+        lookt(r("CM%d" % h, 0, 1024), r("X", 0, 3 * W), r("LA", 64 * h, 64 * h + 64), r("w", 1024 * h, 1024 * h + 1024), A.is_ge)
 
     def hit(h):
+        units("cb%d" % h, "CM%d" % h, 0, r("XW2", 0, 16))
         act(r("HM%d" % h, 0, 128), r("cb%d" % h, 0, 128), AF.Sigmoid, -3400.0, 400.0)
 
-    def finds():
-        counts(0)
+    def first(h):
+        units("tb%d" % h, "TG", 1024 * h, wts("R", 1, 1))
+        cp(zin("A%d" % h), r("tb%d" % h, 0, 64))
+        turn("A%d" % h, "lb%d" % h, 0)
+        return lambda: cp(r("LA", 64 * h, 64 * h + 64), r("lb%d" % h, 0, 64))
+
+    def state(h, i):
+        ps = ("pa", "pb")[h]
+        units(ps, ("C2", "D2")[i - 1], 1024 * h, wts("R", 0, 1))
+        cp(r3("ST%d" % h, i, i + 1), r(ps, 0, 64))
+
+    def nextof(h, last):
+        st = "ST%d" % h
+        if last:
+            ts(r3(st, 0, 1), r3(st, 1, 2), 12, A.logical_shift_right)
+        else:
+            ts(r3(st, 0, 1), r3(st, 1, 2), 4095, A.bitwise_and)
+
+    def refresh(tab, t):
+        mark("ref%d" % t)
+        ask("s", "TG", tab, "LA", 0)
+        if t:
+            ask("s", "TG", tab, "LA", 1)
+            for c in (2, 3):
+                pull(t - 1, c)
+        else:
+            ask("v", "TG", tab, "LA", 1)
+        f0 = first(0)
+        ask("s", "D2", tab, "LD", 0)
+        if not t:
+            ask("v", "C2", tab, "LB", 0)
+        f0()
+        f1 = first(1)
+        ask("s", "TG", "TB", "LA", 0)
+        match(0)
+        f1()
+        state(0, 2)
+        if t:
+            ask("v", "C2", tab, "LB", 0)
         hit(0)
-        for f in before(0, False):
-            f()
+        units("tb0", "TG", 0, wts("F", 0, 6))
+        ask("s", "TG", "TB", "LA", 1)
+        ask("v", "D2", tab, "LD", 1)
+        ask("s", "C2", tab, "LB", 1)
+        state(0, 1)
+        match(1)
+        nextof(0, False)
+
+    def settle(h):
+        dl, st = r(("pa", "pb")[h], 0, 128), r3("ST%d" % h, 1, 3)
+        return (lambda: tt(dl, dl, r("HM%d" % h, 0, 128), A.mult)), (lambda: tt(st, st, dl, A.add))
+
+    def finds(t):
+        mark("find%d" % t)
         for n in range(2 * FINDS):
-            h, last = n % 2, n // 2 == FINDS - 1
-            tb, cb, st, u, q, p, hm, z, dl = names(h)
-            nxt = before(1 - h, (n + 1) // 2 == FINDS - 1) if n + 1 < 2 * FINDS else []
-            step = lambda k: nxt[k]() if nxt else None
-            tt(r(p, 0, 64), r(tb, 0, 64), r(hm, 0, 64), A.mult)
-            step(0)
-            tt(zc(z), r(p, 0, 64), r(tb, 448, 512), A.add)
-            fin = mklist(z, "lb%d" % h, 0, "LA", h)
-            tt(r(dl, 0, 128), r(dl, 0, 128), r(hm, 0, 128), A.mult)
-            if nxt:
-                counts(1 - h)
-            step(2)
-            tt(r(st, 64, 192), r(st, 64, 192), r(dl, 0, 128), A.add)
-            step(1)
-            fin()
-            if not last:
-                ask("s", "TG", "LA", h)
-            if nxt:
-                hit(1 - h)
-            step(3)
-            if not last:
-                ts(r(st, 0, 64), r(st, 128, 192), 4095, A.bitwise_and)
-            step(4)
-            if not last:
-                match(h, n // 2 + 1 == FINDS - 1)
+            h, o, q = n % 2, 1 - n % 2, n // 2
+            tb, st, y, p = "tb%d" % h, "ST%d" % h, r("y%d" % h, 0, 128), r("p%d" % h, 0, 64)
+            mult, plus = settle(o)
+            tt(y, r3(st, 0, 3, 2), r(tb, 0, 128), A.add)
+            if n:
+                mult()
+            hit(o) if n + 1 < 2 * FINDS else None
+            tt(r(tb, 128, 256), y, r(tb, 128, 256), A.max)
+            if n:
+                plus()
+            else:
+                state(1, 1)
+            tt(p, r(tb, 128, 192), r("HM%d" % h, 0, 64), A.mult)
+            if n == 0:
+                state(1, 2)
+            if n + 1 < 2 * FINDS:
+                nextof(o, (n + 1) // 2 == FINDS - 1)
+            tt(zin("A%d" % h), p, r(tb, 320, 384), A.add)
+            turn("A%d" % h, "lb%d" % h, 0)
+            tt(r(("pa", "pb")[h], 0, 128), r(tb, 192, 320), r3(st, 1, 3), A.subtract)
+            if n + 1 < 2 * FINDS:
+                units("tb%d" % o, "TG", 1024 * o, wts("L" if (n + 1) // 2 == FINDS - 1 else "F", 0, 6))
+            cp(r("LA", 64 * h, 64 * h + 64), r("lb%d" % h, 0, 64))
+            if q < FINDS - 1:
+                ask("s", "TG", "TB", "LA", h)
+                match(h)
+            elif h == 0:
+                ask("s", "TG", "TA", "LA", 0)
+
+    def wants(h):
+        tb, cd = "tb%d" % h, "CD%d" % h
+        tt(r("NE%d" % h, 0, 64), r(tb, 0, 64), r(cd, 0, 64), A.not_equal)
+        tt(zin("B%d" % h, 2), r(tb, 128, 256), r(cd, 0, 128), A.add)
+        tt(r3("ZW", 16 * h + 1, 16 * h + 16, 2), r(tb, 64, 128), r("NE%d" % h, 0, 64), A.mult)
+        act(zin("K%d" % h, 2), r(tb, 256, 384))
+        turn("W%d" % h, "lb1", 64 * h)
 
     def boundary(t):
+        mark("bnd%d" % t)
         fast = t == ROUNDS - 1
+        mult, plus = settle(1)
+        cursors = lambda h: ts(r("CD%d" % h, 0, 128), r3("ST%d" % h, 1, 3), 12, A.logical_shift_right)
+        ask("s", "TG", "TA", "LA", 1, 48, 64)
+        ask("v", "TG", "TA", "LA", 1, 0, 48)
+        units("tb0", "TG", 0, wts("B", 0, 6))
+        units("tb1", "TG", 1024, wts("B", 0, 6))
+        mult()
+        cursors(0)
+        plus()
+        wants(0)
+        cursors(1)
+        turn("K0", "cb0", 0)
+        scan(r("CUM", 1, 65), r("ONb", 0, 64), r("lb1", 0, 64), 0.0)
+        wants(1)
+        cp(r("LK", 0, 64), r("cb0", 0, 64))
+        scan(r("CUM", 65, 129), r("ONb", 0, 64), r("lb1", 64, 128), r("CUM", 64, 65))
+        mm(r("pa", 0, 128), r("CUM", 1, 129), BDb, True, True)
+        mm(r("pb", 0, 128), r("M1", 0, 128), r("CUM", 1, 129), True, False)
+        mm(r("pb", 0, 128), r("M2", 0, 128), r("CUM", 0, 128), False, True)
+        act(r("RW", 0, 128), r("pb", 0, 128))
+        turn("M0", "lb0", 0)
+        pull(t, 0, 0)
+        tt(r("CB", 0, 128), r("pa", 0, 128), r("RC", 0, 128), A.subtract)
+        turn("M1", "lb0", 64)
+        for k in range(8):
+            ts(r("CP", 128 * k, 128 * k + 128), r("CB", 0, 128), 16.0 * k, A.is_le)
+        for k in range(8):
+            mm(r("lb1", 128 + k, 129 + k), r("CP", 128 * k, 128 * k + 128), r("ONb", 0, 1), True, True)
+        act(r("MW", 0, 128), r("lb0", 0, 128))
         for h in range(2):
-            ask("vs"[h], "TG", "LA", h)
+            turn("B%d" % h, "cb1", 64 * h)
+        act(r("CW", 0, 128), r("cb1", 0, 128), AF.Identity, 1.0)
+        pull(t, 0, 1)
+        cp(r("LQ", 0, 8), r("lb1", 128, 136))
+        turn("K1", "cb0", 64)
+        LQ, EE = r("LQ", 0, 8), r("EE", 0, 128)
+        lookt(EE, r("RW", 0, 136), LQ, r("IO2", 0, 128), A.is_equal)
+        cp(r("LK", 64, 128), r("cb0", 64, 128))
+        for i, n in enumerate(("MW", "CW")):
+            lookt(r("PM", 128 * i, 128 * i + 128), r(n, 0, 136), LQ, EE, A.mult)
+            mm(r("pa", 128 * i, 128 * i + 128), BDf, r("PM", 128 * i, 128 * i + 128), True, True)
         for h in range(2):
-            ts(r("CD%d" % h, 0, 128), r("ST%d" % h, 64, 192), 12, A.logical_shift_right)
-            units("tb%d" % h, "TG", 1024 * h, "WB", 5)
-        fin = []
-        for h in range(2):
-            tb, cd = "tb%d" % h, "CD%d" % h
-            tt(zc("ZA%d" % h), r(tb, 128, 192), r(cd, 64, 128), A.add)
-            fin.append(mklist("ZA%d" % h, "lb%d" % h, 0, "LB", h))
-            tt(r("NE", 64 * h, 64 * h + 64), r(tb, 0, 64), r(cd, 64, 128), A.not_equal)
-            tt(r("WT", 64 * h, 64 * h + 64), r(tb, 64, 128), r("NE", 64 * h, 64 * h + 64), A.mult)
-        for f in fin:
-            f()
-        for h in range(2):
-            ask("s", "C2", "LB", h)
-        op("v", lambda: V.tensor_tensor_scan(T.INC[:, :], T.RS[:, :], T.WT[:, :], 0.0, A.mult, A.add), [r("RS", 0, 128), r("WT", 0, 128)], [r("INC", 0, 128)])
-        for h in range(2):
-            c = 64 * h
-            mm(r("pa", c, c + 64), r("A2", 0, 128), r("WT", c, c + 64), True, False)
-            mm(r("pa", c, c + 64), r("A1", 0, 128), r("INC", c, c + 64), False, False)
-            for k in range(8):
-                if h:
-                    mm(r("pa", c + k, c + 64, 8), r("ON", 0, 128), r("INC", 7, 64, 8), False, False)
-                mm(r("pa", c + k, c + 64, 8), r("A3", 0, 128), r("INC", c + 7, c + 64, 8), False, k == 7)
-        for h in range(2):
-            mm(r("pa", 128, 136), r("EC%d" % h, 0, 128), r("INC", 64 * h + 7, 64 * h + 64, 8), h == 0, h == 1)
-        cp(r("CEN", 0, 8), r("pa", 128, 136))
-        for h in range(2):
-            cp(zc("ZD%d" % h), r("pa", 64 * h, 64 * h + 64))
-            turn("ZD%d" % h, "cb%d" % h, 0)
-        for g_ in range(8):
-            ts(r("CP", 128 * g_, 128 * g_ + 128), r("IOR", 0, 128), r("CEN", g_, g_ + 1), A.is_ge)
-            mm(r("pb", 16 * g_, 16 * g_ + 16), r("CP", 128 * g_, 128 * g_ + 128), r("ON", 0, 16), True, True)
-        for h in range(2):
-            cp(r("RKW", 64 * h, 64 * h + 64), r("cb%d" % h, 0, 64))
-        tt(r("BX", 0, 128), r("pb", 0, 128), r("RMX", 0, 128), A.mult)
-        mm(r("pb", 128, 136), r("BX", 0, 128), r("GM", 0, 8), True, True)
-        fin = []
-        for h in range(2):
-            tb, cd = "tb%d" % h, "CD%d" % h
-            cp(zc("ZC%d" % h), r(tb, 256, 320))
-            fin.append(mklist("ZC%d" % h, "lb%d" % h, 0, "LK", h))
-            tt(zc("ZB%d" % h), r(tb, 192, 256), r(cd, 0, 64), A.add)
-            fin.append(mklist("ZB%d" % h, "lb%d" % h, 64, "LD", h))
-        for f in fin:
-            f()
-        cp(r("LQ", 0, 8), r("pb", 128, 136))
-        if fast:
-            pull(t, 0)
-        op("v", lambda: V.tensor_tensor(T.CP2[:, :], T.RKW[:, 0:136].indirect(T.LQ[:, 0:8]), ap(cC), A.is_le), [r("RKW", 0, 136), r("LQ", 0, 8), cC], [r("CP2", 0, 128)])
-        mm(r("pa", 0, 128), r("CP2", 0, 128), r("BDb", 0, 128), True, True)
-        if fast:
-            pull(t, 1)
-        tt(r("JX", 0, 128), r("pa", 0, 128), r("RMX", 0, 128), A.mult)
-        mm(r("pa", 128, 136), r("JX", 0, 128), r("GM", 0, 8), True, False)
-        mm(r("pa", 128, 136), r("BX", 0, 128), r("GM16", 0, 8), False, True)
-        cp(r("LJ", 0, 8), r("pa", 128, 136))
-        look("v", r("SM", 0, 128), r("TG", 0, 2064), r("LJ", 0, 8))
-        look("s", r("SC", 0, 128), r("C2", 0, 2064), r("LJ", 0, 8))
-        SWs = (r("SM", 0, 128), r("SC", 0, 128))
-        for i in range(2):
-            mm(r("pb", 128 * i, 128 * i + 128), SWs[i], r("PMX", 128 * i, 128 * i + 128), True, True)
-        cp(r("OW", 0, 256), r("pb", 0, 256))
-        banks = ("cb0", "cb1", "lb0", "lb1")
-        order = (4, 6, 0, 1, 7, 2, 3, 5)
-        for g_ in range(8):
-            b, o = banks[g_ // 2], 256 * (g_ % 2)
+            turn("D%d" % h, "cb0", 128 + 64 * h)
+        pull(t, 1, 0)
+        tt(r("MK", 0, 256), r("pa", 0, 256), r3("RMX", 0, 16), A.mult)
+        cp(r("PU", 0, 256), r("pa", 0, 256))
+        scan(r("OWS", 0, 256), r("RS", 0, 256), r("MK", 0, 256), 0.0)
+        pull(t, 1, 1)
+        ow = r("OWS", 15, 256, 16)
+        ts(r("LG", 0, 16), ow, -1.0, A.add)
+        look("s", r("G3", 0, 256), r("TA", 0, DUMP), r("LG", 0, 16))
+        ts(r("OW1", 0, 16), ow, -1.0 - 2 * 16384, A.add)
+        for k in range(16):
+            e = r("EQ", 256 * k, 256 * k + 256)
+            ts(e, r("PU", 0, 256), r("OWS", 16 * k + 15, 16 * k + 16), A.is_equal)
             for i in range(2):
-                mm(r(b, o + 128 * i, o + 128 * i + 128), r("PB", 256 * g_ + 128 * i, 256 * g_ + 128 * i + 128), SWs[i], True, True)
-        for g_ in order:
-            b, o = banks[g_ // 2], 256 * (g_ % 2)
-            for i in range(2):
-                e, own = r("EQ", 512 * g_ + 256 * i, 512 * g_ + 256 * i + 256), r("OW", 128 * i + 16 * g_, 128 * i + 16 * g_ + 1)
-                if g_ < 5:
-                    ts(e, r(b, o, o + 256), own, A.is_equal)
-                else:
-                    y = r(("ya", "yb")[i], 0, 256)
-                    act(y, r(b, o, o + 256), AF.Abs, own, -1.0)
-                    act(e, y, AF.Relu, 1.0, -1.0)
-        for g_ in order:
-            for i in range(4):
-                mm(r("pa", 16 * g_, 16 * g_ + 16), r("EQ", 512 * g_ + 128 * i, 512 * g_ + 128 * i + 128), r("ON", 0, 16), i == 0, i == 3)
+                mm(r("pb", 0, 64), r("EQ", 256 * k + 128 * i, 256 * k + 128 * i + 128), r("GM8", 0, 64), k + i == 0, k + i == 16)
+            if k == 7:
+                for i in range(2):
+                    mm(r("tb0", 128 * i, 128 * i + 128), r("KEEP", 0, 128), r("G3", 128 * i, 128 * i + 128), True, False)
+                    mm(r("tb0", 128 * i, 128 * i + 128), r("ISN", 0, 128), r("G3", 128 - 128 * i, 256 - 128 * i), False, True)
+                act(r("G4", 0, 256), r("tb0", 0, 256))
+                mm(r("lb1", 160, 176), IDn, r("OW1", 0, 16), True, False)
         for i in range(2):
-            ts(r("Y", 128 * i, 128 * i + 128), r("OW", 128 * i, 128 * i + 128), r("KD", i, i + 1), A.add)
-        tt(r("Y", 0, 256), r("Y", 0, 256), r("RMX", 0, 256), A.mult)
-        ts(r("OK", 0, 128), r("pa", 0, 128), 2.5, A.is_le)
-        for i in range(2):
-            tt(r("YK", 128 * i, 128 * i + 128), r("Y", 128 * i, 128 * i + 128), r("OK", 0, 128), A.mult)
-            mm(r("pb", 8 * i, 8 * i + 8), r("YK", 128 * i, 128 * i + 128), r("GM", 0, 8), True, True)
-        tt(r("LPf", 0, 16), r("pb", 0, 16), r("DL", 0, 16), A.add)
+            tt(r3("OKX", 0, 8, 1, 8 * i, 8 * i + 8), r("pb", 0, 64), r3("RMX", 0, 8, 1, 8 * i, 8 * i + 8), A.mult)
+        mm(r("lb1", 160, 176), r3("OKX", 0, 8), r("GK", 0, 16), False, True)
+        cp(r("LB", 0, 128), r("cb1", 0, 128))
+        tt(r("LPf", 0, 16), r("lb1", 160, 176), r("DL", 0, 16), A.min)
+        cp(r("LD", 0, 128), r("cb0", 128, 256))
         cp(r("LP", 0, 16), r("LPf", 0, 16))
-        look("v", r("G3", 0, 256), TBw, r("LP", 0, 16))
-        ts(r("G4", 0, 256), r("G3", 0, 256), r("PIf", 5, 6), A.mult)
-        ts(r("G5", 0, 128), r("G3", 128, 256), isn, A.mult)
-        ts(r("G5", 128, 256), r("G3", 0, 128), isn, A.mult)
-        tt(r("G4", 0, 256), r("G4", 0, 256), r("G5", 0, 256), A.add)
-        op("v", lambda: V.tensor_copy(ap(TBw).indirect(T.LP[:, 0:16]), T.G4[:, :]), [r("G4", 0, 256), r("LP", 0, 16)], [TBw])
+        TAw = r("TA", 0, DUMP + 256)
+        op("v", lambda: V.tensor_copy(ap(TAw).indirect(T.LP[:, 0:16]), T.G4[:, :]), [r("G4", 0, 256), r("LP", 0, 16)], [TAw])
         if fast:
-            for i, d in ((0, "NL"), (1, "NH")):
-                mv("ys"[i], "yl", r(d, 0, 768), trow(i, 0, 3 * W))
+            for i, d in ((0, "N1"), (1, "N2")):
+                mv("y", "yl", r(d, 0, 768), trow("TA", i, 0, 3 * W))
+            for c in (2, 3):
+                pull(t, c)
         else:
             rebuild("rb%d" % t)
-        for c in (2, 3) if fast else range(4):
-            pull(t, c)
 
-    def pull(t, c):
-        xb = r("xb%d" % t, 0, W)
+    def pull(t, c, part=None):
         d, wv = r("D%d" % (c % 2), 0, 512), r("w", 512 * c, 512 * c + 512)
-        off, cl = r("LK", 32 * c, 32 * c + 32), r("DD%d" % c, 0, 512)
-        op("v", lambda: V.tensor_tensor(ap(d), ap(xb).indirect(ap(off)), ap(wv), A.subtract), [xb, off, wv], [d])
-        if t == ROUNDS - 1 and c > 1:
-            cl = r("tb%d" % (c % 2), 0, 512)
+        cl = r("DD%d" % c, 0, 512)
+        if part != 1:
+            lookt(d, r("xb%d" % t, 0, W), r("LK", 32 * c, 32 * c + 32), wv, A.subtract)
+        if part != 0:
             ts(cl, d, -8.0, A.max, 8.0, A.min)
-            tt(wv, wv, cl, A.add)
-        else:
-            ts(cl, d, -8.0, A.max, 8.0, A.min)
-            add("wa%d%d" % (t, c // 2), wv, cl)
+            if t == ROUNDS - 1:
+                add("wa20", r("yw", 512 * c, 512 * c + 512), cl)
+            else:
+                add("wa%d%d" % (t, c // 2), wv, cl)
 
-    refresh()
     for t in range(ROUNDS):
-        finds()
+        if t == 0:
+            send(0)
+            later()
+        refresh("TA" if t else "TB", t)
+        if t:
+            send(t)
+        if t == ROUNDS - 1:
+            mv("y", "out0", r("yw", 0, K), r("w", 0, K))
+        finds(t)
         boundary(t)
-        if t < ROUNDS - 1:
-            refresh()
-    for i in range(2):
-        dma("y", "out%d" % i, T.yw[:, 1024 * i:1024 * i + 1024], T.w[:, 1024 * i:1024 * i + 1024], None, r("w", 1024 * i, 1024 * i + 1024))
-    for c0, c1, b in ((0, 512, "cb0"), (512, 768, "cb1")):
-        act(r(b, 0, c1 - c0), r("NH", c0, c1), AF.Copy, 0.0, 64.0)
-        tt(r("YF", c0, c1), r("NL", c0, c1), r(b, 0, c1 - c0), A.add)
-    dma("y", "out3", T.yn[:, :], T.YF[:, :], None, r("YF", 0, 768))
-    a_, b_, d_ = (r("PR", 128 * i, 128 * i + 128) for i in range(3))
+    mark("out")
+    tt(r("YF", 0, 768), r("N1", 0, 768), r("N2", 0, 768), A.add)
+    dma("y", "out1", T.yn[:, :], T.YF[:, :], None, r("YF", 0, 768))
+    a_, lo, hi = (r("PR", 128 * i, 128 * i + 128) for i in range(3))
+    b_, d_, m_ = r("cb1", 0, 128), r("cb0", 128, 256), r("cb1", 128, 256)
     y0, y1, y2 = (r("CF", 128 * i, 128 * i + 128) for i in range(3))
-    for k, L in ((a_, "LA"), (b_, "LB"), (d_, "LD")):
-        cp(k, r(L, 0, 128))
-    lo, hi, sm = (r("EQ3", 128 * i, 128 * i + 128) for i in range(3))
+    cp(a_, r("LA", 0, 128))
     tt(lo, a_, b_, A.min)
     tt(hi, a_, b_, A.max)
-    tt(sm, a_, b_, A.add)
     tt(y0, lo, d_, A.min)
+    tt(m_, hi, d_, A.min)
     tt(hi, hi, d_, A.max)
-    tt(sm, sm, d_, A.add)
-    tt(sm, sm, y0, A.subtract)
+    tt(lo, lo, m_, A.max)
     ts(y2, hi, -2.0 * W, A.add)
-    tt(sm, sm, hi, A.subtract)
-    ts(y1, sm, -1.0 * W, A.add)
+    ts(y1, lo, -1.0 * W, A.add)
     dma("y", "out2", T.yc[:, :], T.CF[:, :], None, r("CF", 0, 384))
     for sem in SEMAPHORES:
         if sem == "xs":
-            g.wait_ge(T.sem.xs, nloc)
+            g.wait_ge(T.sem.xs, nloc[0])
         elif count.get(sem, 0):
             known["g"].pop(sem, None)
             wait("g", (sem, count[sem]))

@@ -5,15 +5,16 @@ DUMP = 3 * W
 B, FL, IN, U16, SB = "bfloat16", "float32", "int32", "uint16", "sbuf"
 rNA, rNB, rND, rV, rJB, rJD, rFR, rU0, rU1, rONE, rTWO = 0, 2, 4, 6, 8, 9, 10, 12, 13, 14, 15
 BIG1, BIG2 = 2 ** 15, 2 ** 25
+LATE = 12
 
 SCRATCH = {}
 for _dt, _names in (
     (B, "X:12288 TB:12288 TA:12544 xb0:4096 xb1:4096 xb2:4096 TG:2048 C2:2048 D2:2048 CM0:1024 CM1:1024 CP:1024 EQ:4096 "
-        "N1:768 N2:768 MJ:768 FB:512 VL:768 VH:768 ZR:256 HM0:128 HM1:128 WW:160 XW2:16 GM8:64 GK:16 ONb:128 TWO:128 IDb:128 BDb:128 BD2:128 "
-        "M1:128 M2:128 ISN:128 KEEP:128 RC:128 CUM:136 CB:128 NE0:64 NE1:64 G3:256 G4:256"),
-    (FL, "w:2048 D0:512 D1:512 DD0:512 DD1:512 DD2:512 DD3:512 E5:640 PR:1152 CF:384 y0:128 y1:128 p0:64 p1:64 ONf:256 IDn:128 BDf:128 "
-         "IO2:128 RS:256 RW:136 MW:136 CW:136 EE:128 PM:256 MK:256 OWS:256 OW1:16 DL:16 LPf:16 HV:4 YF:768"),
-    (IN, "NX:768 ME:256 MI:768 FR:256 CU:384 TY:128 CD0:128 CD1:128 HI:4 DI:16"),
+        "N1:768 N2:768 MJ:768 FB:512 LO:256 HM0:128 HM1:128 WW:192 C17:128 NBI:128 XW2:16 GM8:64 GK:16 ONb:128 TWO:128 IDb:128 BDb:128 "
+        "BD2:128 M1:128 M2:128 ISN:128 KEEP:128 SUM:128 RC:128 CUM:136 CB:128 NE0:64 NE1:64 G3:256 G4:256"),
+    (FL, "w:2048 YW:12544 D0:512 D1:512 DD:2048 PR:384 CF:384 y0:192 y1:192 FC:8 CJ:16 ONf:256 IDn:128 BDf:128 "
+         "IO2:128 RS:256 RW:136 MW:136 CW:136 EE:128 PM:256 MK:256 OWS:256 G5:256 OW1:16 DL:16 LPf:16"),
+    (IN, "NX:768 ME:256 FR:256 CU:384 TY:128 CD0:128 CD1:128 HI:4 DI:16"),
     (U16, "LA:128 LB:128 LD:128 LK:128 LQ:8 LG:16 LP:16 PU:256"),
 ):
     for _n in _names.split():
@@ -27,7 +28,7 @@ SCRATCH["ST0"] = (SB, [128, 3, 64], IN)
 SCRATCH["ST1"] = (SB, [128, 3, 64], IN)
 for _n in "tb0 tb1 cb0 cb1 lb0 lb1 pa pb".split():
     SCRATCH[_n] = ("psum", [128, 512], FL)
-GROUPS = "ldx ldw ldn ldm ldf ldc r1 r2 r3 r4 r5 r6 r7 cpa fra wa00 wa01 wa10 wa11 wa20 rb0 rb1 out0 out1 out2 yl".split()
+GROUPS = "ldx ldw ldn ldm ldf ldc r1 r2 r3 r5 cpa fra wa00 wa01 wa10 wa11 wa20 rb0 rb1 out0 out1 out2 yl yw1".split()
 SEMAPHORES = ["qv", "qs", "qt", "qg", "xs", "x0", "x1", "x2"] + GROUPS
 
 
@@ -175,7 +176,8 @@ def rank_program(g, core, T, topo):
         op("t", lambda: P.matmul(ap(o), ap(l), ap(h), start, stop), [l, h], [o])
 
     def act(o, a, f=AF.Copy, bias=0.0, scale=1.0):
-        op("s", lambda: S.activation(ap(o), ap(a), f, bias, scale), [a], [o])
+        x = ap(scale) if isinstance(scale, tuple) else scale
+        op("s", lambda: S.activation(ap(o), ap(a), f, bias, x), [a] + ([scale] if isinstance(scale, tuple) else []), [o])
 
     def look(q, o, win, off):
         if q == "v":
@@ -207,8 +209,8 @@ def rank_program(g, core, T, topo):
     dma("y", "ldm", T.ME[:, :], T.mem[:, :], r("ME", 0, 256))
     dma("y", "ldc", T.CU[:, :], T.cur[:, :], r("CU", 0, 384))
     dma("y", "ldc", T.TY[:, :], T.typ[:, :], r("TY", 0, 128))
-    dma("y", "ldf", T.FR[:, :], T.fro[:, :], r("FR", 0, 256))
     dma("y", "ldx", T.X[:, 0:W], T.x[:, :], r("X", 0, W))
+    dma("y", "ldw", T.D2[:, 0:K], T.w0[:, :], r("D2", 0, K))
 
     nloc = [0]
     for t in range(ROUNDS):
@@ -227,22 +229,21 @@ def rank_program(g, core, T, topo):
     one = lambda a, f=1: ((a, f), (a + 1, f))
     rec = lambda f=1: ((rV, f), (rV + 1, 256 * f))
     typ0 = ((rU0, 2 * W), (rU1, W), (rONE, -W))
-    step = ((rU0, -3 * W), (rU1, -3 * W))
     typ1 = ((rU0, -W), (rU1, -2 * W), (rONE, 3 * W))
     typ2 = ((rU0, -W), (rU1, W), (rONE, W))
     packA = rec(W) + one(rNA)
     packD = rec(W) + one(rND) + ((rJD, -BIG2),)
     keepD = ((rONE, -BIG2), (rJD, BIG2))
-    own = ((rJB, BIG1), (rONE, 4 * W - BIG1))
-    new = ((rJB, -BIG1), (rONE, 4 * W))
+    own = typ1[:2] + ((rJB, BIG1), (rONE, 3 * W - BIG1))
+    new = typ1 + ((rJB, -BIG1),)
     WR = (packA, one(rNA) + typ0)
-    WF = (one(rNA, -1) + step + own, keepD, one(rNA, -1) + one(rNB) + step + new, packD, packA, one(rNA) + typ0)
-    WL = (rec(-1) + step + own, keepD, step + new, packD, packA, rec() + typ0)
+    WF = (own, (), one(rNB) + new, keepD, one(rNA) + typ0, packD, packA)
+    WL = (own, (), rec() + new, keepD, rec() + typ0, packD, packA)
     WB = (rec(), ((rONE, 1), (rJB, -1)), typ1, typ2, one(rFR), rec() + typ1 + ((rTWO, 1),))
-    WPOS = {"R": 0, "F": 2, "L": 8, "B": 14}
+    WPOS = {"R": 0, "F": 2, "L": 10, "B": 18}
 
     def weights(*sets):
-        todo = [(WPOS[n] + i, list(terms)) for n, ws in sets for i, terms in enumerate(ws)]
+        todo = [(WPOS[n] + i, list(terms)) for n, ws in sets for i, terms in enumerate(ws) if terms]
         while todo:
             for a, terms in todo:
                 rw, wt = terms.pop()
@@ -254,9 +255,10 @@ def rank_program(g, core, T, topo):
         return r("WW", 8 * (WPOS[name] + a0), 8 * (WPOS[name] + a0 + n))
 
     ONb, IDn, IDb, BDb, BDf = (r(n, 0, 128) for n in ("ONb", "IDn", "IDb", "BDb", "BDf"))
-    iota(r("WW", 0, 160), [[0, 160]], 0, 0)
-    iota(r("HI", 0, 3), [[1, 3]], 0, 3)
-    iota(r("VL", 0, 768), [[0, 3], [1, 256]], 0, 0)
+    iota(r("HI", 0, 1), [[1, 1]], 0, 1)
+    iota(r("CJ", 0, 16), [[1, 16]], 0, 0)
+    iota(r("LO", 0, 256), [[1, 256]], 0, 0)
+    iota(r("WW", 0, 192), [[0, 192]], 0, 0)
     iota(r("ONf", 0, 256), [[0, 256]], 1, 0)
     sel(IDn, r("ONf", 0, 128), [[-1, 128]], A.is_equal, 0, 0, 1)
     weights(("R", WR), ("F", WF))
@@ -264,60 +266,71 @@ def rank_program(g, core, T, topo):
     def trow(tab, rw, c0, c1):
         return r(tab, c0, c1, 1, rw, 128, 16)
 
-    def rebuild(grp):
-        for d0, d1, s0, a in ((0, 3 * W, 0, 0), (0, 2 * W, W, 1), (W, 3 * W, 0, 2), (2 * W, 3 * W, 0, 1), (0, W, 2 * W, 2)):
+    def turned(grp, tab, rw, to, a):
+        for d0, d1, s0 in ((0, (3 - a) * W, a * W), ((3 - a) * W, 3 * W, 0))[:2 if a else 1]:
+            mv("y", grp, trow("TB", to, d0, d1), trow(tab, rw, s0, s0 + d1 - d0))
+
+    def rebuild(grp, tab, turns):
+        for a in turns:
             for i in range(2):
-                mv("y", grp, trow("TB", 2 * a + i, d0, d1), trow("TA", i, s0, s0 + d1 - d0))
+                turned(grp, tab, i, 2 * a + i, a)
 
-    mset(r("TB", 0, K), 1.0)
-    for i in range(3, 6):
-        act(r("TB", K * i, K * i + K), r("TB", 0, K), AF.Sigmoid, 0.0, 400.0)
-    mset(r("TB", K, 3 * K), 1.0)
-    cp(r("N1", 0, 768), r("NX", 0, 768))
-    mset(r("ZR", 0, 256), 0.0)
-    mv("y", "r1", trow("TA", 0, 0, 3 * W), r("N1", 0, 768))
-    tt(r("N2", 0, 768), r("NX", 0, 768), r("N1", 0, 768), A.subtract)
-    mv("y", "r2", trow("TA", 1, 0, 3 * W), r("N2", 0, 768))
-    dma("y", "ldw", T.D2[:, 0:K], T.w0[:, :], r("D2", 0, K))
-    ts(r("HI", 0, 3), r("HI", 0, 3), 15, A.bitwise_and)
-    for i in range(3):
-        ts(r("MI", 256 * i, 256 * i + 256), r("ME", 0, 256), 2 ** i, A.bitwise_and)
-    cp(r("HV", 0, 3), r("HI", 0, 3))
-    ts(r("MJ", 0, 768), r("MI", 0, 768), 0.0, A.is_equal)
-    for i in range(3):
-        ts(r("VH", 256 * i, 256 * i + 256), r("ZR", 0, 256), r("HV", i, i + 1), A.add)
-    mv("y", "r3", trow("TB", rU0, 0, W), r("ZR", 0, 256))
-    mv("y", "r3", trow("TB", rU1, W, 2 * W), r("ZR", 0, 256))
-    mv("y", "r3", trow("TB", rV, 0, 3 * W), r("VL", 0, 768))
-    mv("y", "r4", trow("TB", rV + 1, 0, 3 * W), r("VH", 0, 768))
-    for s in range(3):
-        for rw, o in ((rJB, 1), (rJD, 2)):
-            mv("y", "r4", trow("TB", rw, W * s, W * s + W), r("MJ", 256 * ((s + o) % 3), 256 * ((s + o) % 3) + 256))
-    rebuild("r5")
-
+    fc = lambda i: r("FC", i, i + 1)
+    ts(r("HI", 0, 1), r("HI", 0, 1), 15, A.bitwise_and)
     mset(r3("ZF", 0, 33), 0.0)
+    for i, (rw, f) in enumerate(((rV, A.is_equal), (rV + 1, A.is_equal), (rV, A.not_equal), (rU0, A.not_equal), (rU1, A.not_equal))):
+        ts(fc(i), r("HI", 0, 1), float(rw), f)
+    mset(r("C17", 0, 64), 0.0)
+    mset(r("C17", 64, 128), 17.0 / 128)
+    tt(fc(2), fc(2), fc(1), A.subtract)
+    mset(r("CUM", 0, 8), 0.0)
+    ts(r("CJ", 0, 16), r("CJ", 0, 16), fc(1), A.mult, fc(2), A.add)
+    for j in range(16):
+        ts(r("TB", 2 * W + 256 * j, 2 * W + 256 * j + 256), r("LO", 0, 256), fc(0), A.mult, r("CJ", j, j + 1), A.add)
+        if j == 7:
+            act(r("TB", W, W + K), r("TB", 2 * W, 2 * W + K), AF.Copy, 0.0, fc(4))
+    act(r("TB", W + K, 2 * W), r("TB", 2 * W + K, 3 * W), AF.Copy, 0.0, fc(4))
+    act(r("TB", 3072, W), r("TB", 2 * W + 3072, 3 * W), AF.Copy, 0.0, fc(3))
+    cp(r("N1", 0, 768), r("NX", 0, 768))
+    ts(r("MJ", 512, 768), r("ME", 0, 256), 4.0, A.is_lt)
+    tt(r("N2", 0, 768), r("NX", 0, 768), r("N1", 0, 768), A.subtract)
+    ts(r("TB", 0, 3072), r("TB", 2 * W, 2 * W + 3072), fc(3), A.mult)
+    for i in range(2):
+        mv("y", "r1", trow("TB", i, 0, 3 * W), r(("N1", "N2")[i], 0, 768))
+    for i in range(2):
+        ts(r("NX", 256 * i, 256 * i + 256), r("ME", 0, 256), 2 ** i, A.bitwise_and)
+    ts(r("MJ", 0, 512), r("NX", 0, 512), 0.0, A.is_equal)
+    for s in range(3):
+        mv("y", "r2", trow("TB", rJB, W * s, W * s + W), r("MJ", 256 * ((s + 1) % 3), 256 * ((s + 1) % 3) + 256))
+    dma("y", "ldf", T.FR[:, :], T.fro[:, :], r("FR", 0, 256))
+    rebuild("r5", "TB", (1, 2))
+    turned("r5", "TB", rJB, rJD, 1)
+
     for i in range(3):
         ts(r("tb0", 128 * i, 128 * i + 128), r("CU", 128 * i, 128 * i + 128), float(W * i), A.add)
     for i in range(5):
-        ts(r("E5", 128 * i, 128 * i + 128), r("TY", 0, 128), float((i + 1) % 3), A.is_equal)
+        ts(r("DD", 128 * i, 128 * i + 128), r("TY", 0, 128), float((i + 1) % 3), A.is_equal)
     for n in range(3):
-        tt(r("PR", 384 * n, 384 * n + 384), r("tb0", 0, 384), r("E5", 128 * (2 - n), 128 * (5 - n)), A.mult)
+        c0 = 640 + 384 * n
+        tt(r("DD", c0, c0 + 384), r("tb0", 0, 384), r("DD", 128 * (2 - n), 128 * (5 - n)), A.mult)
         for i in range(3):
-            mm(r(("lb0", "lb1", "pa")[n], 0, 128), IDn, r("PR", 384 * n + 128 * i, 384 * n + 128 * i + 128), i == 0, i == 2)
-    mset(ONb, 1.0)
+            mm(r(("lb0", "lb1", "pa")[n], 0, 128), IDn, r("DD", c0 + 128 * i, c0 + 128 * i + 128), i == 0, i == 2)
+    act(ONb, r("ONf", 0, 128), AF.Sigmoid, 0.0, 400.0)
+    cp(r("X", W, 2 * W), r("X", 0, W))
     for n, L in enumerate(("LA", "LB", "LD")):
         cp(r(L, 0, 128), r(("lb0", "lb1", "pa")[n], 0, 128))
-    cp(r("X", W, 2 * W), r("X", 0, W))
     act(r("w", 0, K), r("D2", 0, K))
-    act(r("X", 2 * W, 3 * W), r("X", 0, W))
+    act(r("X", 2 * W, 2 * W + 3072), r("X", 0, 3072))
+    cp(r("X", 2 * W + 3072, 3 * W), r("X", 3072, W))
     cp(r("FB", 0, 256), r("FR", 0, 256))
     iota(r("DI", 0, 16), [[1, 16]], 0, 16)
-    band(r("XW2", 0, 16), r("ONb", 0, 16), [[0, 2], [-16, 8]])()
-    tt(r("FB", 256, 512), r("FR", 0, 256), r("FB", 0, 256), A.subtract)
+    iota(r("XW2", 0, 16), [[-2, 2], [0, 8]], 1, 0)
+    iota(r("NBI", 0, 128), [[0, 128]], 0, 0)
+    band(r("XW2", 0, 16), r("XW2", 0, 16), [[0, 2], [-16, 8]])()
+    sel(r("NBI", 0, 128), r("NBI", 0, 128), [[-1, 128]], A.not_equal, -BIG2, 0, 1)
     ts(r("DI", 0, 16), r("DI", 0, 16), 255, A.bitwise_and)
-    mset(r("CUM", 0, 8), 0.0)
+    tt(r("FB", 256, 512), r("FR", 0, 256), r("FB", 0, 256), A.subtract)
     ts(r("DL", 0, 16), r("DI", 0, 16), float(DUMP), A.add)
-
     weights(("L", WL), ("B", WB))
 
     def later():
@@ -343,6 +356,7 @@ def rank_program(g, core, T, topo):
         sel(r("RS", 0, 256), r("ONf", 0, 256), [[0, 16], [1, 16]], A.is_gt, 0, 0, 0)
         sel(r("ISN", 0, 128), IDb, [[0, 8], [-1, 16]], A.is_ge, 0, 1, 0)
         sel(r("KEEP", 0, 128), IDb, [[0, 8], [1, 16]], A.is_ge, 0, -2, 0)
+        sel(r("SUM", 0, 128), BDb, [[16, 8], [0, 16]], A.is_ge, 0, 1, -1)
         sel(r("M1", 0, 128), r("BD2", 0, 128), [[1, 128]], A.is_gt, 0, 0, -1)
         sel(r("M2", 0, 128), r("BD2", 0, 128), [[-1, 128]], A.is_gt, 0, 0, 1)
         for n in ("M1", "M2"):
@@ -350,10 +364,10 @@ def rank_program(g, core, T, topo):
         for k in range(8):
             sel(r3("RMX", 0, 16), r3("RMX", 0, 16), [[0, 16], [-1, 16]], A.not_equal, 1, -16 * k, 1)
 
-    def units(ps, src, c0, wk):
+    def units(ps, src, c0, wk, start=True, stop=True):
         n = wk[2] - wk[1]
         for b in range(8):
-            mm(r(ps, b, 8 * n, 8), r(src, c0 + b, c0 + 1024, 8), wk, True, True)
+            mm(r(ps, b, 8 * n, 8), r(src, c0 + b, c0 + 1024, 8), wk, start and b == 0, stop and b == 7)
 
     def zin(z, n=1):
         i = 16 * ZNAMES.index(z)
@@ -370,23 +384,36 @@ def rank_program(g, core, T, topo):
     def ask(q, buf, tab, L, h, c0=0, c1=64):
         look(q, r(buf, 1024 * h + 16 * c0, 1024 * h + 16 * c1), r(tab, 0, DUMP), r(L, 64 * h + c0, 64 * h + c1))
 
-    def match(h):
-        lookt(r("CM%d" % h, 0, 1024), r("X", 0, 3 * W), r("LA", 64 * h, 64 * h + 64), r("w", 1024 * h, 1024 * h + 1024), A.is_ge)
+    def match(h, c0=0, c1=64):
+        lookt(r("CM%d" % h, 16 * c0, 16 * c1), r("X", 0, 3 * W), r("LA", 64 * h + c0, 64 * h + c1),
+              r("w", 1024 * h + 16 * c0, 1024 * h + 16 * c1), A.is_ge)
 
     def hit(h):
-        units("cb%d" % h, "CM%d" % h, 0, r("XW2", 0, 16))
-        act(r("HM%d" % h, 0, 128), r("cb%d" % h, 0, 128), AF.Sigmoid, -3400.0, 400.0)
+        cb = "cb%d" % h
+        mm(r(cb, 0, 128), ONb, r("C17", 0, 128), True, False)
+        units(cb, "CM%d" % h, 0, r("XW2", 0, 16), False, True)
+        act(r("HM%d" % h, 0, 128), r(cb, 0, 128), AF.Sigmoid, -3400.0, 400.0)
+
+    def answers(h, last):
+        tb, hm = "tb%d" % h, "HM%d" % h
+        units(tb, "TG", 1024 * h, wts("L" if last else "F", 0, 7), True, False)
+        for a0, a1, c0 in ((0, 1, 64), (1, 3, 0), (3, 4, 64), (4, 6, 0), (6, 7, 64)):
+            mm(r(tb, 64 * a0, 64 * a1), r("NBI", 0, 128), r(hm, c0, c0 + 64 * (a1 - a0)), False, a1 == 7)
+
+    def enlist(h):
+        cp(r("LA", 64 * h, 64 * h + 64), r("lb%d" % h, 0, 64))
 
     def first(h):
         units("tb%d" % h, "TG", 1024 * h, wts("R", 1, 1))
-        cp(zin("A%d" % h), r("tb%d" % h, 0, 64))
-        turn("A%d" % h, "lb%d" % h, 0)
-        return lambda: cp(r("LA", 64 * h, 64 * h + 64), r("lb%d" % h, 0, 64))
 
-    def state(h, i):
-        ps = ("pa", "pb")[h]
+        def then():
+            cp(zin("A%d" % h), r("tb%d" % h, 0, 64))
+            turn("A%d" % h, "lb%d" % h, 0)
+        return then
+
+    def state(h, i, ps):
         units(ps, ("C2", "D2")[i - 1], 1024 * h, wts("R", 0, 1))
-        cp(r3("ST%d" % h, i, i + 1), r(ps, 0, 64))
+        return lambda: cp(r3("ST%d" % h, i, i + 1), r(ps, 0, 64))
 
     def nextof(h, last):
         st = "ST%d" % h
@@ -400,64 +427,86 @@ def rank_program(g, core, T, topo):
         ask("s", "TG", tab, "LA", 0)
         if t:
             ask("s", "TG", tab, "LA", 1)
-            for c in (2, 3):
-                pull(t - 1, c)
+            pull(t - 1, 2)
+            pull(t - 1, 3, 0)
+            first(0)()
+            plus = pull(t - 1, 3, 1)
+            ask("s", "D2", tab, "LD", 0)
+            ask("s", "C2", tab, "LB", 1)
+            enlist(0)
+            plus()
+            match(0)
+            first(1)()
+            ask("v", "C2", tab, "LB", 0)
+            enlist(1)
+            hit(0)
+            ask("s", "TG", "TB", "LA", 0)
+            ask("v", "D2", tab, "LD", 1)
         else:
             ask("v", "TG", tab, "LA", 1)
-        f0 = first(0)
-        ask("s", "D2", tab, "LD", 0)
+            ask("s", "D2", tab, "LD", 0)
+            ask("v", "C2", tab, "LB", 0)
+            for f in [first(0), first(1)]:
+                f()
+            ask("s", "C2", tab, "LB", 1)
+            ask("v", "D2", tab, "LD", 1)
+            enlist(0)
+            enlist(1)
+            ask("s", "TG", "TB", "LA", 0)
+            match(0)
+        fin = [state(0, 2, "pa"), state(0, 1, "lb0"), state(1, 1, "pb")]
         if not t:
-            ask("v", "C2", tab, "LB", 0)
-        f0()
-        f1 = first(1)
-        ask("s", "TG", "TB", "LA", 0)
-        match(0)
-        f1()
-        state(0, 2)
-        if t:
-            ask("v", "C2", tab, "LB", 0)
-        hit(0)
-        units("tb0", "TG", 0, wts("F", 0, 6))
+            hit(0)
         ask("s", "TG", "TB", "LA", 1)
-        ask("v", "D2", tab, "LD", 1)
-        ask("s", "C2", tab, "LB", 1)
-        state(0, 1)
-        match(1)
+        fin.append(state(1, 2, "lb1"))
+        for f in fin[:3]:
+            f()
+        answers(0, False)
         nextof(0, False)
+        nextof(1, False)
+        fin[3]()
+        match(1)
 
     def settle(h):
-        dl, st = r(("pa", "pb")[h], 0, 128), r3("ST%d" % h, 1, 3)
-        return (lambda: tt(dl, dl, r("HM%d" % h, 0, 128), A.mult)), (lambda: tt(st, st, dl, A.add))
+        tt(r3("ST%d" % h, 1, 3), r("y%d" % h, 64, 192), r("tb%d" % h, 320, 448), A.max)
 
     def finds(t):
         mark("find%d" % t)
+        aside = numbers() if t == ROUNDS - 1 else iter(())
         for n in range(2 * FINDS):
             h, o, q = n % 2, 1 - n % 2, n // 2
-            tb, st, y, p = "tb%d" % h, "ST%d" % h, r("y%d" % h, 0, 128), r("p%d" % h, 0, 64)
-            mult, plus = settle(o)
-            tt(y, r3(st, 0, 3, 2), r(tb, 0, 128), A.add)
-            if n:
-                mult()
-            hit(o) if n + 1 < 2 * FINDS else None
-            tt(r(tb, 128, 256), y, r(tb, 128, 256), A.max)
-            if n:
-                plus()
-            else:
-                state(1, 1)
-            tt(p, r(tb, 128, 192), r("HM%d" % h, 0, 64), A.mult)
-            if n == 0:
-                state(1, 2)
-            if n + 1 < 2 * FINDS:
-                nextof(o, (n + 1) // 2 == FINDS - 1)
-            tt(zin("A%d" % h), p, r(tb, 320, 384), A.add)
+            tb, st, y = "tb%d" % h, "ST%d" % h, "y%d" % h
+            more, late, last = n + 1 < 2 * FINDS, 0 < n < 2 * FINDS - 2, (n + 1) // 2 == FINDS - 1
+            kept = lambda: tt(r(y, 64, 128), r(y, 64, 128), r(tb, 192, 256), A.max)
+            if more and not late:
+                hit(o)
+            tt(r(y, 0, 64), r3(st, 0, 1), r(tb, 0, 64), A.add)
+            tt(r(y, 64, 128), r3(st, 1, 2), r(tb, 64, 128), A.add)
+            tt(r(y, 0, 64), r(y, 0, 64), r(tb, 128, 192), A.max)
+            tt(r(tb, 192, 256), r3(st, 2, 3), r(tb, 192, 256), A.add)
+            tt(zin("A%d" % h), r(y, 0, 64), r(tb, 256, 320), A.max)
             turn("A%d" % h, "lb%d" % h, 0)
-            tt(r(("pa", "pb")[h], 0, 128), r(tb, 192, 320), r3(st, 1, 3), A.subtract)
-            if n + 1 < 2 * FINDS:
-                units("tb%d" % o, "TG", 1024 * o, wts("L" if (n + 1) // 2 == FINDS - 1 else "F", 0, 6))
-            cp(r("LA", 64 * h, 64 * h + 64), r("lb%d" % h, 0, 64))
+            tt(r(y, 128, 192), r3(st, 2, 3), r(tb, 64, 128), A.add)
+            if n:
+                settle(o)
+            if late:
+                match(o, 64 - LATE, 64)
+                hit(o)
+                enlist(h)
+                kept()
+                nextof(o, last)
+            else:
+                kept()
+                if n and more:
+                    nextof(o, last)
+                enlist(h)
+            if more:
+                answers(o, last)
             if q < FINDS - 1:
                 ask("s", "TG", "TB", "LA", h)
-                match(h)
+                if n > 3:
+                    next(aside, lambda: None)()
+                match(h, 0, 64 - LATE if n < 2 * FINDS - 3 else 64)
             elif h == 0:
                 ask("s", "TG", "TA", "LA", 0)
 
@@ -472,27 +521,24 @@ def rank_program(g, core, T, topo):
     def boundary(t):
         mark("bnd%d" % t)
         fast = t == ROUNDS - 1
-        mult, plus = settle(1)
         cursors = lambda h: ts(r("CD%d" % h, 0, 128), r3("ST%d" % h, 1, 3), 12, A.logical_shift_right)
-        ask("s", "TG", "TA", "LA", 1, 48, 64)
-        ask("v", "TG", "TA", "LA", 1, 0, 48)
+        ask("s", "TG", "TA", "LA", 1, 36, 64)
+        ask("v", "TG", "TA", "LA", 1, 0, 36)
         units("tb0", "TG", 0, wts("B", 0, 6))
+        settle(1)
         units("tb1", "TG", 1024, wts("B", 0, 6))
-        mult()
         cursors(0)
-        plus()
-        wants(0)
         cursors(1)
-        turn("K0", "cb0", 0)
-        scan(r("CUM", 1, 65), r("ONb", 0, 64), r("lb1", 0, 64), 0.0)
+        wants(0)
         wants(1)
-        cp(r("LK", 0, 64), r("cb0", 0, 64))
-        scan(r("CUM", 65, 129), r("ONb", 0, 64), r("lb1", 64, 128), r("CUM", 64, 65))
+        turn("K0", "cb0", 0)
+        scan(r("CUM", 1, 129), ONb, r("lb1", 0, 128), 0.0)
         mm(r("pa", 0, 128), r("CUM", 1, 129), BDb, True, True)
         mm(r("pb", 0, 128), r("M1", 0, 128), r("CUM", 1, 129), True, False)
         mm(r("pb", 0, 128), r("M2", 0, 128), r("CUM", 0, 128), False, True)
         act(r("RW", 0, 128), r("pb", 0, 128))
         turn("M0", "lb0", 0)
+        cp(r("LK", 0, 64), r("cb0", 0, 64))
         pull(t, 0, 0)
         tt(r("CB", 0, 128), r("pa", 0, 128), r("RC", 0, 128), A.subtract)
         turn("M1", "lb0", 64)
@@ -520,6 +566,9 @@ def rank_program(g, core, T, topo):
         cp(r("PU", 0, 256), r("pa", 0, 256))
         scan(r("OWS", 0, 256), r("RS", 0, 256), r("MK", 0, 256), 0.0)
         pull(t, 1, 1)
+        if fast:
+            pull(t, 2)
+            pull(t, 3)
         ow = r("OWS", 15, 256, 16)
         ts(r("LG", 0, 16), ow, -1.0, A.add)
         look("s", r("G3", 0, 256), r("TA", 0, DUMP), r("LG", 0, 16))
@@ -531,9 +580,10 @@ def rank_program(g, core, T, topo):
                 mm(r("pb", 0, 64), r("EQ", 256 * k + 128 * i, 256 * k + 128 * i + 128), r("GM8", 0, 64), k + i == 0, k + i == 16)
             if k == 7:
                 for i in range(2):
-                    mm(r("tb0", 128 * i, 128 * i + 128), r("KEEP", 0, 128), r("G3", 128 * i, 128 * i + 128), True, False)
-                    mm(r("tb0", 128 * i, 128 * i + 128), r("ISN", 0, 128), r("G3", 128 - 128 * i, 256 - 128 * i), False, True)
-                act(r("G4", 0, 256), r("tb0", 0, 256))
+                    if not fast:
+                        mm(r("tb0", 128 * i, 128 * i + 128), r("KEEP", 0, 128), r("G3", 128 * i, 128 * i + 128), True, False)
+                    mm(r("tb0", 128 * i, 128 * i + 128), r("SUM" if fast else "ISN", 0, 128), r("G3", 128 - 128 * i, 256 - 128 * i), fast, True)
+                act(r("G5" if fast else "G4", 0, 256), r("tb0", 0, 256))
                 mm(r("lb1", 160, 176), IDn, r("OW1", 0, 16), True, False)
         for i in range(2):
             tt(r3("OKX", 0, 8, 1, 8 * i, 8 * i + 8), r("pb", 0, 64), r3("RMX", 0, 8, 1, 8 * i, 8 * i + 8), A.mult)
@@ -542,21 +592,31 @@ def rank_program(g, core, T, topo):
         tt(r("LPf", 0, 16), r("lb1", 160, 176), r("DL", 0, 16), A.min)
         cp(r("LD", 0, 128), r("cb0", 128, 256))
         cp(r("LP", 0, 16), r("LPf", 0, 16))
-        TAw = r("TA", 0, DUMP + 256)
-        op("v", lambda: V.tensor_copy(ap(TAw).indirect(T.LP[:, 0:16]), T.G4[:, :]), [r("G4", 0, 256), r("LP", 0, 16)], [TAw])
+        tab, val = r("YW" if fast else "TA", 0, DUMP + 256), r("G5" if fast else "G4", 0, 256)
+        op("v", lambda: V.tensor_copy(ap(tab).indirect(T.LP[:, 0:16]), ap(val)), [val, r("LP", 0, 16)], [tab])
         if fast:
-            for i, d in ((0, "N1"), (1, "N2")):
-                mv("y", "yl", r(d, 0, 768), trow("TA", i, 0, 3 * W))
-            for c in (2, 3):
-                pull(t, c)
+            dma("y", "out1", T.yn[:, :], T.YW[0:128:16, 0:3 * W], None, trow("YW", 0, 0, 3 * W))
         else:
-            rebuild("rb%d" % t)
+            rebuild("rb%d" % t, "TA", (0, 1, 2))
+
+    def numbers():
+        for i, d in ((0, "N1"), (1, "N2")):
+            mv("y", "yl", r(d, 0, 768), trow("TA", i, 0, 3 * W))
+        for c0, c1, b in ((0, 512, "pa"), (512, 768, "pb")):
+            for i, d in enumerate(("N1", "N2")):
+                mm(r(b, 0, c1 - c0), IDb, r(d, c0, c1), i == 0, i == 1)
+        for c0 in (0, 256, 512):
+            yield lambda c0=c0: act(r("DD", c0, c0 + 256), r(("pa", "pb")[c0 // 512], c0 % 512, c0 % 512 + 256))
+        yield lambda: mv("y", "yw1", trow("YW", 0, 0, 3 * W), r("DD", 0, 768))
 
     def pull(t, c, part=None):
         d, wv = r("D%d" % (c % 2), 0, 512), r("w", 512 * c, 512 * c + 512)
-        cl = r("DD%d" % c, 0, 512)
+        cl = r("DD", 512 * c, 512 * c + 512)
         if part != 1:
             lookt(d, r("xb%d" % t, 0, W), r("LK", 32 * c, 32 * c + 32), wv, A.subtract)
+        if part != 0 and c == 3 and t < ROUNDS - 1:
+            ts(r("cb1", 0, 512), d, -8.0, A.max, 8.0, A.min)
+            return lambda: tt(wv, wv, r("cb1", 0, 512), A.add)
         if part != 0:
             ts(cl, d, -8.0, A.max, 8.0, A.min)
             if t == ROUNDS - 1:
@@ -576,8 +636,6 @@ def rank_program(g, core, T, topo):
         finds(t)
         boundary(t)
     mark("out")
-    tt(r("YF", 0, 768), r("N1", 0, 768), r("N2", 0, 768), A.add)
-    dma("y", "out1", T.yn[:, :], T.YF[:, :], None, r("YF", 0, 768))
     a_, lo, hi = (r("PR", 128 * i, 128 * i + 128) for i in range(3))
     b_, d_, m_ = r("cb1", 0, 128), r("cb0", 128, 256), r("cb1", 128, 256)
     y0, y1, y2 = (r("CF", 128 * i, 128 * i + 128) for i in range(3))

@@ -4,37 +4,56 @@ ROUNDS, FINDS, W, K = 3, 6, 4096, 2048
 DUMP = 3 * W
 B, FL, IN, U16, SB = "bfloat16", "float32", "int32", "uint16", "sbuf"
 rNA, rNB, rND, rV, rJB, rJD, rFR, rU0, rU1, rONE, rTWO = 0, 2, 4, 6, 8, 9, 10, 12, 13, 14, 15
-BIG1, BIG2 = 2 ** 15, 2 ** 25
-LATE = 12
+BIG1, BIG2, BIG3, BIG4 = 2 ** 15, 2 ** 26, 2 ** 28, 2 ** 29
+Z = 8192
+CUTS = (42, 48, 54, 64)
 
 SCRATCH = {}
 for _dt, _names in (
     (B, "X:12288 TB:12288 TA:12544 xb0:4096 xb1:4096 xb2:4096 TG:2048 C2:2048 D2:2048 CM0:1024 CM1:1024 CP:1024 EQ:4096 "
-        "N1:768 N2:768 MJ:768 FB:512 LO:256 HM0:128 HM1:128 WW:192 C17:128 NBI:128 XW2:16 GM8:64 GK:16 ONb:128 TWO:128 IDb:128 BDb:128 "
-        "BD2:128 M1:128 M2:128 ISN:128 KEEP:128 SUM:128 RC:128 CUM:136 CB:128 NE0:64 NE1:64 G3:256 G4:256"),
-    (FL, "w:2048 YW:12544 D0:512 D1:512 DD:2048 PR:384 CF:384 y0:192 y1:192 FC:8 CJ:16 ONf:256 IDn:128 BDf:128 "
+        "N1:768 N2:768 MJ:768 FB:512 LO:256 HM0:128 HM1:128 WW:208 C17:128 NBI:128 XW2:16 GM8:64 GK:16 ONb:128 TWO:128 IDb:128 ID64:128 "
+        "BDb:128 BD2:128 M1:128 M2:128 ISN:128 KEEP:128 SUM:128 RC:128 CUM:136 CB:128 NE0:64 NE1:64 G3:256 G4:256"),
+    (FL, "w:2048 YW:12544 DD:2048 D0:1024 NID:128 PR:384 CF:384 y0:192 y1:192 FC:8 CJ:16 ONf:256 IDn:128 IDs:128 BDf:128 "
          "IO2:128 RS:256 RW:136 MW:136 CW:136 EE:128 PM:256 MK:256 OWS:256 G5:256 OW1:16 DL:16 LPf:16"),
     (IN, "NX:768 ME:256 FR:256 CU:384 TY:128 CD0:128 CD1:128 HI:4 DI:16"),
     (U16, "LA:128 LB:128 LD:128 LK:128 LQ:8 LG:16 LP:16 PU:256"),
 ):
     for _n in _names.split():
         SCRATCH[_n.split(":")[0]] = (SB, [128, int(_n.split(":")[1])], _dt)
-ZNAMES = "A0 A1 B0 D0 K0 M0 B1 D1 K1 M1".split()
+ZNAMES = "A0 A1 B0 D0 B1 D1".split()
+ZSMALL = "W0 W1 K0 k0 M0 m0 K1 k1 M1 m1".split()
 SCRATCH["ZF"] = (SB, [128, 16 * len(ZNAMES) + 1, 8], FL)
-SCRATCH["ZW"] = (SB, [128, 33, 8], B)
+SCRATCH["ZW"] = (SB, [128, 16 * len(ZSMALL) + 1, 8], B)
 SCRATCH["RMX"] = (SB, [128, 16, 16], FL)
 SCRATCH["OKX"] = (SB, [128, 8, 16], B)
 SCRATCH["ST0"] = (SB, [128, 3, 64], IN)
 SCRATCH["ST1"] = (SB, [128, 3, 64], IN)
 for _n in "tb0 tb1 cb0 cb1 lb0 lb1 pa pb".split():
     SCRATCH[_n] = ("psum", [128, 512], FL)
-GROUPS = "ldx ldw ldn ldm ldf ldc r1 r2 r3 r5 cpa fra wa00 wa01 wa10 wa11 wa20 rb0 rb1 out0 out1 out2 yl yw1".split()
-SEMAPHORES = ["qv", "qs", "qt", "qg", "xs", "x0", "x1", "x2"] + GROUPS
+GROUPS = "ldx ldw ldn ldm ldf ldc r1 r2 r3 r5 cpa wa00 wa10 wa20 rb0 rb1 out0 out1 out2 yl yw1".split()
+SEMAPHORES = ["qv", "qs", "qt", "qg", "xs", "xh", "x0", "x1", "x2"] + GROUPS
 
 
 def rank_program(g, core, T, topo):
+    n_ = len(T.cores)
+
+    def takers(rk):
+        return [T.cores[(rk - 1 - t) % n_] for t in range(ROUNDS)]
+
+    def helper(rk):
+        c0 = T.cores[rk]
+        return [c for c in topo.cores_of(c0)
+                if c not in T.cores and topo.die(c) == topo.die(c0) and all(topo.may_write(c, d) for d in takers(rk))][0]
+
     rank = T.rank_of(core)
     if rank is None:
+        for rk in range(n_):
+            if core == helper(rk):
+                g.wait_ge(T.sem.xh, len(topo.engines(T.cores[rk], core)))
+                for t, dst in enumerate(takers(rk)):
+                    rid, pid, _se = topo.addr(dst)
+                    g.remote_dma(T["xb%d" % t][:, :], T.X[:, 0:W], T.sem["x%d" % t], T.sem.xs, pid, rid, topo.mask(core, dst))
+                g.wait_ge(T.sem.xs, sum(len(topo.engines(core, dst)) for dst in takers(rk)))
         return
     Q = {"v": g.vector, "s": g.scalar, "t": g.tensor, "g": g, "y": g.sync}
     V, S, P = g.vector, g.scalar, g.tensor
@@ -69,6 +88,8 @@ def rank_program(g, core, T, topo):
         if a[6] == 16 and b[6] == 16 and a[4] % 16 != b[4] % 16:
             return False
         if a[3] == b[3] and a[3] > 1 and (a[1] - b[1]) % a[3]:
+            return False
+        if a[7] and b[7] and (a[7][3] >= b[7][4] or b[7][3] >= a[7][4]):
             return False
         return True
 
@@ -168,9 +189,7 @@ def rank_program(g, core, T, topo):
         op("v", lambda: V.memset(ap(o), c), [], [o])
 
     def scan(o, keep, a, init):
-        rd = [keep, a] + ([init] if isinstance(init, tuple) else [])
-        x = ap(init) if isinstance(init, tuple) else init
-        op("v", lambda: V.tensor_tensor_scan(ap(o), ap(keep), ap(a), x, A.mult, A.add), rd, [o])
+        op("v", lambda: V.tensor_tensor_scan(ap(o), ap(keep), ap(a), init, A.mult, A.add), [keep, a], [o])
 
     def mm(o, l, h, start, stop):
         op("t", lambda: P.matmul(ap(o), ap(l), ap(h), start, stop), [l, h], [o])
@@ -209,41 +228,44 @@ def rank_program(g, core, T, topo):
     dma("y", "ldm", T.ME[:, :], T.mem[:, :], r("ME", 0, 256))
     dma("y", "ldc", T.CU[:, :], T.cur[:, :], r("CU", 0, 384))
     dma("y", "ldc", T.TY[:, :], T.typ[:, :], r("TY", 0, 128))
+    dma("y", "ldf", T.FR[:, :], T.fro[:, :], r("FR", 0, 256))
     dma("y", "ldx", T.X[:, 0:W], T.x[:, :], r("X", 0, W))
     dma("y", "ldw", T.D2[:, 0:K], T.w0[:, :], r("D2", 0, K))
 
-    nloc = [0]
     for t in range(ROUNDS):
-        src = T.cores[(rank + 1 + t) % len(T.cores)]
+        src = helper((rank + 1 + t) % n_)
         count["x%d" % t] = len(topo.engines(src, core))
         acc["xb%d" % t] = [(r("xb%d" % t, 0, W), True, ("x%d" % t, count["x%d" % t]), "dma")]
 
-    def send(t):
+    def send():
         wait("g", ("ldx", 0))
-        wait("g", ("qv", count["qv"]) if t else ("r5", 0))
-        dst = T.cores[(rank - 1 - t) % len(T.cores)]
-        rid, pid, _se = topo.addr(dst)
-        g.remote_dma(T["xb%d" % t][:, :], T.X[:, 0:W], T.sem["x%d" % t], T.sem.xs, pid, rid, topo.mask(core, dst))
-        nloc[0] += len(topo.engines(core, dst))
+        wait("g", ("r5", 0))
+        rid, pid, _se = topo.addr(helper(rank))
+        g.remote_dma(T.X[:, 0:W], T.X[:, 0:W], T.sem.xh, T.sem.xs, pid, rid, topo.mask(core, helper(rank)))
 
-    one = lambda a, f=1: ((a, f), (a + 1, f))
     rec = lambda f=1: ((rV, f), (rV + 1, 256 * f))
     typ0 = ((rU0, 2 * W), (rU1, W), (rONE, -W))
     typ1 = ((rU0, -W), (rU1, -2 * W), (rONE, 3 * W))
     typ2 = ((rU0, -W), (rU1, W), (rONE, W))
-    packA = rec(W) + one(rNA)
-    packD = rec(W) + one(rND) + ((rJD, -BIG2),)
+    num = lambda a, f=1: ((a, f), (a + 1, 64 * f), (rONE, K * f))
+    pack = lambda a: num(a, Z)[:2] + rec() + ((rONE, K),)
+    times = lambda terms, f: tuple((rw, wt * f) for rw, wt in terms)
+    packD = pack(rND) + ((rJD, -BIG2),)
     keepD = ((rONE, -BIG2), (rJD, BIG2))
-    own = typ1[:2] + ((rJB, BIG1), (rONE, 3 * W - BIG1))
-    new = typ1 + ((rJB, -BIG1),)
-    WR = (packA, one(rNA) + typ0)
-    WF = (own, (), one(rNB) + new, keepD, one(rNA) + typ0, packD, packA)
-    WL = (own, (), rec() + new, keepD, rec() + typ0, packD, packA)
-    WB = (rec(), ((rONE, 1), (rJB, -1)), typ1, typ2, one(rFR), rec() + typ1 + ((rTWO, 1),))
+    WR = (pack(rNA), num(rNA) + typ0)
+    WF = (times(typ1, Z) + ((rONE, K * Z - BIG3), (rTWO, -W), (rJB, BIG3)), keepD, (), times(num(rNB) + typ1, Z) + ((rJB, -BIG3),), (),
+          times(num(rNA) + typ0, Z), packD, pack(rNA))
+    WL = (typ1 + ((rONE, -K - BIG1), (rJB, BIG1)), keepD, (), rec() + typ1 + ((rJB, -BIG1),), (), rec() + typ0, packD, pack(rNA))
+    WB = (rec() + ((rONE, K),), ((rONE, 1), (rJB, -1)), typ1 + ((rONE, -K),), typ2 + ((rONE, -K),), ((rFR, 1),), ((rFR + 1, 1),),
+          rec()[:1] + ((rONE, 1),), rec()[1:] + typ1)
     WPOS = {"R": 0, "F": 2, "L": 10, "B": 18}
 
     def weights(*sets):
-        todo = [(WPOS[n] + i, list(terms)) for n, ws in sets for i, terms in enumerate(ws) if terms]
+        todo = []
+        for n, ws in sets:
+            for i, terms in enumerate(ws):
+                if terms:
+                    todo.append((WPOS[n] + i, [(rw, sum(wt for r_, wt in terms if r_ == rw)) for rw in sorted(set(r_ for r_, _w in terms))]))
         while todo:
             for a, terms in todo:
                 rw, wt = terms.pop()
@@ -258,7 +280,7 @@ def rank_program(g, core, T, topo):
     iota(r("HI", 0, 1), [[1, 1]], 0, 1)
     iota(r("CJ", 0, 16), [[1, 16]], 0, 0)
     iota(r("LO", 0, 256), [[1, 256]], 0, 0)
-    iota(r("WW", 0, 192), [[0, 192]], 0, 0)
+    iota(r("WW", 0, 208), [[0, 208]], 0, 0)
     iota(r("ONf", 0, 256), [[0, 256]], 1, 0)
     sel(IDn, r("ONf", 0, 128), [[-1, 128]], A.is_equal, 0, 0, 1)
     weights(("R", WR), ("F", WF))
@@ -277,23 +299,20 @@ def rank_program(g, core, T, topo):
 
     fc = lambda i: r("FC", i, i + 1)
     ts(r("HI", 0, 1), r("HI", 0, 1), 15, A.bitwise_and)
-    mset(r3("ZF", 0, 33), 0.0)
     for i, (rw, f) in enumerate(((rV, A.is_equal), (rV + 1, A.is_equal), (rV, A.not_equal), (rU0, A.not_equal), (rU1, A.not_equal))):
         ts(fc(i), r("HI", 0, 1), float(rw), f)
-    mset(r("C17", 0, 64), 0.0)
-    mset(r("C17", 64, 128), 17.0 / 128)
     tt(fc(2), fc(2), fc(1), A.subtract)
-    mset(r("CUM", 0, 8), 0.0)
     ts(r("CJ", 0, 16), r("CJ", 0, 16), fc(1), A.mult, fc(2), A.add)
     for j in range(16):
         ts(r("TB", 2 * W + 256 * j, 2 * W + 256 * j + 256), r("LO", 0, 256), fc(0), A.mult, r("CJ", j, j + 1), A.add)
-        if j == 7:
-            act(r("TB", W, W + K), r("TB", 2 * W, 2 * W + K), AF.Copy, 0.0, fc(4))
-    act(r("TB", W + K, 2 * W), r("TB", 2 * W + K, 3 * W), AF.Copy, 0.0, fc(4))
+        if j % 4 == 3:
+            act(r("TB", W + 256 * j - 768, W + 256 * j + 256), r("TB", 2 * W + 256 * j - 768, 2 * W + 256 * j + 256), AF.Copy, 0.0, fc(4))
     act(r("TB", 3072, W), r("TB", 2 * W + 3072, 3 * W), AF.Copy, 0.0, fc(3))
-    cp(r("N1", 0, 768), r("NX", 0, 768))
+    ts(r("N2", 0, 768), r("NX", 0, 768), 1.0 / 64, A.mult, 160 - 31.5 / 64, A.add)
     ts(r("MJ", 512, 768), r("ME", 0, 256), 4.0, A.is_lt)
-    tt(r("N2", 0, 768), r("NX", 0, 768), r("N1", 0, 768), A.subtract)
+    ts(r("NX", 0, 768), r("NX", 0, 768), 63, A.bitwise_and)
+    ts(r("N2", 0, 768), r("N2", 0, 768), -192.0, A.add)
+    cp(r("N1", 0, 768), r("NX", 0, 768))
     ts(r("TB", 0, 3072), r("TB", 2 * W, 2 * W + 3072), fc(3), A.mult)
     for i in range(2):
         mv("y", "r1", trow("TB", i, 0, 3 * W), r(("N1", "N2")[i], 0, 768))
@@ -302,9 +321,13 @@ def rank_program(g, core, T, topo):
     ts(r("MJ", 0, 512), r("NX", 0, 512), 0.0, A.is_equal)
     for s in range(3):
         mv("y", "r2", trow("TB", rJB, W * s, W * s + W), r("MJ", 256 * ((s + 1) % 3), 256 * ((s + 1) % 3) + 256))
-    dma("y", "ldf", T.FR[:, :], T.fro[:, :], r("FR", 0, 256))
     rebuild("r5", "TB", (1, 2))
     turned("r5", "TB", rJB, rJD, 1)
+    mv("y", "r3", r("X", 2 * W, 3 * W), r("X", 0, W))
+    mset(r3("ZF", 0, 33), 0.0)
+    mset(r("C17", 0, 64), 0.0)
+    mset(r("C17", 64, 128), 17.0 / 128)
+    mset(r("CUM", 0, 8), 0.0)
 
     for i in range(3):
         ts(r("tb0", 128 * i, 128 * i + 128), r("CU", 128 * i, 128 * i + 128), float(W * i), A.add)
@@ -316,30 +339,34 @@ def rank_program(g, core, T, topo):
         for i in range(3):
             mm(r(("lb0", "lb1", "pa")[n], 0, 128), IDn, r("DD", c0 + 128 * i, c0 + 128 * i + 128), i == 0, i == 2)
     act(ONb, r("ONf", 0, 128), AF.Sigmoid, 0.0, 400.0)
-    cp(r("X", W, 2 * W), r("X", 0, W))
-    for n, L in enumerate(("LA", "LB", "LD")):
-        cp(r(L, 0, 128), r(("lb0", "lb1", "pa")[n], 0, 128))
+    cp(r("X", W, W + K), r("X", 0, K))
     act(r("w", 0, K), r("D2", 0, K))
-    act(r("X", 2 * W, 2 * W + 3072), r("X", 0, 3072))
-    cp(r("X", 2 * W + 3072, 3 * W), r("X", 3072, W))
+    act(r("X", W + K, 2 * W), r("X", K, W))
     cp(r("FB", 0, 256), r("FR", 0, 256))
     iota(r("DI", 0, 16), [[1, 16]], 0, 16)
     iota(r("XW2", 0, 16), [[-2, 2], [0, 8]], 1, 0)
     iota(r("NBI", 0, 128), [[0, 128]], 0, 0)
     band(r("XW2", 0, 16), r("XW2", 0, 16), [[0, 2], [-16, 8]])()
-    sel(r("NBI", 0, 128), r("NBI", 0, 128), [[-1, 128]], A.not_equal, -BIG2, 0, 1)
+    sel(r("NBI", 0, 128), r("NBI", 0, 128), [[-1, 128]], A.not_equal, -BIG4, 0, 1)
+    sel(r("IDs", 0, 128), IDn, [[-1, 128]], A.not_equal, 1.0 / Z, 0, 1)
     ts(r("DI", 0, 16), r("DI", 0, 16), 255, A.bitwise_and)
     tt(r("FB", 256, 512), r("FR", 0, 256), r("FB", 0, 256), A.subtract)
     ts(r("DL", 0, 16), r("DI", 0, 16), float(DUMP), A.add)
+    for n, L in enumerate(("LA", "LB")):
+        cp(r(L, 0, 128), r(("lb0", "lb1")[n], 0, 128))
+    sel(r("NID", 0, 128), IDn, [[-1, 128]], A.not_equal, -1, 0, 1)
     weights(("L", WL), ("B", WB))
 
     def later():
-        mv("y", "cpa", r("TA", 0, 3 * W), r("TB", 0, 3 * W))
-        for s in range(3):
-            for i in range(2):
-                mv("y", "fra", trow("TA", rFR + i, W * s, W * s + W), r("FB", 256 * i, 256 * i + 256))
-        iota(r3("ZF", 33, 16 * len(ZNAMES) + 1), [[0, 1024]], 0, 0)
-        iota(r3("ZW", 0, 33), [[0, 264]], 0, 0)
+        g.sync.wait_ge(T.sem.xs, len(topo.engines(core, helper(rank))))
+        for rw in range(16):
+            if rw in (rFR, rFR + 1):
+                for s in range(3):
+                    mv("y", "cpa", trow("TA", rw, W * s, W * s + W), r("FB", 256 * (rw - rFR), 256 * (rw - rFR) + 256))
+            else:
+                mv("y", "cpa", trow("TA", rw, 0, 3 * W), trow("TB", rw, 0, 3 * W))
+        iota(r3("ZF", 33, 16 * len(ZNAMES) + 1), [[0, 512]], 0, 0)
+        iota(r3("ZW", 0, 161), [[0, 1288]], 0, 0)
         iota(r3("RMX", 0, 16), [[0, 256]], 0, 0)
         iota(r("TWO", 0, 128), [[0, 128]], 2, 0)
         iota(r("GK", 0, 16), [[0, 16]], 16384, 0)
@@ -356,7 +383,10 @@ def rank_program(g, core, T, topo):
         sel(r("RS", 0, 256), r("ONf", 0, 256), [[0, 16], [1, 16]], A.is_gt, 0, 0, 0)
         sel(r("ISN", 0, 128), IDb, [[0, 8], [-1, 16]], A.is_ge, 0, 1, 0)
         sel(r("KEEP", 0, 128), IDb, [[0, 8], [1, 16]], A.is_ge, 0, -2, 0)
-        sel(r("SUM", 0, 128), BDb, [[16, 8], [0, 16]], A.is_ge, 0, 1, -1)
+        sel(r("ID64", 0, 128), IDb, [[-1, 128]], A.not_equal, 64, 0, 1)
+        iota(r("SUM", 0, 128), [[0, 128]], 0, 0)
+        for rw, wt in num(rNA):
+            sel(r("SUM", 0, 128), r("SUM", 0, 128), [[-16, 8], [0, 16]], A.not_equal, wt, -rw, 1)
         sel(r("M1", 0, 128), r("BD2", 0, 128), [[1, 128]], A.is_gt, 0, 0, -1)
         sel(r("M2", 0, 128), r("BD2", 0, 128), [[-1, 128]], A.is_gt, 0, 0, 1)
         for n in ("M1", "M2"):
@@ -370,16 +400,17 @@ def rank_program(g, core, T, topo):
             mm(r(ps, b, 8 * n, 8), r(src, c0 + b, c0 + 1024, 8), wk, start and b == 0, stop and b == 7)
 
     def zin(z, n=1):
-        i = 16 * ZNAMES.index(z)
-        return r3("ZF", i + 1, i + 16 * n, 2)
+        buf, i = ("ZF", 16 * ZNAMES.index(z)) if z in ZNAMES else ("ZW", 16 * ZSMALL.index(z))
+        return r3(buf, i + 1, i + 16 * n, 2)
 
-    def turn(z, ps, pc):
-        if z[0] == "W":
-            buf, i, ident = "ZW", 16 * int(z[1]), "IDb"
+    def turn(z, ps, pc, words=False):
+        if z in ZNAMES:
+            buf, at, ident = "ZF", [16 * ZNAMES.index(z)], "IDs" if words else "IDn"
         else:
-            buf, i, ident = "ZF", 16 * ZNAMES.index(z), "IDn"
-        mm(r(ps, pc, pc + 64), r3(buf, i + 1, i + 17), r(ident, 0, 128, 2), True, False)
-        mm(r(ps, pc, pc + 64), r3(buf, i, i + 16), r(ident, 1, 128, 2), False, True)
+            buf, at, ident = "ZW", [16 * ZSMALL.index(n) for n in (z, z.lower()) if n in ZSMALL], "IDb"
+        for i in at:
+            mm(r(ps, pc, pc + 64), r3(buf, i + 1, i + 17), r(ident, 0, 128, 2), i == at[0], False)
+            mm(r(ps, pc, pc + 64), r3(buf, i, i + 16), r(ident, 1, 128, 2), False, i == at[-1])
 
     def ask(q, buf, tab, L, h, c0=0, c1=64):
         look(q, r(buf, 1024 * h + 16 * c0, 1024 * h + 16 * c1), r(tab, 0, DUMP), r(L, 64 * h + c0, 64 * h + c1))
@@ -388,17 +419,24 @@ def rank_program(g, core, T, topo):
         lookt(r("CM%d" % h, 16 * c0, 16 * c1), r("X", 0, 3 * W), r("LA", 64 * h + c0, 64 * h + c1),
               r("w", 1024 * h + 16 * c0, 1024 * h + 16 * c1), A.is_ge)
 
-    def hit(h):
+    def counts(h, c0, c1):
+        for b in range(8):
+            mm(r("cb%d" % h, b, 128, 8, 2 * c0, 2 * c1), r("CM%d" % h, 16 * c0 + b, 16 * c1, 8), r("XW2", 0, 16), False, b == 7)
+
+    def hit(h, early=False, c0=0):
         cb = "cb%d" % h
-        mm(r(cb, 0, 128), ONb, r("C17", 0, 128), True, False)
-        units(cb, "CM%d" % h, 0, r("XW2", 0, 16), False, True)
+        if not early:
+            mm(r(cb, 0, 128), ONb, r("C17", 0, 128), True, False)
+        counts(h, c0, 64)
         act(r("HM%d" % h, 0, 128), r(cb, 0, 128), AF.Sigmoid, -3400.0, 400.0)
 
     def answers(h, last):
         tb, hm = "tb%d" % h, "HM%d" % h
-        units(tb, "TG", 1024 * h, wts("L" if last else "F", 0, 7), True, False)
-        for a0, a1, c0 in ((0, 1, 64), (1, 3, 0), (3, 4, 64), (4, 6, 0), (6, 7, 64)):
-            mm(r(tb, 64 * a0, 64 * a1), r("NBI", 0, 128), r(hm, c0, c0 + 64 * (a1 - a0)), False, a1 == 7)
+        units(tb, "TG", 1024 * h, wts("L" if last else "F", 0, 8), True, False)
+        for a0, a1, c0 in ((0, 1, 64), (1, 2, 64), (2, 4, 0), (5, 7, 0), (7, 8, 64)):
+            mm(r(tb, 64 * a0, 64 * a1), r("NBI", 0, 128), r(hm, c0, c0 + 64 * (a1 - a0)), False, a1 == 8)
+        if not last:
+            mm(r("cb%d" % h, 0, 128), ONb, r("C17", 0, 128), True, False)
 
     def enlist(h):
         cp(r("LA", 64 * h, 64 * h + 64), r("lb%d" % h, 0, 64))
@@ -415,40 +453,36 @@ def rank_program(g, core, T, topo):
         units(ps, ("C2", "D2")[i - 1], 1024 * h, wts("R", 0, 1))
         return lambda: cp(r3("ST%d" % h, i, i + 1), r(ps, 0, 64))
 
-    def nextof(h, last):
-        st = "ST%d" % h
-        if last:
-            ts(r3(st, 0, 1), r3(st, 1, 2), 12, A.logical_shift_right)
-        else:
-            ts(r3(st, 0, 1), r3(st, 1, 2), 4095, A.bitwise_and)
-
     def refresh(tab, t):
         mark("ref%d" % t)
         ask("s", "TG", tab, "LA", 0)
         if t:
             ask("s", "TG", tab, "LA", 1)
-            pull(t - 1, 2)
-            pull(t - 1, 3, 0)
+            for c in (2, 3):
+                tt(r("w", 512 * c, 512 * c + 512), r("w", 512 * c, 512 * c + 512), r(("pa", "pb")[c % 2], 0, 512), A.add)
+            cp(r("LD", 0, 128), r("cb0", 128, 256))
+            ask("v", "C2", tab, "LB", 1, 0, 44)
             first(0)()
-            plus = pull(t - 1, 3, 1)
             ask("s", "D2", tab, "LD", 0)
-            ask("s", "C2", tab, "LB", 1)
+            ask("s", "C2", tab, "LB", 1, 44, 64)
+            ask("v", "C2", tab, "LB", 0, 0, 32)
             enlist(0)
-            plus()
+            ask("v", "C2", tab, "LB", 0, 32, 64)
+            ask("s", "TG", "TB", "LA", 0)
             match(0)
             first(1)()
-            ask("v", "C2", tab, "LB", 0)
+            ask("v", "D2", tab, "LD", 1, 0, 28)
             enlist(1)
             hit(0)
-            ask("s", "TG", "TB", "LA", 0)
-            ask("v", "D2", tab, "LD", 1)
+            ask("v", "D2", tab, "LD", 1, 28, 64)
         else:
             ask("v", "TG", tab, "LA", 1)
-            ask("s", "D2", tab, "LD", 0)
+            ask("s", "C2", tab, "LB", 1)
+            cp(r("LD", 0, 128), r("pa", 0, 128))
             ask("v", "C2", tab, "LB", 0)
             for f in [first(0), first(1)]:
                 f()
-            ask("s", "C2", tab, "LB", 1)
+            ask("s", "D2", tab, "LD", 0)
             ask("v", "D2", tab, "LD", 1)
             enlist(0)
             enlist(1)
@@ -462,135 +496,167 @@ def rank_program(g, core, T, topo):
         for f in fin[:3]:
             f()
         answers(0, False)
-        nextof(0, False)
-        nextof(1, False)
+        match(1, 0, CUTS[0])
         fin[3]()
-        match(1)
 
     def settle(h):
-        tt(r3("ST%d" % h, 1, 3), r("y%d" % h, 64, 192), r("tb%d" % h, 320, 448), A.max)
+        tt(r3("ST%d" % h, 1, 3), r("y%d" % h, 64, 192), r("tb%d" % h, 384, 512), A.max)
 
     def finds(t):
         mark("find%d" % t)
         aside = numbers() if t == ROUNDS - 1 else iter(())
+        minus = less(8, 16)
         for n in range(2 * FINDS):
             h, o, q = n % 2, 1 - n % 2, n // 2
             tb, st, y = "tb%d" % h, "ST%d" % h, "y%d" % h
-            more, late, last = n + 1 < 2 * FINDS, 0 < n < 2 * FINDS - 2, (n + 1) // 2 == FINDS - 1
-            kept = lambda: tt(r(y, 64, 128), r(y, 64, 128), r(tb, 192, 256), A.max)
+            more, late, last = n + 1 < 2 * FINDS, n < 2 * FINDS - 2, (n + 1) // 2 == FINDS - 1
             if more and not late:
-                hit(o)
-            tt(r(y, 0, 64), r3(st, 0, 1), r(tb, 0, 64), A.add)
-            tt(r(y, 64, 128), r3(st, 1, 2), r(tb, 64, 128), A.add)
-            tt(r(y, 0, 64), r(y, 0, 64), r(tb, 128, 192), A.max)
-            tt(r(tb, 192, 256), r3(st, 2, 3), r(tb, 192, 256), A.add)
-            tt(zin("A%d" % h), r(y, 0, 64), r(tb, 256, 320), A.max)
-            turn("A%d" % h, "lb%d" % h, 0)
-            tt(r(y, 128, 192), r3(st, 2, 3), r(tb, 64, 128), A.add)
-            if n:
+                hit(o, True)
+            if late and n:
+                counts(o, 0, 32)
+            if not more:
                 settle(o)
+                units("tb0", "TG", 0, wts("B", 0, 8))
+            rest = [lambda: tt(r(tb, 256, 320), r3(st, 1, 2), r(tb, 128, 192), A.add),
+                    lambda: tt(r(y, 128, 192), r3(st, 2, 3), r(tb, 128, 192), A.add)]
+            if n and more:
+                rest.append(lambda: settle(o))
+            tt(r(y, 0, 128), r3(st, 0, 3, 2) if q == FINDS - 1 else r3(st, 1, 3), r(tb, 0, 128), A.add)
             if late:
-                match(o, 64 - LATE, 64)
-                hit(o)
-                enlist(h)
-                kept()
-                nextof(o, last)
+                match(o, CUTS[0], CUTS[1])
+                if n:
+                    counts(o, 32, 48)
             else:
-                kept()
-                if n and more:
-                    nextof(o, last)
+                rest.pop(0)()
+            tt(r(y, 0, 64), r(y, 0, 64), r(tb, 192, 256), A.max)
+            if late:
+                match(o, CUTS[1], CUTS[2])
+            else:
+                rest.pop()()
+            if not more:
+                cursors(0)
+            tt(zin("A%d" % h), r(y, 0, 64), r(tb, 320, 384), A.max)
+            turn("A%d" % h, "lb%d" % h, 0, q < FINDS - 1)
+            if late:
+                match(o, CUTS[2], CUTS[3])
+                hit(o, n > 0, 48 if n else 0)
+            for f in rest:
+                f()
+            if more and last:
+                ts(r3("ST%d" % o, 0, 1), r3("ST%d" % o, 1, 2), Z - 1, A.bitwise_and)
+            if not more:
+                wants(0)
+                act(zin("K0", 4), r("tb0", 256, 512))
+            if late:
+                enlist(h)
+            tt(r(y, 64, 128), r(y, 64, 128), r(tb, 256, 320), A.max)
+            if not late:
                 enlist(h)
             if more:
                 answers(o, last)
+            if n > 5:
+                next(minus, None)
+                next(minus, None)
             if q < FINDS - 1:
                 ask("s", "TG", "TB", "LA", h)
-                if n > 3:
+                if n > 2:
                     next(aside, lambda: None)()
-                match(h, 0, 64 - LATE if n < 2 * FINDS - 3 else 64)
+                match(h, 0, CUTS[0] if n < 2 * FINDS - 3 else 64)
             elif h == 0:
-                ask("s", "TG", "TA", "LA", 0)
+                ask("s", "TG", "TA", "LA", 0, 28, 64)
+                ask("v", "TG", "TA", "LA", 0, 0, 28)
+
+    def cursors(h):
+        ts(r("CD%d" % h, 0, 128), r3("ST%d" % h, 1, 3), Z - 1, A.bitwise_and)
 
     def wants(h):
         tb, cd = "tb%d" % h, "CD%d" % h
         tt(r("NE%d" % h, 0, 64), r(tb, 0, 64), r(cd, 0, 64), A.not_equal)
         tt(zin("B%d" % h, 2), r(tb, 128, 256), r(cd, 0, 128), A.add)
-        tt(r3("ZW", 16 * h + 1, 16 * h + 16, 2), r(tb, 64, 128), r("NE%d" % h, 0, 64), A.mult)
-        act(zin("K%d" % h, 2), r(tb, 256, 384))
-        turn("W%d" % h, "lb1", 64 * h)
+        tt(zin("W%d" % h), r(tb, 64, 128), r("NE%d" % h, 0, 64), A.mult)
 
     def boundary(t):
         mark("bnd%d" % t)
         fast = t == ROUNDS - 1
-        cursors = lambda h: ts(r("CD%d" % h, 0, 128), r3("ST%d" % h, 1, 3), 12, A.logical_shift_right)
         ask("s", "TG", "TA", "LA", 1, 36, 64)
-        ask("v", "TG", "TA", "LA", 1, 0, 36)
-        units("tb0", "TG", 0, wts("B", 0, 6))
         settle(1)
-        units("tb1", "TG", 1024, wts("B", 0, 6))
-        cursors(0)
-        cursors(1)
-        wants(0)
-        wants(1)
+        ask("v", "TG", "TA", "LA", 1, 0, 36)
         turn("K0", "cb0", 0)
-        scan(r("CUM", 1, 129), ONb, r("lb1", 0, 128), 0.0)
-        mm(r("pa", 0, 128), r("CUM", 1, 129), BDb, True, True)
-        mm(r("pb", 0, 128), r("M1", 0, 128), r("CUM", 1, 129), True, False)
-        mm(r("pb", 0, 128), r("M2", 0, 128), r("CUM", 0, 128), False, True)
-        act(r("RW", 0, 128), r("pb", 0, 128))
+        turn("W0", "lb1", 0)
         turn("M0", "lb0", 0)
+        units("tb1", "TG", 1024, wts("B", 0, 8))
+        turn("B0", "cb1", 0)
         cp(r("LK", 0, 64), r("cb0", 0, 64))
-        pull(t, 0, 0)
-        tt(r("CB", 0, 128), r("pa", 0, 128), r("RC", 0, 128), A.subtract)
+        cursors(1)
+        near(t, 0, 256)
+        wants(1)
+        turn("W1", "lb1", 64)
+        act(zin("K1", 4), r("tb1", 256, 512))
+        near(t, 256, 512)
+        scan(r("CUM", 1, 129), ONb, r("lb1", 0, 128), 0.0)
+        mm(r("tb0", 0, 128), r("CUM", 1, 129), BDb, True, True)
+        mm(r("tb1", 0, 128), r("M1", 0, 128), r("CUM", 1, 129), True, False)
+        mm(r("tb1", 0, 128), r("M2", 0, 128), r("CUM", 0, 128), False, True)
+        act(r("RW", 0, 128), r("tb1", 0, 128))
+        turn("K1", "cb0", 64)
         turn("M1", "lb0", 64)
+        turn("B1", "cb1", 64)
+        near(t, 512, 768)
+        tt(r("CB", 0, 128), r("tb0", 0, 128), r("RC", 0, 128), A.subtract)
+        cp(r("LK", 64, 128), r("cb0", 64, 128))
+        act(r("MW", 0, 128), r("lb0", 0, 128))
         for k in range(8):
             ts(r("CP", 128 * k, 128 * k + 128), r("CB", 0, 128), 16.0 * k, A.is_le)
         for k in range(8):
             mm(r("lb1", 128 + k, 129 + k), r("CP", 128 * k, 128 * k + 128), r("ONb", 0, 1), True, True)
-        act(r("MW", 0, 128), r("lb0", 0, 128))
-        for h in range(2):
-            turn("B%d" % h, "cb1", 64 * h)
         act(r("CW", 0, 128), r("cb1", 0, 128), AF.Identity, 1.0)
-        pull(t, 0, 1)
+        near(t, 768, 1024)
         cp(r("LQ", 0, 8), r("lb1", 128, 136))
-        turn("K1", "cb0", 64)
+        pull(t, 2)
+        pull(t, 3)
+        cut(t, 0, 0, 256)
         LQ, EE = r("LQ", 0, 8), r("EE", 0, 128)
         lookt(EE, r("RW", 0, 136), LQ, r("IO2", 0, 128), A.is_equal)
-        cp(r("LK", 64, 128), r("cb0", 64, 128))
+        if fast:
+            cp(r("PR", 0, 128), r("LA", 0, 128))
+        else:
+            cp(r("LB", 0, 128), r("cb1", 0, 128))
         for i, n in enumerate(("MW", "CW")):
             lookt(r("PM", 128 * i, 128 * i + 128), r(n, 0, 136), LQ, EE, A.mult)
-            mm(r("pa", 128 * i, 128 * i + 128), BDf, r("PM", 128 * i, 128 * i + 128), True, True)
-        for h in range(2):
-            turn("D%d" % h, "cb0", 128 + 64 * h)
-        pull(t, 1, 0)
-        tt(r("MK", 0, 256), r("pa", 0, 256), r3("RMX", 0, 16), A.mult)
-        cp(r("PU", 0, 256), r("pa", 0, 256))
+            mm(r("tb0", 256 + 128 * i, 384 + 128 * i), BDf, r("PM", 128 * i, 128 * i + 128), True, True)
+        cut(t, 0, 256, 512)
+        plain(2)
+        cut(t, 1, 0, 256)
+        tt(r("MK", 0, 256), r("tb0", 256, 512), r3("RMX", 0, 16), A.mult)
+        cp(r("PU", 0, 256), r("tb0", 256, 512))
         scan(r("OWS", 0, 256), r("RS", 0, 256), r("MK", 0, 256), 0.0)
-        pull(t, 1, 1)
-        if fast:
-            pull(t, 2)
-            pull(t, 3)
+        cut(t, 1, 256, 512)
+        plain(3)
         ow = r("OWS", 15, 256, 16)
         ts(r("LG", 0, 16), ow, -1.0, A.add)
-        look("s", r("G3", 0, 256), r("TA", 0, DUMP), r("LG", 0, 16))
         ts(r("OW1", 0, 16), ow, -1.0 - 2 * 16384, A.add)
+        mm(r("lb1", 160, 176), IDn, r("OW1", 0, 16), True, False)
+        look("s", r("G3", 0, 256), r("TA", 0, DUMP), r("LG", 0, 16))
         for k in range(16):
-            e = r("EQ", 256 * k, 256 * k + 256)
-            ts(e, r("PU", 0, 256), r("OWS", 16 * k + 15, 16 * k + 16), A.is_equal)
+            ts(r("EQ", 256 * k, 256 * k + 256), r("PU", 0, 256), r("OWS", 16 * k + 15, 16 * k + 16), A.is_equal)
             for i in range(2):
-                mm(r("pb", 0, 64), r("EQ", 256 * k + 128 * i, 256 * k + 128 * i + 128), r("GM8", 0, 64), k + i == 0, k + i == 16)
-            if k == 7:
+                mm(r("tb1", 128, 192), r("EQ", 256 * k + 128 * i, 256 * k + 128 * i + 128), r("GM8", 0, 64), k + i == 0, k + i == 16)
+            if k == 8:
                 for i in range(2):
+                    o = r("lb0", 256 + 128 * i, 384 + 128 * i)
                     if not fast:
-                        mm(r("tb0", 128 * i, 128 * i + 128), r("KEEP", 0, 128), r("G3", 128 * i, 128 * i + 128), True, False)
-                    mm(r("tb0", 128 * i, 128 * i + 128), r("SUM" if fast else "ISN", 0, 128), r("G3", 128 - 128 * i, 256 - 128 * i), fast, True)
-                act(r("G5" if fast else "G4", 0, 256), r("tb0", 0, 256))
-                mm(r("lb1", 160, 176), IDn, r("OW1", 0, 16), True, False)
+                        mm(o, r("KEEP", 0, 128), r("G3", 128 * i, 128 * i + 128), True, False)
+                    mm(o, r("SUM" if fast else "ISN", 0, 128), r("G3", 128 - 128 * i, 256 - 128 * i), fast, True)
+                act(r("G5" if fast else "G4", 0, 256), r("lb0", 256, 512))
+        cut(t, 2)
         for i in range(2):
-            tt(r3("OKX", 0, 8, 1, 8 * i, 8 * i + 8), r("pb", 0, 64), r3("RMX", 0, 8, 1, 8 * i, 8 * i + 8), A.mult)
+            tt(r3("OKX", 0, 8, 1, 8 * i, 8 * i + 8), r("tb1", 128, 192), r3("RMX", 0, 8, 1, 8 * i, 8 * i + 8), A.mult)
         mm(r("lb1", 160, 176), r3("OKX", 0, 8), r("GK", 0, 16), False, True)
-        cp(r("LB", 0, 128), r("cb1", 0, 128))
+        for h in range(2):
+            turn("D%d" % h, "cb0", 128 + 64 * h)
+        cut(t, 3, 0, 384)
         tt(r("LPf", 0, 16), r("lb1", 160, 176), r("DL", 0, 16), A.min)
-        cp(r("LD", 0, 128), r("cb0", 128, 256))
+        cut(t, 3, 384, 512)
         cp(r("LP", 0, 16), r("LPf", 0, 16))
         tab, val = r("YW" if fast else "TA", 0, DUMP + 256), r("G5" if fast else "G4", 0, 256)
         op("v", lambda: V.tensor_copy(ap(tab).indirect(T.LP[:, 0:16]), ap(val)), [val, r("LP", 0, 16)], [tab])
@@ -600,38 +666,50 @@ def rank_program(g, core, T, topo):
             rebuild("rb%d" % t, "TA", (0, 1, 2))
 
     def numbers():
-        for i, d in ((0, "N1"), (1, "N2")):
-            mv("y", "yl", r(d, 0, 768), trow("TA", i, 0, 3 * W))
         for c0, c1, b in ((0, 512, "pa"), (512, 768, "pb")):
             for i, d in enumerate(("N1", "N2")):
-                mm(r(b, 0, c1 - c0), IDb, r(d, c0, c1), i == 0, i == 1)
-        for c0 in (0, 256, 512):
-            yield lambda c0=c0: act(r("DD", c0, c0 + 256), r(("pa", "pb")[c0 // 512], c0 % 512, c0 % 512 + 256))
-        yield lambda: mv("y", "yw1", trow("YW", 0, 0, 3 * W), r("DD", 0, 768))
+                mm(r(b, 0, c1 - c0), r(("IDb", "ID64")[i], 0, 128), r(d, c0, c1), i == 0, i == 1)
+        yield lambda: act(r("DD", 0, 512), r("pa", 0, 512), AF.Identity, float(K))
 
-    def pull(t, c, part=None):
-        d, wv = r("D%d" % (c % 2), 0, 512), r("w", 512 * c, 512 * c + 512)
-        cl = r("DD", 512 * c, 512 * c + 512)
-        if part != 1:
-            lookt(d, r("xb%d" % t, 0, W), r("LK", 32 * c, 32 * c + 32), wv, A.subtract)
-        if part != 0 and c == 3 and t < ROUNDS - 1:
-            ts(r("cb1", 0, 512), d, -8.0, A.max, 8.0, A.min)
-            return lambda: tt(wv, wv, r("cb1", 0, 512), A.add)
-        if part != 0:
-            ts(cl, d, -8.0, A.max, 8.0, A.min)
-            if t == ROUNDS - 1:
-                add("wa20", r("yw", 512 * c, 512 * c + 512), cl)
-            else:
-                add("wa%d%d" % (t, c // 2), wv, cl)
+        def rest():
+            act(r("DD", 512, 768), r("pb", 0, 256), AF.Identity, float(K))
+            mv("y", "yw1", trow("YW", 0, 0, 3 * W), r("DD", 0, 768))
+        yield rest
+
+    def pull(t, c):
+        c0 = 512 * (c % 2)
+        look("s", r("CM%d" % (c // 2), c0, c0 + 512), r("xb%d" % t, 0, W), r("LK", 32 * c, 32 * c + 32))
+
+    def less(a, b):
+        for i in range(a, b):
+            c0 = 128 * (i % 4)
+            mm(r(("pa", "pb")[i // 4 % 2], c0, c0 + 128), r("NID", 0, 128), r("w", 128 * i, 128 * i + 128), c0 == 0, False)
+            yield None
+
+    def plain(c):
+        c0 = 512 * (c % 2)
+        mm(r(("pa", "pb")[c % 2], 0, 512), IDb, r("CM%d" % (c // 2), c0, c0 + 512), False, True)
+
+    def near(t, c0, c1):
+        lookt(r("D0", c0, c1), r("xb%d" % t, 0, W), r("LK", c0 // 16, c1 // 16), r("w", c0, c1), A.subtract)
+
+    def cut(t, c, a=0, b=512):
+        d = r("D0", 512 * c + a, 512 * c + b) if c < 2 else r(("pa", "pb")[c % 2], a, b)
+        if c > 1 and t < ROUNDS - 1:
+            ts(d, d, -8.0, A.max, 8.0, A.min)
+            return
+        ts(r("DD", 512 * c + a, 512 * c + b), d, -8.0, A.max, 8.0, A.min)
+        if b == 512:
+            add("wa%d0" % t, r("w" if t < ROUNDS - 1 else "yw", 512 * c, 512 * c + 512), r("DD", 512 * c, 512 * c + 512))
 
     for t in range(ROUNDS):
         if t == 0:
-            send(0)
+            send()
             later()
         refresh("TA" if t else "TB", t)
-        if t:
-            send(t)
         if t == ROUNDS - 1:
+            for i, d in ((0, "N1"), (1, "N2")):
+                mv("y", "yl", r(d, 0, 768), trow("TA", i, 0, 3 * W))
             mv("y", "out0", r("yw", 0, K), r("w", 0, K))
         finds(t)
         boundary(t)
@@ -639,11 +717,10 @@ def rank_program(g, core, T, topo):
     a_, lo, hi = (r("PR", 128 * i, 128 * i + 128) for i in range(3))
     b_, d_, m_ = r("cb1", 0, 128), r("cb0", 128, 256), r("cb1", 128, 256)
     y0, y1, y2 = (r("CF", 128 * i, 128 * i + 128) for i in range(3))
-    cp(a_, r("LA", 0, 128))
-    tt(lo, a_, b_, A.min)
     tt(hi, a_, b_, A.max)
-    tt(y0, lo, d_, A.min)
+    tt(lo, a_, b_, A.min)
     tt(m_, hi, d_, A.min)
+    tt(y0, lo, d_, A.min)
     tt(hi, hi, d_, A.max)
     tt(lo, lo, m_, A.max)
     ts(y2, hi, -2.0 * W, A.add)
@@ -651,7 +728,7 @@ def rank_program(g, core, T, topo):
     dma("y", "out2", T.yc[:, :], T.CF[:, :], None, r("CF", 0, 384))
     for sem in SEMAPHORES:
         if sem == "xs":
-            g.wait_ge(T.sem.xs, nloc[0])
+            g.wait_ge(T.sem.xs, len(topo.engines(core, helper(rank))))
         elif count.get(sem, 0):
             known["g"].pop(sem, None)
             wait("g", (sem, count[sem]))

@@ -4,16 +4,16 @@ ROUNDS, FINDS, W, K = 3, 6, 4096, 2048
 DUMP = 3 * W
 B, FL, IN, U16, SB = "bfloat16", "float32", "int32", "uint16", "sbuf"
 rNA, rNB, rND, rV, rJB, rJD, rFR, rU0, rU1, rONE, rTWO = 0, 2, 4, 6, 8, 9, 10, 12, 13, 14, 15
-BIG1, BIG2, BIG3, BIG4 = 2 ** 15, 2 ** 26, 2 ** 28, 2 ** 29
+BIG1, BIG2, BIG4 = 2 ** 15, 2 ** 26, 2 ** 29
 Z = 8192
-CUTS = (42, 48, 54, 64)
+CUT = 48
 
 SCRATCH = {}
 for _dt, _names in (
-    (B, "X:12288 TB:12288 TA:12544 xb0:4096 xb1:4096 xb2:4096 TG:2048 C2:2048 D2:2048 CM0:1024 CM1:1024 CP:1024 EQ:4096 "
-        "N1:768 N2:768 MJ:768 FB:512 LO:256 HM0:128 HM1:128 WW:208 C17:128 NBI:128 XW2:16 GM8:64 GK:16 ONb:128 TWO:128 IDb:128 ID64:128 "
+    (B, "X:12288 TB:12288 TA:12544 xb0:4096 xb1:4096 xb2:4096 TG:2048 C2:2048 D2:2048 CM0:1024 CM1:1024 EQ:4096 CK:64 "
+        "N1:768 N2:768 MJ:768 LO:256 HM0:128 HM1:128 WW:208 C17:128 NBI:128 PBI:128 XW2:16 GM8:64 GK:16 ONb:128 TWO:128 IDb:128 ID64:128 "
         "BDb:128 BD2:128 M1:128 M2:128 ISN:128 KEEP:128 SUM:128 RC:128 CUM:136 CB:128 NE0:64 NE1:64 G3:256 G4:256"),
-    (FL, "w:2048 YW:12544 DD:2048 D0:1024 NID:128 PR:384 CF:384 y0:192 y1:192 FC:8 CJ:16 ONf:256 IDn:128 IDs:128 BDf:128 "
+    (FL, "w:2048 YW:12544 DD:2048 D0:1024 NID:128 PR:384 CF:384 y0:192 y1:192 p0:64 p1:64 FC:8 CJ:16 ONf:256 IDn:128 IDs:128 BDf:128 "
          "IO2:128 RS:256 RW:136 MW:136 CW:136 EE:128 PM:256 MK:256 OWS:256 G5:256 OW1:16 DL:16 LPf:16"),
     (IN, "NX:768 ME:256 FR:256 CU:384 TY:128 CD0:128 CD1:128 HI:4 DI:16"),
     (U16, "LA:128 LB:128 LD:128 LK:128 LQ:8 LG:16 LP:16 PU:256"),
@@ -21,7 +21,7 @@ for _dt, _names in (
     for _n in _names.split():
         SCRATCH[_n.split(":")[0]] = (SB, [128, int(_n.split(":")[1])], _dt)
 ZNAMES = "A0 A1 B0 D0 B1 D1".split()
-ZSMALL = "W0 W1 K0 k0 M0 m0 K1 k1 M1 m1".split()
+ZSMALL = "E0 E1 W0 W1 K0 k0 M0 m0 K1 k1 M1 m1".split()
 SCRATCH["ZF"] = (SB, [128, 16 * len(ZNAMES) + 1, 8], FL)
 SCRATCH["ZW"] = (SB, [128, 16 * len(ZSMALL) + 1, 8], B)
 SCRATCH["RMX"] = (SB, [128, 16, 16], FL)
@@ -253,9 +253,10 @@ def rank_program(g, core, T, topo):
     packD = pack(rND) + ((rJD, -BIG2),)
     keepD = ((rONE, -BIG2), (rJD, BIG2))
     WR = (pack(rNA), num(rNA) + typ0)
-    WF = (times(typ1, Z) + ((rONE, K * Z - BIG3), (rTWO, -W), (rJB, BIG3)), keepD, (), times(num(rNB) + typ1, Z) + ((rJB, -BIG3),), (),
-          times(num(rNA) + typ0, Z), packD, pack(rNA))
-    WL = (typ1 + ((rONE, -K - BIG1), (rJB, BIG1)), keepD, (), rec() + typ1 + ((rJB, -BIG1),), (), rec() + typ0, packD, pack(rNA))
+    base = typ1 + ((rONE, K - Z), (rJB, Z))
+    less_ = times(base, -1) + ((rTWO, 0.5),)
+    WF = (times(num(rNB) + typ1 + less_, Z) + ((rJB, -BIG2),), keepD, (), times(num(rNA) + typ0 + less_, Z), (), packD, pack(rNA), base)
+    WL = (rec() + typ1 + less_ + ((rJB, -BIG1),), keepD, (), rec() + typ0 + less_, (), packD, pack(rNA), base)
     WB = (rec() + ((rONE, K),), ((rONE, 1), (rJB, -1)), typ1 + ((rONE, -K),), typ2 + ((rONE, -K),), ((rFR, 1),), ((rFR + 1, 1),),
           rec()[:1] + ((rONE, 1),), rec()[1:] + typ1)
     WPOS = {"R": 0, "F": 2, "L": 10, "B": 18}
@@ -278,7 +279,7 @@ def rank_program(g, core, T, topo):
 
     ONb, IDn, IDb, BDb, BDf = (r(n, 0, 128) for n in ("ONb", "IDn", "IDb", "BDb", "BDf"))
     iota(r("HI", 0, 1), [[1, 1]], 0, 1)
-    iota(r("CJ", 0, 16), [[1, 16]], 0, 0)
+    iota(r("CJ", 0, 16), [[1, 16]], -1, 0)
     iota(r("LO", 0, 256), [[1, 256]], 0, 0)
     iota(r("WW", 0, 208), [[0, 208]], 0, 0)
     iota(r("ONf", 0, 256), [[0, 256]], 1, 0)
@@ -299,10 +300,13 @@ def rank_program(g, core, T, topo):
 
     fc = lambda i: r("FC", i, i + 1)
     ts(r("HI", 0, 1), r("HI", 0, 1), 15, A.bitwise_and)
-    for i, (rw, f) in enumerate(((rV, A.is_equal), (rV + 1, A.is_equal), (rV, A.not_equal), (rU0, A.not_equal), (rU1, A.not_equal))):
+    mset(r3("ZF", 0, 33), 0.0)
+    for i, rw, f in ((1, rV + 1, A.is_equal), (2, rV, A.not_equal), (0, rV, A.is_equal), (3, rU0, A.not_equal), (4, rU1, A.not_equal)):
         ts(fc(i), r("HI", 0, 1), float(rw), f)
-    tt(fc(2), fc(2), fc(1), A.subtract)
+    mset(r("C17", 0, 64), 0.0)
     ts(r("CJ", 0, 16), r("CJ", 0, 16), fc(1), A.mult, fc(2), A.add)
+    mset(r("C17", 64, 128), 17.0 / 128)
+    mset(r("CUM", 0, 8), 0.0)
     for j in range(16):
         ts(r("TB", 2 * W + 256 * j, 2 * W + 256 * j + 256), r("LO", 0, 256), fc(0), A.mult, r("CJ", j, j + 1), A.add)
         if j % 4 == 3:
@@ -318,21 +322,18 @@ def rank_program(g, core, T, topo):
         mv("y", "r1", trow("TB", i, 0, 3 * W), r(("N1", "N2")[i], 0, 768))
     for i in range(2):
         ts(r("NX", 256 * i, 256 * i + 256), r("ME", 0, 256), 2 ** i, A.bitwise_and)
+    for i in range(3):
+        ts(r("tb0", 128 * i, 128 * i + 128), r("CU", 128 * i, 128 * i + 128), float(W * i), A.add)
     ts(r("MJ", 0, 512), r("NX", 0, 512), 0.0, A.is_equal)
     for s in range(3):
         mv("y", "r2", trow("TB", rJB, W * s, W * s + W), r("MJ", 256 * ((s + 1) % 3), 256 * ((s + 1) % 3) + 256))
     rebuild("r5", "TB", (1, 2))
     turned("r5", "TB", rJB, rJD, 1)
     mv("y", "r3", r("X", 2 * W, 3 * W), r("X", 0, W))
-    mset(r3("ZF", 0, 33), 0.0)
-    mset(r("C17", 0, 64), 0.0)
-    mset(r("C17", 64, 128), 17.0 / 128)
-    mset(r("CUM", 0, 8), 0.0)
 
-    for i in range(3):
-        ts(r("tb0", 128 * i, 128 * i + 128), r("CU", 128 * i, 128 * i + 128), float(W * i), A.add)
-    for i in range(5):
+    for i in (4, 3, 2, 1, 0):
         ts(r("DD", 128 * i, 128 * i + 128), r("TY", 0, 128), float((i + 1) % 3), A.is_equal)
+    cp(r("EQ", 0, 256), r("FR", 0, 256))
     for n in range(3):
         c0 = 640 + 384 * n
         tt(r("DD", c0, c0 + 384), r("tb0", 0, 384), r("DD", 128 * (2 - n), 128 * (5 - n)), A.mult)
@@ -342,32 +343,38 @@ def rank_program(g, core, T, topo):
     cp(r("X", W, W + K), r("X", 0, K))
     act(r("w", 0, K), r("D2", 0, K))
     act(r("X", W + K, 2 * W), r("X", K, W))
-    cp(r("FB", 0, 256), r("FR", 0, 256))
     iota(r("DI", 0, 16), [[1, 16]], 0, 16)
+    iota(r("ME", 0, 256), [[0, 16], [-1, 16]], 16, 1)
+    mset(r3("ZW", 0, 33), 0.0)
+    mset(r("CK", 0, 64), -0.5 / 128)
+    mset(IDb, 1.0)
     iota(r("XW2", 0, 16), [[-2, 2], [0, 8]], 1, 0)
     iota(r("NBI", 0, 128), [[0, 128]], 0, 0)
     band(r("XW2", 0, 16), r("XW2", 0, 16), [[0, 2], [-16, 8]])()
     sel(r("NBI", 0, 128), r("NBI", 0, 128), [[-1, 128]], A.not_equal, -BIG4, 0, 1)
+    sel(r("PBI", 0, 128), r("NBI", 0, 128), [[-1, 128]], A.not_equal, BIG4, 0, 1)
     sel(r("IDs", 0, 128), IDn, [[-1, 128]], A.not_equal, 1.0 / Z, 0, 1)
     ts(r("DI", 0, 16), r("DI", 0, 16), 255, A.bitwise_and)
-    tt(r("FB", 256, 512), r("FR", 0, 256), r("FB", 0, 256), A.subtract)
+    tt(r("EQ", 256, 512), r("FR", 0, 256), r("EQ", 0, 256), A.subtract)
+    ts(r("ME", 0, 256), r("ME", 0, 256), 15, A.bitwise_and)
     ts(r("DL", 0, 16), r("DI", 0, 16), float(DUMP), A.add)
     for n, L in enumerate(("LA", "LB")):
         cp(r(L, 0, 128), r(("lb0", "lb1")[n], 0, 128))
-    sel(r("NID", 0, 128), IDn, [[-1, 128]], A.not_equal, -1, 0, 1)
-    weights(("L", WL), ("B", WB))
+    ts(r3("RMX", 0, 16), r("ME", 0, 256), 0.0, A.is_equal)
+    sel(IDb, IDb, [[-1, 128]], A.is_equal, 0, 0, 1)
 
     def later():
         g.sync.wait_ge(T.sem.xs, len(topo.engines(core, helper(rank))))
         for rw in range(16):
             if rw in (rFR, rFR + 1):
                 for s in range(3):
-                    mv("y", "cpa", trow("TA", rw, W * s, W * s + W), r("FB", 256 * (rw - rFR), 256 * (rw - rFR) + 256))
+                    mv("y", "cpa", trow("TA", rw, W * s, W * s + W), r("EQ", 256 * (rw - rFR), 256 * (rw - rFR) + 256))
             else:
                 mv("y", "cpa", trow("TA", rw, 0, 3 * W), trow("TB", rw, 0, 3 * W))
+        sel(r("NID", 0, 128), IDn, [[-1, 128]], A.not_equal, -1, 0, 1)
+        weights(("L", WL), ("B", WB))
         iota(r3("ZF", 33, 16 * len(ZNAMES) + 1), [[0, 512]], 0, 0)
-        iota(r3("ZW", 0, 161), [[0, 1288]], 0, 0)
-        iota(r3("RMX", 0, 16), [[0, 256]], 0, 0)
+        iota(r3("ZW", 33, 16 * len(ZSMALL) + 1), [[0, 1280]], 0, 0)
         iota(r("TWO", 0, 128), [[0, 128]], 2, 0)
         iota(r("GK", 0, 16), [[0, 16]], 16384, 0)
         for n in ("RW", "MW", "CW"):
@@ -375,7 +382,6 @@ def rank_program(g, core, T, topo):
         fin = [band(BDb, ONb, [[-16, 8], [0, 16]]), band(BDf, r("ONf", 0, 128), [[-16, 8], [0, 16]]),
                band(r("BD2", 0, 128), r("TWO", 0, 128), [[-16, 8], [0, 16]]), band(r("GM8", 0, 64), r("ONb", 0, 64), [[-16, 8], [0, 8]]),
                band(r("GK", 0, 16), r("GK", 0, 16), [[0, 2], [-16, 8]])]
-        sel(IDb, ONb, [[-1, 128]], A.is_equal, 0, 0, 1)
         for f in fin:
             f()
         iota(r("RC", 0, 128), [[0, 8], [1, 16]], 0, 0)
@@ -391,8 +397,6 @@ def rank_program(g, core, T, topo):
         sel(r("M2", 0, 128), r("BD2", 0, 128), [[-1, 128]], A.is_gt, 0, 0, 1)
         for n in ("M1", "M2"):
             sel(r(n, 0, 128), r(n, 0, 128), [[-1, 128]], A.not_equal, 1, 0, 1)
-        for k in range(8):
-            sel(r3("RMX", 0, 16), r3("RMX", 0, 16), [[0, 16], [-1, 16]], A.not_equal, 1, -16 * k, 1)
 
     def units(ps, src, c0, wk, start=True, stop=True):
         n = wk[2] - wk[1]
@@ -403,14 +407,14 @@ def rank_program(g, core, T, topo):
         buf, i = ("ZF", 16 * ZNAMES.index(z)) if z in ZNAMES else ("ZW", 16 * ZSMALL.index(z))
         return r3(buf, i + 1, i + 16 * n, 2)
 
-    def turn(z, ps, pc, words=False):
+    def turn(z, ps, pc, words=False, onto=False, stop=True):
         if z in ZNAMES:
             buf, at, ident = "ZF", [16 * ZNAMES.index(z)], "IDs" if words else "IDn"
         else:
             buf, at, ident = "ZW", [16 * ZSMALL.index(n) for n in (z, z.lower()) if n in ZSMALL], "IDb"
         for i in at:
-            mm(r(ps, pc, pc + 64), r3(buf, i + 1, i + 17), r(ident, 0, 128, 2), i == at[0], False)
-            mm(r(ps, pc, pc + 64), r3(buf, i, i + 16), r(ident, 1, 128, 2), False, i == at[-1])
+            mm(r(ps, pc, pc + 64), r3(buf, i + 1, i + 17), r(ident, 0, 128, 2), i == at[0] and not onto, False)
+            mm(r(ps, pc, pc + 64), r3(buf, i, i + 16), r(ident, 1, 128, 2), False, i == at[-1] and stop)
 
     def ask(q, buf, tab, L, h, c0=0, c1=64):
         look(q, r(buf, 1024 * h + 16 * c0, 1024 * h + 16 * c1), r(tab, 0, DUMP), r(L, 64 * h + c0, 64 * h + c1))
@@ -419,24 +423,21 @@ def rank_program(g, core, T, topo):
         lookt(r("CM%d" % h, 16 * c0, 16 * c1), r("X", 0, 3 * W), r("LA", 64 * h + c0, 64 * h + c1),
               r("w", 1024 * h + 16 * c0, 1024 * h + 16 * c1), A.is_ge)
 
-    def counts(h, c0, c1):
-        for b in range(8):
-            mm(r("cb%d" % h, b, 128, 8, 2 * c0, 2 * c1), r("CM%d" % h, 16 * c0 + b, 16 * c1, 8), r("XW2", 0, 16), False, b == 7)
-
-    def hit(h, early=False, c0=0):
+    def hit(h, early=False):
         cb = "cb%d" % h
         if not early:
             mm(r(cb, 0, 128), ONb, r("C17", 0, 128), True, False)
-        counts(h, c0, 64)
+        units(cb, "CM%d" % h, 0, r("XW2", 0, 16), False, True)
         act(r("HM%d" % h, 0, 128), r(cb, 0, 128), AF.Sigmoid, -3400.0, 400.0)
 
     def answers(h, last):
         tb, hm = "tb%d" % h, "HM%d" % h
         units(tb, "TG", 1024 * h, wts("L" if last else "F", 0, 8), True, False)
-        for a0, a1, c0 in ((0, 1, 64), (1, 2, 64), (2, 4, 0), (5, 7, 0), (7, 8, 64)):
-            mm(r(tb, 64 * a0, 64 * a1), r("NBI", 0, 128), r(hm, c0, c0 + 64 * (a1 - a0)), False, a1 == 8)
+        for a, c0, wt in ((0, 64, "PBI"), (3, 0, "PBI"), (1, 64, "NBI"), (2, 0, "NBI"), (5, 64, "NBI"), (6, 64, "NBI")):
+            mm(r(tb, 64 * a, 64 * a + 64), r(wt, 0, 128), r(hm, c0, c0 + 64), False, a == 6)
         if not last:
             mm(r("cb%d" % h, 0, 128), ONb, r("C17", 0, 128), True, False)
+        mm(r("lb%d" % h, 0, 64), ONb, r("CK", 0, 64), True, False)
 
     def enlist(h):
         cp(r("LA", 64 * h, 64 * h + 64), r("lb%d" % h, 0, 64))
@@ -458,23 +459,23 @@ def rank_program(g, core, T, topo):
         ask("s", "TG", tab, "LA", 0)
         if t:
             ask("s", "TG", tab, "LA", 1)
-            for c in (2, 3):
-                tt(r("w", 512 * c, 512 * c + 512), r("w", 512 * c, 512 * c + 512), r(("pa", "pb")[c % 2], 0, 512), A.add)
+            plus(3, 0, 512)
             cp(r("LD", 0, 128), r("cb0", 128, 256))
-            ask("v", "C2", tab, "LB", 1, 0, 44)
+            ask("v", "C2", tab, "LB", 1, 0, 52)
+            ask("v", "D2", tab, "LD", 1, 0, 16)
             first(0)()
             ask("s", "D2", tab, "LD", 0)
-            ask("s", "C2", tab, "LB", 1, 44, 64)
-            ask("v", "C2", tab, "LB", 0, 0, 32)
+            ask("s", "C2", tab, "LB", 1, 52, 64)
+            ask("v", "C2", tab, "LB", 0, 0, 40)
             enlist(0)
-            ask("v", "C2", tab, "LB", 0, 32, 64)
+            ask("v", "C2", tab, "LB", 0, 40, 64)
             ask("s", "TG", "TB", "LA", 0)
             match(0)
             first(1)()
-            ask("v", "D2", tab, "LD", 1, 0, 28)
+            ask("v", "D2", tab, "LD", 1, 16, 48)
             enlist(1)
             hit(0)
-            ask("v", "D2", tab, "LD", 1, 28, 64)
+            ask("v", "D2", tab, "LD", 1, 48, 64)
         else:
             ask("v", "TG", tab, "LA", 1)
             ask("s", "C2", tab, "LB", 1)
@@ -488,19 +489,20 @@ def rank_program(g, core, T, topo):
             enlist(1)
             ask("s", "TG", "TB", "LA", 0)
             match(0)
-        fin = [state(0, 2, "pa"), state(0, 1, "lb0"), state(1, 1, "pb")]
+        fin = [state(0, 2, "pa"), state(0, 1, "cb1"), state(1, 1, "pb")]
         if not t:
             hit(0)
         ask("s", "TG", "TB", "LA", 1)
         fin.append(state(1, 2, "lb1"))
-        for f in fin[:3]:
+        for f in fin[:2]:
             f()
         answers(0, False)
-        match(1, 0, CUTS[0])
-        fin[3]()
+        match(1, 0, CUT)
+        for f in fin[2:]:
+            f()
 
     def settle(h):
-        tt(r3("ST%d" % h, 1, 3), r("y%d" % h, 64, 192), r("tb%d" % h, 384, 512), A.max)
+        tt(r3("ST%d" % h, 1, 3), r("y%d" % h, 64, 192), r("tb%d" % h, 320, 448), A.max)
 
     def finds(t):
         mark("find%d" % t)
@@ -512,38 +514,28 @@ def rank_program(g, core, T, topo):
             more, late, last = n + 1 < 2 * FINDS, n < 2 * FINDS - 2, (n + 1) // 2 == FINDS - 1
             if more and not late:
                 hit(o, True)
-            if late and n:
-                counts(o, 0, 32)
             if not more:
                 settle(o)
                 units("tb0", "TG", 0, wts("B", 0, 8))
-            rest = [lambda: tt(r(tb, 256, 320), r3(st, 1, 2), r(tb, 128, 192), A.add),
-                    lambda: tt(r(y, 128, 192), r3(st, 2, 3), r(tb, 128, 192), A.add)]
+            tt(r(y, 0, 64), r("p%d" % h, 0, 64) if q == FINDS - 1 else r3(st, 1, 2), r(tb, 0, 64), A.max)
+            cp(zin("E%d" % h), r(tb, 448, 512))
+            turn("E%d" % h, "lb%d" % h, 0, False, True, False)
             if n and more:
-                rest.append(lambda: settle(o))
-            tt(r(y, 0, 128), r3(st, 0, 3, 2) if q == FINDS - 1 else r3(st, 1, 3), r(tb, 0, 128), A.add)
-            if late:
-                match(o, CUTS[0], CUTS[1])
-                if n:
-                    counts(o, 32, 48)
-            else:
-                rest.pop(0)()
-            tt(r(y, 0, 64), r(y, 0, 64), r(tb, 192, 256), A.max)
-            if late:
-                match(o, CUTS[1], CUTS[2])
-            else:
-                rest.pop()()
+                settle(o)
             if not more:
                 cursors(0)
-            tt(zin("A%d" % h), r(y, 0, 64), r(tb, 320, 384), A.max)
-            turn("A%d" % h, "lb%d" % h, 0, q < FINDS - 1)
-            if late:
-                match(o, CUTS[2], CUTS[3])
-                hit(o, n > 0, 48 if n else 0)
-            for f in rest:
-                f()
+            tt(zin("A%d" % h), r(y, 0, 64), r(tb, 192, 256), A.min)
+            turn("A%d" % h, "lb%d" % h, 0, q < FINDS - 1, True)
             if more and last:
                 ts(r3("ST%d" % o, 0, 1), r3("ST%d" % o, 1, 2), Z - 1, A.bitwise_and)
+            if late:
+                match(o, CUT, 64)
+                hit(o, n > 0)
+            tt(r(tb, 256, 320), r3(st, 1, 2), r(tb, 128, 192), A.add)
+            tt(r(y, 64, 128), r3(st, 2, 3), r(tb, 64, 128), A.add)
+            tt(r(y, 128, 192), r3(st, 2, 3), r(tb, 128, 192), A.add)
+            if more and last:
+                ts(r("p%d" % o, 0, 64), r3("ST%d" % o, 0, 1), 0.5 - W, A.add)
             if not more:
                 wants(0)
                 act(zin("K0", 4), r("tb0", 256, 512))
@@ -554,14 +546,13 @@ def rank_program(g, core, T, topo):
                 enlist(h)
             if more:
                 answers(o, last)
-            if n > 5:
-                next(minus, None)
+            if n > 2:
                 next(minus, None)
             if q < FINDS - 1:
                 ask("s", "TG", "TB", "LA", h)
-                if n > 2:
+                if n > 0:
                     next(aside, lambda: None)()
-                match(h, 0, CUTS[0] if n < 2 * FINDS - 3 else 64)
+                match(h, 0, CUT if n < 2 * FINDS - 3 else 64)
             elif h == 0:
                 ask("s", "TG", "TA", "LA", 0, 28, 64)
                 ask("v", "TG", "TA", "LA", 0, 0, 28)
@@ -606,9 +597,9 @@ def rank_program(g, core, T, topo):
         cp(r("LK", 64, 128), r("cb0", 64, 128))
         act(r("MW", 0, 128), r("lb0", 0, 128))
         for k in range(8):
-            ts(r("CP", 128 * k, 128 * k + 128), r("CB", 0, 128), 16.0 * k, A.is_le)
+            ts(r("EQ", 128 * k, 128 * k + 128), r("CB", 0, 128), 16.0 * k, A.is_le)
         for k in range(8):
-            mm(r("lb1", 128 + k, 129 + k), r("CP", 128 * k, 128 * k + 128), r("ONb", 0, 1), True, True)
+            mm(r("lb1", 128 + k, 129 + k), r("EQ", 128 * k, 128 * k + 128), r("ONb", 0, 1), True, True)
         act(r("CW", 0, 128), r("cb1", 0, 128), AF.Identity, 1.0)
         near(t, 768, 1024)
         cp(r("LQ", 0, 8), r("lb1", 128, 136))
@@ -654,10 +645,16 @@ def rank_program(g, core, T, topo):
         mm(r("lb1", 160, 176), r3("OKX", 0, 8), r("GK", 0, 16), False, True)
         for h in range(2):
             turn("D%d" % h, "cb0", 128 + 64 * h)
-        cut(t, 3, 0, 384)
+        cut(t, 3)
         tt(r("LPf", 0, 16), r("lb1", 160, 176), r("DL", 0, 16), A.min)
-        cut(t, 3, 384, 512)
+        if not fast:
+            plus(2, 0, 256)
         cp(r("LP", 0, 16), r("LPf", 0, 16))
+        if fast:
+            tt(r("PR", 256, 384), r("PR", 0, 128), r("cb1", 0, 128), A.max)
+            tt(r("PR", 128, 256), r("PR", 0, 128), r("cb1", 0, 128), A.min)
+        else:
+            plus(2, 256, 512)
         tab, val = r("YW" if fast else "TA", 0, DUMP + 256), r("G5" if fast else "G4", 0, 256)
         op("v", lambda: V.tensor_copy(ap(tab).indirect(T.LP[:, 0:16]), ap(val)), [val, r("LP", 0, 16)], [tab])
         if fast:
@@ -690,6 +687,10 @@ def rank_program(g, core, T, topo):
         c0 = 512 * (c % 2)
         mm(r(("pa", "pb")[c % 2], 0, 512), IDb, r("CM%d" % (c // 2), c0, c0 + 512), False, True)
 
+    def plus(c, a, b):
+        wv = r("w", 512 * c + a, 512 * c + b)
+        tt(wv, wv, r(("pa", "pb")[c % 2], a, b), A.add)
+
     def near(t, c0, c1):
         lookt(r("D0", c0, c1), r("xb%d" % t, 0, W), r("LK", c0 // 16, c1 // 16), r("w", c0, c1), A.subtract)
 
@@ -714,11 +715,8 @@ def rank_program(g, core, T, topo):
         finds(t)
         boundary(t)
     mark("out")
-    a_, lo, hi = (r("PR", 128 * i, 128 * i + 128) for i in range(3))
-    b_, d_, m_ = r("cb1", 0, 128), r("cb0", 128, 256), r("cb1", 128, 256)
+    lo, hi, d_, m_ = r("PR", 128, 256), r("PR", 256, 384), r("cb0", 128, 256), r("cb1", 128, 256)
     y0, y1, y2 = (r("CF", 128 * i, 128 * i + 128) for i in range(3))
-    tt(hi, a_, b_, A.max)
-    tt(lo, a_, b_, A.min)
     tt(m_, hi, d_, A.min)
     tt(y0, lo, d_, A.min)
     tt(hi, hi, d_, A.max)

from concourse.mybir import AluOpType as A, ActivationFunctionType as AF

ROUNDS, FINDS, W, K = 3, 6, 4096, 2048
DUMP = 3 * W
B, FL, IN, U16, SB = "bfloat16", "float32", "int32", "uint16", "sbuf"
rNA, rNB, rND, rV, rJB, rJD, rFR, rU0, rU1, rONE, rTWO = 0, 2, 4, 6, 8, 9, 10, 12, 13, 14, 15
BIG1, BIG2, BIG4 = 2 ** 15, 2 ** 26, 2 ** 29
Z = 8192
CUT = 48

SCRATCH = {}
for _dt, _names in (
    (B, "X:12288 TB:12288 TA:12544 xb0:4096 xb1:4096 xb2:4096 TG:2048 C2:2048 D2:2048 CM0:1024 CM1:1024 EQ:4096 CK:64 "
        "N1:768 N2:768 MJ:768 LO:256 HM0:128 HM1:128 WW:208 C17:128 NBI:128 PBI:128 XW2:16 GM8:64 GK:16 ONb:128 TWO:128 IDb:128 ID64:128 "
        "BDb:128 BD2:128 M1:128 M2:128 ISN:128 KEEP:128 SUM:128 RC:128 CUM:136 CB:128 NE0:64 NE1:64 G3:256 G4:256"),
    (FL, "w:2048 YW:12544 DD:2048 D0:1024 NID:128 PR:384 CF:384 y0:192 y1:192 p0:64 p1:64 FC:8 CJ:16 ONf:256 IDn:128 IDs:128 BDf:128 "
         "IO2:128 RS:256 RW:136 MW:136 CW:136 EE:128 PM:256 MK:256 OWS:256 G5:256 OW1:16 DL:16 LPf:16"),
    (IN, "NX:768 ME:256 FR:256 CU:384 TY:128 CD0:128 CD1:128 HI:4 DI:16"),
    (U16, "LA:128 LB:128 LD:128 LK:128 LQ:8 LG:16 LP:16 PU:256"),
):
    for _n in _names.split():
        SCRATCH[_n.split(":")[0]] = (SB, [128, int(_n.split(":")[1])], _dt)
ZNAMES = "A0 A1 B0 D0 B1 D1".split()
ZSMALL = "E0 E1 W0 W1 K0 k0 M0 m0 K1 k1 M1 m1".split()
SCRATCH["ZF"] = (SB, [128, 16 * len(ZNAMES) + 1, 8], FL)
SCRATCH["ZW"] = (SB, [128, 16 * len(ZSMALL) + 1, 8], B)
SCRATCH["RMX"] = (SB, [128, 16, 16], FL)
SCRATCH["OKX"] = (SB, [128, 8, 16], B)
SCRATCH["ST0"] = (SB, [128, 3, 64], IN)
SCRATCH["ST1"] = (SB, [128, 3, 64], IN)
for _n in "tb0 tb1 cb0 cb1 lb0 lb1 pa pb".split():
    SCRATCH[_n] = ("psum", [128, 512], FL)
GROUPS = "ldx ldw ldn ldm ldf ldc r1 r2 r3 r5 cpa wa00 wa10 wa20 rb0 rb1 out0 out1 out2 yl yw1".split()
SEMAPHORES = ["qv", "qs", "qt", "qg", "xs", "xh", "x0", "x1", "x2"] + GROUPS


def rank_program(g, core, T, topo):
    n_ = len(T.cores)

    def takers(rk):
        return [T.cores[(rk - 1 - t) % n_] for t in range(ROUNDS)]

    def helper(rk):
        c0 = T.cores[rk]
        return [c for c in topo.cores_of(c0)
                if c not in T.cores and topo.die(c) == topo.die(c0) and all(topo.may_write(c, d) for d in takers(rk))][0]

    rank = T.rank_of(core)
    if rank is None:
        for rk in range(n_):
            if core == helper(rk):
                g.wait_ge(T.sem.xh, len(topo.engines(T.cores[rk], core)))
                for t, dst in enumerate(takers(rk)):
                    rid, pid, _se = topo.addr(dst)
                    g.remote_dma(T["xb%d" % t][:, :], T.X[:, 0:W], T.sem["x%d" % t], T.sem.xs, pid, rid, topo.mask(core, dst))
                g.wait_ge(T.sem.xs, sum(len(topo.engines(core, dst)) for dst in takers(rk)))
        return
    Q = {"v": g.vector, "s": g.scalar, "t": g.tensor, "g": g, "y": g.sync}
    V, S, P = g.vector, g.scalar, g.tensor
    SEMOF = {"v": "qv", "s": "qs", "t": "qt", "g": "qg"}
    count, known, clock, acc, closed = {}, {q: {} for q in Q}, {}, {}, {}

    def r(name, c0, c1, step=1, p0=0, p1=128, ps=1):
        return (name, c0, c1, step, p0, p1, ps, None)

    def r3(name, a0, a1, astep=1, b0=0, b1=None):
        n = SCRATCH[name][1][2]
        b1 = n if b1 is None else b1
        last = a0 + (a1 - 1 - a0) // astep * astep
        return (name, a0 * n + b0, last * n + b1, 1, 0, 128, 1, (a0, a1, astep, b0, b1))

    def ap(k):
        if k[7]:
            a0, a1, st, b0, b1 = k[7]
            return T[k[0]][:, a0:a1:st, b0:b1]
        if k[6] != 1:
            return T[k[0]][k[4]:k[5]:k[6], k[1]:k[2]]
        if k[3] != 1:
            return T[k[0]][k[4]:k[5], k[1]:k[2]:k[3]]
        return T[k[0]][k[4]:k[5], k[1]:k[2]]

    def psum(n):
        return n in SCRATCH and SCRATCH[n][0] == "psum"

    def meet(a, b):
        if a[1] >= b[2] or b[1] >= a[2] or a[4] >= b[5] or b[4] >= a[5]:
            return False
        if a[6] == 16 and b[6] == 16 and a[4] % 16 != b[4] % 16:
            return False
        if a[3] == b[3] and a[3] > 1 and (a[1] - b[1]) % a[3]:
            return False
        if a[7] and b[7] and (a[7][3] >= b[7][4] or b[7][3] >= a[7][4]):
            return False
        return True

    def cover(a, b):
        if a == b:
            return True
        whole = a[7] is None or (a[7][2] == 1 and a[7][4] - a[7][3] == SCRATCH[a[0]][1][2])
        return whole and a[3] == 1 and a[6] == 1 and a[1] <= b[1] and a[2] >= b[2] and a[4] <= b[4] and a[5] >= b[5]

    def wait(q, ev):
        sem, n = ev
        if sem in GROUPS:
            n = count[sem]
            closed[sem] = True
        if known[q].get(sem, 0) >= n:
            return
        Q[q].wait_ge(T.sem[sem], n)
        known[q][sem] = n
        for k2, n2 in clock.get((sem, n), {}).items():
            if known[q].get(k2, 0) < n2:
                known[q][k2] = n2

    def deps(q, reads, writes):
        best = {}
        for isw, lst in ((False, reads), (True, writes)):
            for k in lst:
                for (k2, w2, ev, q2) in acc.get(k[0], []):
                    if psum(k[0]):
                        if q2 == q and (q == "t" or not (isw or w2) or not meet(k, k2)):
                            continue
                    elif not ((isw or w2) and meet(k, k2)):
                        continue
                    best[ev[0]] = max(best.get(ev[0], 0), ev[1])
        for s_ in sorted(best):
            wait(q, (s_, best[s_]))

    def note(q, reads, writes, ev, dma):
        tag = "dma" if dma else q
        for isw, lst in ((False, reads), (True, writes)):
            for k in lst:
                old = acc.get(k[0], [])
                if psum(k[0]):
                    old = [o for o in old if o[3] == tag and o[0] != k]
                    if isw and tag != "t":
                        old = [o for o in old if not cover(k, o[0])]
                elif isw:
                    old = [o for o in old if not cover(k, o[0])]
                elif not dma:
                    old = [o for o in old if not (o[3] == tag and not o[1] and o[0] == k)]
                acc[k[0]] = old + [(k, isw, ev, tag)]

    def op(q, fn, reads, writes):
        deps(q, reads, writes)
        sem = SEMOF[q]
        count[sem] = count.get(sem, 0) + 1
        ev = (sem, count[sem])
        fn().then_inc(T.sem[sem], 1)
        c = dict(known[q])
        c[sem] = count[sem]
        clock[ev] = c
        note(q, reads, writes, ev, False)

    def dma(q, grp, out, in_, outk=None, ink=None):
        assert not closed.get(grp)
        rd, wr = [ink] if ink else [], [outk] if outk else []
        deps(q, rd, wr)
        count[grp] = count.get(grp, 0) + 16
        Q[q].dma_start(out, in_).then_inc(T.sem[grp], 16)
        note(q, rd, wr, (grp, 0), True)

    def mv(q, grp, o, i):
        dma(q, grp, ap(o), ap(i), o, i)

    def add(grp, o, i):
        assert not closed.get(grp)
        deps("g", [i], [o])
        count[grp] = count.get(grp, 0) + 16
        g.dma_start(ap(o), ap(i), accum_op=A.add).then_inc(T.sem[grp], 16)
        note("g", [i], [o], (grp, 0), True)

    def tt(o, a, b, f):
        op("v", lambda: V.tensor_tensor(ap(o), ap(a), ap(b), f), [a, b], [o])

    def ts(o, a, s1, f, s2=None, f2=None):
        rd = [a] + [k for k in (s1, s2) if isinstance(k, tuple)]
        x1 = ap(s1) if isinstance(s1, tuple) else s1
        x2 = ap(s2) if isinstance(s2, tuple) else s2
        if f2 is None:
            op("v", lambda: V.tensor_scalar(ap(o), ap(a), x1, None, f), rd, [o])
        else:
            op("v", lambda: V.tensor_scalar(ap(o), ap(a), x1, x2, f, f2), rd, [o])

    def cp(o, a):
        op("v", lambda: V.tensor_copy(ap(o), ap(a)), [a], [o])

    def mset(o, c):
        op("v", lambda: V.memset(ap(o), c), [], [o])

    def scan(o, keep, a, init):
        op("v", lambda: V.tensor_tensor_scan(ap(o), ap(keep), ap(a), init, A.mult, A.add), [keep, a], [o])

    def mm(o, l, h, start, stop):
        op("t", lambda: P.matmul(ap(o), ap(l), ap(h), start, stop), [l, h], [o])

    def act(o, a, f=AF.Copy, bias=0.0, scale=1.0):
        x = ap(scale) if isinstance(scale, tuple) else scale
        op("s", lambda: S.activation(ap(o), ap(a), f, bias, x), [a] + ([scale] if isinstance(scale, tuple) else []), [o])

    def look(q, o, win, off):
        if q == "v":
            op("v", lambda: V.tensor_copy(ap(o), ap(win).indirect(ap(off))), [win, off], [o])
        else:
            op("s", lambda: S.activation(ap(o), ap(win).indirect(ap(off)), AF.Copy), [win, off], [o])

    def lookt(o, win, off, b, f):
        op("v", lambda: V.tensor_tensor(ap(o), ap(win).indirect(ap(off)), ap(b), f), [win, off, b], [o])

    def iota(o, pat, base, cm):
        if SCRATCH[o[0]][2] == IN:
            op("g", lambda: g.iota(ap(o), pat, base, cm), [], [o])
        else:
            op("g", lambda: g.iota(ap(o), pat, base, cm, allow_small_or_imprecise_dtypes=True), [], [o])

    def sel(o, a, pat, f, fill, base, cm):
        op("g", lambda: g.affine_select(ap(o), ap(a), pat, f, float(fill), base, cm), [a], [o])

    def band(o, a, pat):
        sel(o, a, pat, A.is_ge, 0, 0, 1)
        return lambda: sel(o, o, [[-s_, n] for s_, n in pat], A.is_ge, 0, 15, -1)

    def mark(name):
        pass

    mark("setup")
    dma("y", "ldn", T.NX[:, :], T.nxt[:, :], r("NX", 0, 768))
    dma("y", "ldm", T.ME[:, :], T.mem[:, :], r("ME", 0, 256))
    dma("y", "ldc", T.CU[:, :], T.cur[:, :], r("CU", 0, 384))
    dma("y", "ldc", T.TY[:, :], T.typ[:, :], r("TY", 0, 128))
    dma("y", "ldf", T.FR[:, :], T.fro[:, :], r("FR", 0, 256))
    dma("y", "ldx", T.X[:, 0:W], T.x[:, :], r("X", 0, W))
    dma("y", "ldw", T.D2[:, 0:K], T.w0[:, :], r("D2", 0, K))

    for t in range(ROUNDS):
        src = helper((rank + 1 + t) % n_)
        count["x%d" % t] = len(topo.engines(src, core))
        acc["xb%d" % t] = [(r("xb%d" % t, 0, W), True, ("x%d" % t, count["x%d" % t]), "dma")]

    def send():
        wait("g", ("ldx", 0))
        wait("g", ("r5", 0))
        rid, pid, _se = topo.addr(helper(rank))
        g.remote_dma(T.X[:, 0:W], T.X[:, 0:W], T.sem.xh, T.sem.xs, pid, rid, topo.mask(core, helper(rank)))

    rec = lambda f=1: ((rV, f), (rV + 1, 256 * f))
    typ0 = ((rU0, 2 * W), (rU1, W), (rONE, -W))
    typ1 = ((rU0, -W), (rU1, -2 * W), (rONE, 3 * W))
    typ2 = ((rU0, -W), (rU1, W), (rONE, W))
    num = lambda a, f=1: ((a, f), (a + 1, 64 * f), (rONE, K * f))
    pack = lambda a: num(a, Z)[:2] + rec() + ((rONE, K),)
    times = lambda terms, f: tuple((rw, wt * f) for rw, wt in terms)
    packD = pack(rND) + ((rJD, -BIG2),)
    keepD = ((rONE, -BIG2), (rJD, BIG2))
    WR = (pack(rNA), num(rNA) + typ0)
    base = typ1 + ((rONE, K - Z), (rJB, Z))
    less_ = times(base, -1) + ((rTWO, 0.5),)
    WF = (times(num(rNB) + typ1 + less_, Z) + ((rJB, -BIG2),), keepD, (), times(num(rNA) + typ0 + less_, Z), (), packD, pack(rNA), base)
    WL = (rec() + typ1 + less_ + ((rJB, -BIG1),), keepD, (), rec() + typ0 + less_, (), packD, pack(rNA), base)
    WB = (rec() + ((rONE, K),), ((rONE, 1), (rJB, -1)), typ1 + ((rONE, -K),), typ2 + ((rONE, -K),), ((rFR, 1),), ((rFR + 1, 1),),
          rec()[:1] + ((rONE, 1),), rec()[1:] + typ1)
    WPOS = {"R": 0, "F": 2, "L": 10, "B": 18}

    def weights(*sets):
        todo = []
        for n, ws in sets:
            for i, terms in enumerate(ws):
                if terms:
                    todo.append((WPOS[n] + i, [(rw, sum(wt for r_, wt in terms if r_ == rw)) for rw in sorted(set(r_ for r_, _w in terms))]))
        while todo:
            for a, terms in todo:
                rw, wt = terms.pop()
                k = r("WW", 8 * a, 8 * a + 8)
                sel(k, k, [[-16, 8]], A.not_equal, wt, -rw, 1)
            todo = [x for x in todo if x[1]]

    def wts(name, a0, n):
        return r("WW", 8 * (WPOS[name] + a0), 8 * (WPOS[name] + a0 + n))

    ONb, IDn, IDb, BDb, BDf = (r(n, 0, 128) for n in ("ONb", "IDn", "IDb", "BDb", "BDf"))
    iota(r("HI", 0, 1), [[1, 1]], 0, 1)
    iota(r("CJ", 0, 16), [[1, 16]], -1, 0)
    iota(r("LO", 0, 256), [[1, 256]], 0, 0)
    iota(r("WW", 0, 208), [[0, 208]], 0, 0)
    iota(r("ONf", 0, 256), [[0, 256]], 1, 0)
    sel(IDn, r("ONf", 0, 128), [[-1, 128]], A.is_equal, 0, 0, 1)
    weights(("R", WR), ("F", WF))

    def trow(tab, rw, c0, c1):
        return r(tab, c0, c1, 1, rw, 128, 16)

    def turned(grp, tab, rw, to, a):
        for d0, d1, s0 in ((0, (3 - a) * W, a * W), ((3 - a) * W, 3 * W, 0))[:2 if a else 1]:
            mv("y", grp, trow("TB", to, d0, d1), trow(tab, rw, s0, s0 + d1 - d0))

    def rebuild(grp, tab, turns):
        for a in turns:
            for i in range(2):
                turned(grp, tab, i, 2 * a + i, a)

    fc = lambda i: r("FC", i, i + 1)
    ts(r("HI", 0, 1), r("HI", 0, 1), 15, A.bitwise_and)
    mset(r3("ZF", 0, 33), 0.0)
    for i, rw, f in ((1, rV + 1, A.is_equal), (2, rV, A.not_equal), (0, rV, A.is_equal), (3, rU0, A.not_equal), (4, rU1, A.not_equal)):
        ts(fc(i), r("HI", 0, 1), float(rw), f)
    mset(r("C17", 0, 64), 0.0)
    ts(r("CJ", 0, 16), r("CJ", 0, 16), fc(1), A.mult, fc(2), A.add)
    mset(r("C17", 64, 128), 17.0 / 128)
    mset(r("CUM", 0, 8), 0.0)
    for j in range(16):
        ts(r("TB", 2 * W + 256 * j, 2 * W + 256 * j + 256), r("LO", 0, 256), fc(0), A.mult, r("CJ", j, j + 1), A.add)
        if j % 4 == 3:
            act(r("TB", W + 256 * j - 768, W + 256 * j + 256), r("TB", 2 * W + 256 * j - 768, 2 * W + 256 * j + 256), AF.Copy, 0.0, fc(4))
    act(r("TB", 3072, W), r("TB", 2 * W + 3072, 3 * W), AF.Copy, 0.0, fc(3))
    ts(r("N2", 0, 768), r("NX", 0, 768), 1.0 / 64, A.mult, 160 - 31.5 / 64, A.add)
    ts(r("MJ", 512, 768), r("ME", 0, 256), 4.0, A.is_lt)
    ts(r("NX", 0, 768), r("NX", 0, 768), 63, A.bitwise_and)
    ts(r("N2", 0, 768), r("N2", 0, 768), -192.0, A.add)
    cp(r("N1", 0, 768), r("NX", 0, 768))
    ts(r("TB", 0, 3072), r("TB", 2 * W, 2 * W + 3072), fc(3), A.mult)
    for i in range(2):
        mv("y", "r1", trow("TB", i, 0, 3 * W), r(("N1", "N2")[i], 0, 768))
    for i in range(2):
        ts(r("NX", 256 * i, 256 * i + 256), r("ME", 0, 256), 2 ** i, A.bitwise_and)
    for i in range(3):
        ts(r("tb0", 128 * i, 128 * i + 128), r("CU", 128 * i, 128 * i + 128), float(W * i), A.add)
    ts(r("MJ", 0, 512), r("NX", 0, 512), 0.0, A.is_equal)
    for s in range(3):
        mv("y", "r2", trow("TB", rJB, W * s, W * s + W), r("MJ", 256 * ((s + 1) % 3), 256 * ((s + 1) % 3) + 256))
    rebuild("r5", "TB", (1, 2))
    turned("r5", "TB", rJB, rJD, 1)
    mv("y", "r3", r("X", 2 * W, 3 * W), r("X", 0, W))

    for i in (4, 3, 2, 1, 0):
        ts(r("DD", 128 * i, 128 * i + 128), r("TY", 0, 128), float((i + 1) % 3), A.is_equal)
    cp(r("EQ", 0, 256), r("FR", 0, 256))
    for n in range(3):
        c0 = 640 + 384 * n
        tt(r("DD", c0, c0 + 384), r("tb0", 0, 384), r("DD", 128 * (2 - n), 128 * (5 - n)), A.mult)
        for i in range(3):
            mm(r(("lb0", "lb1", "pa")[n], 0, 128), IDn, r("DD", c0 + 128 * i, c0 + 128 * i + 128), i == 0, i == 2)
    act(ONb, r("ONf", 0, 128), AF.Sigmoid, 0.0, 400.0)
    cp(r("X", W, W + K), r("X", 0, K))
    act(r("w", 0, K), r("D2", 0, K))
    act(r("X", W + K, 2 * W), r("X", K, W))
    iota(r("DI", 0, 16), [[1, 16]], 0, 16)
    iota(r("ME", 0, 256), [[0, 16], [-1, 16]], 16, 1)
    mset(r3("ZW", 0, 33), 0.0)
    mset(r("CK", 0, 64), -0.5 / 128)
    mset(IDb, 1.0)
    iota(r("XW2", 0, 16), [[-2, 2], [0, 8]], 1, 0)
    iota(r("NBI", 0, 128), [[0, 128]], 0, 0)
    band(r("XW2", 0, 16), r("XW2", 0, 16), [[0, 2], [-16, 8]])()
    sel(r("NBI", 0, 128), r("NBI", 0, 128), [[-1, 128]], A.not_equal, -BIG4, 0, 1)
    sel(r("PBI", 0, 128), r("NBI", 0, 128), [[-1, 128]], A.not_equal, BIG4, 0, 1)
    sel(r("IDs", 0, 128), IDn, [[-1, 128]], A.not_equal, 1.0 / Z, 0, 1)
    ts(r("DI", 0, 16), r("DI", 0, 16), 255, A.bitwise_and)
    tt(r("EQ", 256, 512), r("FR", 0, 256), r("EQ", 0, 256), A.subtract)
    ts(r("ME", 0, 256), r("ME", 0, 256), 15, A.bitwise_and)
    ts(r("DL", 0, 16), r("DI", 0, 16), float(DUMP), A.add)
    for n, L in enumerate(("LA", "LB")):
        cp(r(L, 0, 128), r(("lb0", "lb1")[n], 0, 128))
    ts(r3("RMX", 0, 16), r("ME", 0, 256), 0.0, A.is_equal)
    sel(IDb, IDb, [[-1, 128]], A.is_equal, 0, 0, 1)

    def later():
        g.sync.wait_ge(T.sem.xs, len(topo.engines(core, helper(rank))))
        for rw in range(16):
            if rw in (rFR, rFR + 1):
                for s in range(3):
                    mv("y", "cpa", trow("TA", rw, W * s, W * s + W), r("EQ", 256 * (rw - rFR), 256 * (rw - rFR) + 256))
            else:
                mv("y", "cpa", trow("TA", rw, 0, 3 * W), trow("TB", rw, 0, 3 * W))
        sel(r("NID", 0, 128), IDn, [[-1, 128]], A.not_equal, -1, 0, 1)
        weights(("L", WL), ("B", WB))
        iota(r3("ZF", 33, 16 * len(ZNAMES) + 1), [[0, 512]], 0, 0)
        iota(r3("ZW", 33, 16 * len(ZSMALL) + 1), [[0, 1280]], 0, 0)
        iota(r("TWO", 0, 128), [[0, 128]], 2, 0)
        iota(r("GK", 0, 16), [[0, 16]], 16384, 0)
        for n in ("RW", "MW", "CW"):
            iota(r(n, 128, 136), [[0, 8]], 0, 0)
        fin = [band(BDb, ONb, [[-16, 8], [0, 16]]), band(BDf, r("ONf", 0, 128), [[-16, 8], [0, 16]]),
               band(r("BD2", 0, 128), r("TWO", 0, 128), [[-16, 8], [0, 16]]), band(r("GM8", 0, 64), r("ONb", 0, 64), [[-16, 8], [0, 8]]),
               band(r("GK", 0, 16), r("GK", 0, 16), [[0, 2], [-16, 8]])]
        for f in fin:
            f()
        iota(r("RC", 0, 128), [[0, 8], [1, 16]], 0, 0)
        iota(r("IO2", 0, 128), [[2, 128]], 1, 0)
        sel(r("RS", 0, 256), r("ONf", 0, 256), [[0, 16], [1, 16]], A.is_gt, 0, 0, 0)
        sel(r("ISN", 0, 128), IDb, [[0, 8], [-1, 16]], A.is_ge, 0, 1, 0)
        sel(r("KEEP", 0, 128), IDb, [[0, 8], [1, 16]], A.is_ge, 0, -2, 0)
        sel(r("ID64", 0, 128), IDb, [[-1, 128]], A.not_equal, 64, 0, 1)
        iota(r("SUM", 0, 128), [[0, 128]], 0, 0)
        for rw, wt in num(rNA):
            sel(r("SUM", 0, 128), r("SUM", 0, 128), [[-16, 8], [0, 16]], A.not_equal, wt, -rw, 1)
        sel(r("M1", 0, 128), r("BD2", 0, 128), [[1, 128]], A.is_gt, 0, 0, -1)
        sel(r("M2", 0, 128), r("BD2", 0, 128), [[-1, 128]], A.is_gt, 0, 0, 1)
        for n in ("M1", "M2"):
            sel(r(n, 0, 128), r(n, 0, 128), [[-1, 128]], A.not_equal, 1, 0, 1)

    def units(ps, src, c0, wk, start=True, stop=True):
        n = wk[2] - wk[1]
        for b in range(8):
            mm(r(ps, b, 8 * n, 8), r(src, c0 + b, c0 + 1024, 8), wk, start and b == 0, stop and b == 7)

    def zin(z, n=1):
        buf, i = ("ZF", 16 * ZNAMES.index(z)) if z in ZNAMES else ("ZW", 16 * ZSMALL.index(z))
        return r3(buf, i + 1, i + 16 * n, 2)

    def turn(z, ps, pc, words=False, onto=False, stop=True):
        if z in ZNAMES:
            buf, at, ident = "ZF", [16 * ZNAMES.index(z)], "IDs" if words else "IDn"
        else:
            buf, at, ident = "ZW", [16 * ZSMALL.index(n) for n in (z, z.lower()) if n in ZSMALL], "IDb"
        for i in at:
            mm(r(ps, pc, pc + 64), r3(buf, i + 1, i + 17), r(ident, 0, 128, 2), i == at[0] and not onto, False)
            mm(r(ps, pc, pc + 64), r3(buf, i, i + 16), r(ident, 1, 128, 2), False, i == at[-1] and stop)

    def ask(q, buf, tab, L, h, c0=0, c1=64):
        look(q, r(buf, 1024 * h + 16 * c0, 1024 * h + 16 * c1), r(tab, 0, DUMP), r(L, 64 * h + c0, 64 * h + c1))

    def match(h, c0=0, c1=64):
        lookt(r("CM%d" % h, 16 * c0, 16 * c1), r("X", 0, 3 * W), r("LA", 64 * h + c0, 64 * h + c1),
              r("w", 1024 * h + 16 * c0, 1024 * h + 16 * c1), A.is_ge)

    def hit(h, early=False):
        cb = "cb%d" % h
        if not early:
            mm(r(cb, 0, 128), ONb, r("C17", 0, 128), True, False)
        units(cb, "CM%d" % h, 0, r("XW2", 0, 16), False, True)
        act(r("HM%d" % h, 0, 128), r(cb, 0, 128), AF.Sigmoid, -3400.0, 400.0)

    def answers(h, last):
        tb, hm = "tb%d" % h, "HM%d" % h
        units(tb, "TG", 1024 * h, wts("L" if last else "F", 0, 8), True, False)
        for a, c0, wt in ((0, 64, "PBI"), (3, 0, "PBI"), (1, 64, "NBI"), (2, 0, "NBI"), (5, 64, "NBI"), (6, 64, "NBI")):
            mm(r(tb, 64 * a, 64 * a + 64), r(wt, 0, 128), r(hm, c0, c0 + 64), False, a == 6)
        if not last:
            mm(r("cb%d" % h, 0, 128), ONb, r("C17", 0, 128), True, False)
        mm(r("lb%d" % h, 0, 64), ONb, r("CK", 0, 64), True, False)

    def enlist(h):
        cp(r("LA", 64 * h, 64 * h + 64), r("lb%d" % h, 0, 64))

    def first(h):
        units("tb%d" % h, "TG", 1024 * h, wts("R", 1, 1))

        def then():
            cp(zin("A%d" % h), r("tb%d" % h, 0, 64))
            turn("A%d" % h, "lb%d" % h, 0)
        return then

    def state(h, i, ps):
        units(ps, ("C2", "D2")[i - 1], 1024 * h, wts("R", 0, 1))
        return lambda: cp(r3("ST%d" % h, i, i + 1), r(ps, 0, 64))

    def refresh(tab, t):
        mark("ref%d" % t)
        ask("s", "TG", tab, "LA", 0)
        if t:
            ask("s", "TG", tab, "LA", 1)
            plus(3, 0, 512)
            cp(r("LD", 0, 128), r("cb0", 128, 256))
            ask("v", "C2", tab, "LB", 1, 0, 52)
            ask("v", "D2", tab, "LD", 1, 0, 16)
            first(0)()
            ask("s", "D2", tab, "LD", 0)
            ask("s", "C2", tab, "LB", 1, 52, 64)
            ask("v", "C2", tab, "LB", 0, 0, 40)
            enlist(0)
            ask("v", "C2", tab, "LB", 0, 40, 64)
            ask("s", "TG", "TB", "LA", 0)
            match(0)
            first(1)()
            ask("v", "D2", tab, "LD", 1, 16, 48)
            enlist(1)
            hit(0)
            ask("v", "D2", tab, "LD", 1, 48, 64)
        else:
            ask("v", "TG", tab, "LA", 1)
            ask("s", "C2", tab, "LB", 1)
            cp(r("LD", 0, 128), r("pa", 0, 128))
            ask("v", "C2", tab, "LB", 0)
            for f in [first(0), first(1)]:
                f()
            ask("s", "D2", tab, "LD", 0)
            ask("v", "D2", tab, "LD", 1)
            enlist(0)
            enlist(1)
            ask("s", "TG", "TB", "LA", 0)
            match(0)
        fin = [state(0, 2, "pa"), state(0, 1, "cb1"), state(1, 1, "pb")]
        if not t:
            hit(0)
        ask("s", "TG", "TB", "LA", 1)
        fin.append(state(1, 2, "lb1"))
        for f in fin[:2]:
            f()
        answers(0, False)
        match(1, 0, CUT)
        for f in fin[2:]:
            f()

    def settle(h):
        tt(r3("ST%d" % h, 1, 3), r("y%d" % h, 64, 192), r("tb%d" % h, 320, 448), A.max)

    def finds(t):
        mark("find%d" % t)
        aside = numbers() if t == ROUNDS - 1 else iter(())
        minus = less(8, 16)
        for n in range(2 * FINDS):
            h, o, q = n % 2, 1 - n % 2, n // 2
            tb, st, y = "tb%d" % h, "ST%d" % h, "y%d" % h
            more, late, last = n + 1 < 2 * FINDS, n < 2 * FINDS - 2, (n + 1) // 2 == FINDS - 1
            if more and not late:
                hit(o, True)
            if not more:
                settle(o)
                units("tb0", "TG", 0, wts("B", 0, 8))
            tt(r(y, 0, 64), r("p%d" % h, 0, 64) if q == FINDS - 1 else r3(st, 1, 2), r(tb, 0, 64), A.max)
            cp(zin("E%d" % h), r(tb, 448, 512))
            turn("E%d" % h, "lb%d" % h, 0, False, True, False)
            if n and more:
                settle(o)
            if not more:
                cursors(0)
            tt(zin("A%d" % h), r(y, 0, 64), r(tb, 192, 256), A.min)
            turn("A%d" % h, "lb%d" % h, 0, q < FINDS - 1, True)
            if more and last:
                ts(r3("ST%d" % o, 0, 1), r3("ST%d" % o, 1, 2), Z - 1, A.bitwise_and)
            if late:
                match(o, CUT, 64)
                hit(o, n > 0)
            tt(r(tb, 256, 320), r3(st, 1, 2), r(tb, 128, 192), A.add)
            tt(r(y, 64, 128), r3(st, 2, 3), r(tb, 64, 128), A.add)
            tt(r(y, 128, 192), r3(st, 2, 3), r(tb, 128, 192), A.add)
            if more and last:
                ts(r("p%d" % o, 0, 64), r3("ST%d" % o, 0, 1), 0.5 - W, A.add)
            if not more:
                wants(0)
                act(zin("K0", 4), r("tb0", 256, 512))
            if late:
                enlist(h)
            tt(r(y, 64, 128), r(y, 64, 128), r(tb, 256, 320), A.max)
            if not late:
                enlist(h)
            if more:
                answers(o, last)
            if n > 2:
                next(minus, None)
            if q < FINDS - 1:
                ask("s", "TG", "TB", "LA", h)
                if n > 0:
                    next(aside, lambda: None)()
                match(h, 0, CUT if n < 2 * FINDS - 3 else 64)
            elif h == 0:
                ask("s", "TG", "TA", "LA", 0, 28, 64)
                ask("v", "TG", "TA", "LA", 0, 0, 28)

    def cursors(h):
        ts(r("CD%d" % h, 0, 128), r3("ST%d" % h, 1, 3), Z - 1, A.bitwise_and)

    def wants(h):
        tb, cd = "tb%d" % h, "CD%d" % h
        tt(r("NE%d" % h, 0, 64), r(tb, 0, 64), r(cd, 0, 64), A.not_equal)
        tt(zin("B%d" % h, 2), r(tb, 128, 256), r(cd, 0, 128), A.add)
        tt(zin("W%d" % h), r(tb, 64, 128), r("NE%d" % h, 0, 64), A.mult)

    def boundary(t):
        mark("bnd%d" % t)
        fast = t == ROUNDS - 1
        ask("s", "TG", "TA", "LA", 1, 36, 64)
        settle(1)
        ask("v", "TG", "TA", "LA", 1, 0, 36)
        turn("K0", "cb0", 0)
        turn("W0", "lb1", 0)
        turn("M0", "lb0", 0)
        units("tb1", "TG", 1024, wts("B", 0, 8))
        turn("B0", "cb1", 0)
        cp(r("LK", 0, 64), r("cb0", 0, 64))
        cursors(1)
        near(t, 0, 256)
        wants(1)
        turn("W1", "lb1", 64)
        act(zin("K1", 4), r("tb1", 256, 512))
        near(t, 256, 512)
        scan(r("CUM", 1, 129), ONb, r("lb1", 0, 128), 0.0)
        mm(r("tb0", 0, 128), r("CUM", 1, 129), BDb, True, True)
        mm(r("tb1", 0, 128), r("M1", 0, 128), r("CUM", 1, 129), True, False)
        mm(r("tb1", 0, 128), r("M2", 0, 128), r("CUM", 0, 128), False, True)
        act(r("RW", 0, 128), r("tb1", 0, 128))
        turn("K1", "cb0", 64)
        turn("M1", "lb0", 64)
        turn("B1", "cb1", 64)
        near(t, 512, 768)
        tt(r("CB", 0, 128), r("tb0", 0, 128), r("RC", 0, 128), A.subtract)
        cp(r("LK", 64, 128), r("cb0", 64, 128))
        act(r("MW", 0, 128), r("lb0", 0, 128))
        for k in range(8):
            ts(r("EQ", 128 * k, 128 * k + 128), r("CB", 0, 128), 16.0 * k, A.is_le)
        for k in range(8):
            mm(r("lb1", 128 + k, 129 + k), r("EQ", 128 * k, 128 * k + 128), r("ONb", 0, 1), True, True)
        act(r("CW", 0, 128), r("cb1", 0, 128), AF.Identity, 1.0)
        near(t, 768, 1024)
        cp(r("LQ", 0, 8), r("lb1", 128, 136))
        pull(t, 2)
        pull(t, 3)
        cut(t, 0, 0, 256)
        LQ, EE = r("LQ", 0, 8), r("EE", 0, 128)
        lookt(EE, r("RW", 0, 136), LQ, r("IO2", 0, 128), A.is_equal)
        if fast:
            cp(r("PR", 0, 128), r("LA", 0, 128))
        else:
            cp(r("LB", 0, 128), r("cb1", 0, 128))
        for i, n in enumerate(("MW", "CW")):
            lookt(r("PM", 128 * i, 128 * i + 128), r(n, 0, 136), LQ, EE, A.mult)
            mm(r("tb0", 256 + 128 * i, 384 + 128 * i), BDf, r("PM", 128 * i, 128 * i + 128), True, True)
        cut(t, 0, 256, 512)
        plain(2)
        cut(t, 1, 0, 256)
        tt(r("MK", 0, 256), r("tb0", 256, 512), r3("RMX", 0, 16), A.mult)
        cp(r("PU", 0, 256), r("tb0", 256, 512))
        scan(r("OWS", 0, 256), r("RS", 0, 256), r("MK", 0, 256), 0.0)
        cut(t, 1, 256, 512)
        plain(3)
        ow = r("OWS", 15, 256, 16)
        ts(r("LG", 0, 16), ow, -1.0, A.add)
        ts(r("OW1", 0, 16), ow, -1.0 - 2 * 16384, A.add)
        mm(r("lb1", 160, 176), IDn, r("OW1", 0, 16), True, False)
        look("s", r("G3", 0, 256), r("TA", 0, DUMP), r("LG", 0, 16))
        for k in range(16):
            ts(r("EQ", 256 * k, 256 * k + 256), r("PU", 0, 256), r("OWS", 16 * k + 15, 16 * k + 16), A.is_equal)
            for i in range(2):
                mm(r("tb1", 128, 192), r("EQ", 256 * k + 128 * i, 256 * k + 128 * i + 128), r("GM8", 0, 64), k + i == 0, k + i == 16)
            if k == 8:
                for i in range(2):
                    o = r("lb0", 256 + 128 * i, 384 + 128 * i)
                    if not fast:
                        mm(o, r("KEEP", 0, 128), r("G3", 128 * i, 128 * i + 128), True, False)
                    mm(o, r("SUM" if fast else "ISN", 0, 128), r("G3", 128 - 128 * i, 256 - 128 * i), fast, True)
                act(r("G5" if fast else "G4", 0, 256), r("lb0", 256, 512))
        cut(t, 2)
        for i in range(2):
            tt(r3("OKX", 0, 8, 1, 8 * i, 8 * i + 8), r("tb1", 128, 192), r3("RMX", 0, 8, 1, 8 * i, 8 * i + 8), A.mult)
        mm(r("lb1", 160, 176), r3("OKX", 0, 8), r("GK", 0, 16), False, True)
        for h in range(2):
            turn("D%d" % h, "cb0", 128 + 64 * h)
        cut(t, 3)
        tt(r("LPf", 0, 16), r("lb1", 160, 176), r("DL", 0, 16), A.min)
        if not fast:
            plus(2, 0, 256)
        cp(r("LP", 0, 16), r("LPf", 0, 16))
        if fast:
            tt(r("PR", 256, 384), r("PR", 0, 128), r("cb1", 0, 128), A.max)
            tt(r("PR", 128, 256), r("PR", 0, 128), r("cb1", 0, 128), A.min)
        else:
            plus(2, 256, 512)
        tab, val = r("YW" if fast else "TA", 0, DUMP + 256), r("G5" if fast else "G4", 0, 256)
        op("v", lambda: V.tensor_copy(ap(tab).indirect(T.LP[:, 0:16]), ap(val)), [val, r("LP", 0, 16)], [tab])
        if fast:
            dma("y", "out1", T.yn[:, :], T.YW[0:128:16, 0:3 * W], None, trow("YW", 0, 0, 3 * W))
        else:
            rebuild("rb%d" % t, "TA", (0, 1, 2))

    def numbers():
        for c0, c1, b in ((0, 512, "pa"), (512, 768, "pb")):
            for i, d in enumerate(("N1", "N2")):
                mm(r(b, 0, c1 - c0), r(("IDb", "ID64")[i], 0, 128), r(d, c0, c1), i == 0, i == 1)
        yield lambda: act(r("DD", 0, 512), r("pa", 0, 512), AF.Identity, float(K))

        def rest():
            act(r("DD", 512, 768), r("pb", 0, 256), AF.Identity, float(K))
            mv("y", "yw1", trow("YW", 0, 0, 3 * W), r("DD", 0, 768))
        yield rest

    def pull(t, c):
        c0 = 512 * (c % 2)
        look("s", r("CM%d" % (c // 2), c0, c0 + 512), r("xb%d" % t, 0, W), r("LK", 32 * c, 32 * c + 32))

    def less(a, b):
        for i in range(a, b):
            c0 = 128 * (i % 4)
            mm(r(("pa", "pb")[i // 4 % 2], c0, c0 + 128), r("NID", 0, 128), r("w", 128 * i, 128 * i + 128), c0 == 0, False)
            yield None

    def plain(c):
        c0 = 512 * (c % 2)
        mm(r(("pa", "pb")[c % 2], 0, 512), IDb, r("CM%d" % (c // 2), c0, c0 + 512), False, True)

    def plus(c, a, b):
        wv = r("w", 512 * c + a, 512 * c + b)
        tt(wv, wv, r(("pa", "pb")[c % 2], a, b), A.add)

    def near(t, c0, c1):
        lookt(r("D0", c0, c1), r("xb%d" % t, 0, W), r("LK", c0 // 16, c1 // 16), r("w", c0, c1), A.subtract)

    def cut(t, c, a=0, b=512):
        d = r("D0", 512 * c + a, 512 * c + b) if c < 2 else r(("pa", "pb")[c % 2], a, b)
        if c > 1 and t < ROUNDS - 1:
            ts(d, d, -8.0, A.max, 8.0, A.min)
            return
        ts(r("DD", 512 * c + a, 512 * c + b), d, -8.0, A.max, 8.0, A.min)
        if b == 512:
            add("wa%d0" % t, r("w" if t < ROUNDS - 1 else "yw", 512 * c, 512 * c + 512), r("DD", 512 * c, 512 * c + 512))

    for t in range(ROUNDS):
        if t == 0:
            send()
            later()
        refresh("TA" if t else "TB", t)
        if t == ROUNDS - 1:
            for i, d in ((0, "N1"), (1, "N2")):
                mv("y", "yl", r(d, 0, 768), trow("TA", i, 0, 3 * W))
            mv("y", "out0", r("yw", 0, K), r("w", 0, K))
        finds(t)
        boundary(t)
    mark("out")
    lo, hi, d_, m_ = r("PR", 128, 256), r("PR", 256, 384), r("cb0", 128, 256), r("cb1", 128, 256)
    y0, y1, y2 = (r("CF", 128 * i, 128 * i + 128) for i in range(3))
    tt(m_, hi, d_, A.min)
    tt(y0, lo, d_, A.min)
    tt(hi, hi, d_, A.max)
    tt(lo, lo, m_, A.max)
    ts(y2, hi, -2.0 * W, A.add)
    ts(y1, lo, -1.0 * W, A.add)
    dma("y", "out2", T.yc[:, :], T.CF[:, :], None, r("CF", 0, 384))
    for sem in SEMAPHORES:
        if sem == "xs":
            g.wait_ge(T.sem.xs, len(topo.engines(core, helper(rank))))
        elif count.get(sem, 0):
            known["g"].pop(sem, None)
            wait("g", (sem, count[sem]))
